import numpy as np, ml_dtypes
CORES = [2,6,10,14,18,22,26,30]
N = 8
import mx_ref
BF = ml_dtypes.bfloat16
def gcols(t, e):
    v = np.concatenate([t.reshape(8, 16, -1, 4), np.zeros((8, 16, 1, 4), BF)], axis=2)
    return np.ascontiguousarray(np.stack([v[g][:, e[g]] for g in range(8)])).reshape(128, -1)
def tile(rs):
    return np.stack(rs, axis=2).reshape(128, -1).astype(BF)
def pick(q, e):
    c = np.concatenate([q[0].reshape(128, -1, 4), np.zeros((128, 1, 4), np.uint8)], axis=1); s = np.concatenate([q[1], np.ones((16, 1), np.uint8)], axis=1)
    return (np.ascontiguousarray(c[:, e].reshape(128, -1)), np.ascontiguousarray(s[:, e]))
def join(*qs):
    return (np.concatenate([q[0] for q in qs], axis=1), np.concatenate([q[1] for q in qs], axis=1))
def put(q, e, v):
    c, s = q[0].reshape(128, -1, 4).copy(), q[1].copy(); c[:, e] = v[0].reshape(128, -1, 4); s[:, e] = v[1]
    return (c.reshape(128, -1), s)
def pk(c, s):
    return (np.ascontiguousarray(c), mx_ref.live(s))
def emit(q):
    return q[0], q[1]
def packed(v, rng):
    q = [mx_ref.quantize(np.ascontiguousarray(v[r])) for r in range(N)]
    return np.stack([a for a, b in q]), np.stack([mx_ref.plane(b, rng) for a, b in q])
def values_of_codes():
    e, c = np.zeros((128, 128, 4), np.float32), np.zeros((128, 2, 4), np.uint8)
    e[np.arange(128), np.arange(128), 0] = 1
    c[:127, :, 0] = np.arange(256).reshape(2, 128).T[:127]
    return mx_ref.matmul(mx_ref.quantize(e.reshape(128, 512).astype(BF)), (c.reshape(128, 8), np.full((16, 2), 127, np.uint8))).T.reshape(-1).astype(np.float64)
CODE_VALUE, SCALE_VALUE = values_of_codes(), 2.0 ** (np.arange(256) - 127.0)
def decode(q):
    return (CODE_VALUE[q[0]].reshape(16, 8, -1, 4) * SCALE_VALUE[q[1]][:, None, :, None] + 0.0).reshape(128, -1).astype(np.float32)
def f(rng, *shape):
    return mx_ref.flush((rng.standard_normal(shape, dtype=np.float32) * np.exp2(rng.integers(-2, 3, shape[:-1] + (1,)))).astype(BF))
def wide(rng, *shape, cols=0):
    v = rng.standard_normal(shape, dtype=np.float32) * np.exp2(rng.integers(-12, 13, shape)).astype(np.float32)
    if cols: v *= np.repeat(np.exp2(rng.integers(-cols, cols + 1, shape[:-2] + (1, shape[-1] // 4))) * (rng.random(shape[:-2] + (1, shape[-1] // 4)) > 0.0625), 4, axis=-1).astype(np.float32)
    return mx_ref.flush(v.astype(BF))
S, Z, E, C, A, R = 24, 16, 6, 384, 144, 3
DEPTH = np.arange(E)
AWAY = np.abs(np.arange(S)[:, None] - np.arange(S))
CONE = DEPTH[:, None, None] - AWAY[:, None, :, None] >= DEPTH
def cuts(p):
    rich = (p[::16] > 0).reshape(8, S, Z)[:, :, :E]
    good = 2 * np.sum(rich[:, None, None] & CONE, axis=(3, 4)) > np.sum(CONE, axis=(2, 3))
    return np.sum((good[:, :, :, None, None] & CONE).any(axis=(1, 2)), axis=2)
def slots(a):
    n = a[:, :, None]
    return np.where(DEPTH < n, Z * np.arange(S)[:, None] + n - 1 - DEPTH, -1).reshape(8, A)
def places(a, s):
    n, c, k = a[:, :, None], np.arange(S)[:, None], np.arange(Z)
    i = k - Z + n
    return np.where(i < 0, Z * c + k + n, np.where(i < s[:, :, None], C + E * c + i, Z * c + n - 1 - i)).reshape(8, C)
def big(v):
    v = v.astype(np.float32)
    v[np.abs(v) < np.float32(2.0 ** -16)] = 0
    return v.astype(BF)
def numbers_of(rng):
    return {"x": big(f(rng, N, 128, 4 * C)), "u": np.array(f(rng, N, 128, 512)), "v": np.array(f(rng, N, 128, 512))}
def weights(rng, still=[], fade=[]):
    w = big(f(rng, N, 128, 2048)).reshape(N, 8, 16, 4, 8, 16, 4)
    for i in still:
        w[:, :, i] = 0
        w[:, :, :, :, :, i] = 0
    for g in fade:
        w[:, g, 0, 0, g, 0, 0] = -64
        w[:, g, 0, 0, g, 1, 0] = 0.25
    c, p = packed(w.reshape(N, 128, 2048), rng)
    return {"wc": c, "ws": p}
def setup_inputs(rng):
    return {**numbers_of(rng), **weights(rng)}
def setup_inputs_zeros(rng):
    d = numbers_of(rng)
    x = d["x"].reshape(N, 8, 16, C, 4)
    x.transpose(0, 1, 3, 2, 4)[rng.permutation(N * 8 * C).reshape(N, 8, C) % 3 == 0] = 0
    for r in range(N): x[r][:, :, rng.permutation(C)[:C // 8]] = 0
    x[int(rng.integers(N))].reshape(8, 16, S, Z, 4)[:, :, :, :E] = 0
    return {"x": x.reshape(N, 128, 4 * C), "u": d["u"], "v": d["v"], **weights(rng)}
def setup_inputs_cones(rng):
    d = numbers_of(rng)
    x = d["x"].astype(np.float32).reshape(N, 8, 16, C, 4)
    u = d["u"].reshape(N, 128, 128, 4)
    x[:, :, :8] = 0
    u[:, :, ::16] = 0
    c, k = np.arange(C) // Z, np.arange(C) % Z
    o = rng.permutation(8)
    low = int(o[2])
    size = np.where(rng.permutation(N) < N // 2, 2.0 ** -30, 1.0)
    for r in range(N):
        m, n = rng.integers(E + 1, S - E, 2)
        at = int(rng.integers(E, S - E))
        one = 2 * int(rng.integers(E // 2, (S - E) // 2)) + 1
        even = c % 2 == 0
        side = c < m if r % 2 else c >= n
        h = r // 2 % 2 * (E - 2)
        cone = (k + np.abs(c - (S - 1 - h if r % 2 else h)) < E)
        more = rng.permutation(np.flatnonzero(cone & ~side))
        side[more[:int(np.sum(cone)) // 2 + 1 - int(np.sum(cone & side))]] = True
        kinds = [even, ~even, side, k + np.abs(c - at) < E, even | (c == one) & (k == 0)]
        rich = np.zeros((8, C), bool)
        rich[o[r % 2]] = True
        rich[low] = (k <= 2 * E) | (k == Z - 1)
        for g, i in zip(o[3:], rng.permutation(5)): rich[g] = kinds[i]
        small = np.where(np.arange(8) == low, 2.0 ** -30, size[r])
        mark = np.where(rich, 1, -rng.integers(0, 2, (8, C))) * small[:, None]
        for g in rng.permutation(np.delete(o, 2))[:4]:
            j = int(rng.integers(C))
            mark[g, j] = 2.0 ** 30 if rich[g, j] else -2.0 ** 30
        x[r, :, 0, :, 0] = mark
        x[r, low, 7, :, 0] = 2.0 ** -30
        for g in range(8): u[r, 16 * g, 16 * g, 0] = small[g]
        u[r, 16 * low + 1, 16 * low, 0] = 2.0 ** -30
    return {"x": x.reshape(N, 128, 4 * C).astype(BF), "u": u.reshape(N, 128, 512), "v": d["v"], **weights(rng, range(8), [low])}
def setup_inputs_huge(rng):
    d = numbers_of(rng)
    x = 2.0 ** 30 * (0.8 + 0.2 * rng.random((N, 128, C, 4)))
    c = np.stack([rng.permutation(C) % 2 * 2.0 - 1.0 for r in range(N)])
    c[rng.permutation(N) < N // 2] = 1
    x *= c[:, None, :, None]
    u = d["u"].reshape(N, 128, 8, 16, 4)
    s = np.stack([rng.permutation(8) % 2 * 2.0 - 1.0 for r in range(N)])
    a = 2.0 ** 30 * (1 - 0.1 * rng.random((N, 128, 8, 4))) * s[:, None, :, None]
    u[:, :, :, 0] = a.astype(np.float32).astype(BF)
    w = np.zeros((N, 128, 4, 128, 4), np.float32)
    i = np.arange(128)
    for b in range(4): w[:, i, b, i, b] = -1
    wc, ws = packed(w.reshape(N, 128, 2048).astype(BF), rng)
    return {"x": x.astype(np.float32).reshape(N, 128, 4 * C).astype(BF), "u": u.reshape(N, 128, 512), "v": d["v"], "wc": wc, "ws": ws}
def setup_inputs_spread(rng):
    d = setup_inputs(rng)
    d["x"] = big(wide(rng, N, 128, 4 * C, cols=6))
    return d
def check_inputs(d):
    b = []
    for k in ("x", "u", "v"):
        a = np.abs(d[k].astype(np.float32))
        if not (np.isfinite(a).all() and ((a == 0) | (a >= 2.0 ** -30) & (a <= 2.0 ** 30)).all()): b.append("a value of " + k)
    if ((d["wc"] & 0x7F) == 0x7F).any(): b.append("a code of wc that is no number")
    z = np.zeros((128, 4, 4), np.float32)
    z[:, 1] = 2.0 ** -30
    z[:, 2] = 2.0 ** 30
    c, s = emit(mx_ref.quantize(z.reshape(128, 16).astype(BF)))
    for r in range(N):
        p = mx_ref.live(d["ws"][r])
        if not ((p == s[0, 0]) | (p >= s[0, 1]) & (p <= s[0, 2])).all(): b.append("a scale of ws")
    return b
def reference(x, u, v, wc, ws):
    qu = [mx_ref.quantize(u[r]) for r in range(N)]
    lay = [pk(wc[r], ws[r]) for r in range(N)]
    now = [x[r] for r in range(N)]
    a = []
    for t in range(R):
        a, held, sent = [], [], []
        for r in range(N):
            q = mx_ref.quantize(now[r])
            a.append(cuts(mx_ref.matmul(qu[r], q)))
            held.append(decode(q).astype(BF))
            sent.append(mx_ref.quantize(gcols(held[r], slots(a[r]))))
        for r in range(N):
            s = (r - 1 - t) % N
            d = decode(sent[s])
            h = tile([mx_ref.matmul(pick(lay[r], np.arange(128 * b, 128 * b + 128)), sent[s]) * np.float32(0.015625) + d[:, b::4] for b in range(4)])
            now[r] = gcols(np.concatenate([held[r], h], axis=1), places(a[r], a[s]))
    y, oa = np.zeros((N, 128, C), np.float32), np.zeros((N, 8, S), np.float32)
    oc, osc = np.zeros((N, 128, 4 * C), np.uint8), np.zeros((N, 16, C), np.uint8)
    for r in range(N):
        q = mx_ref.quantize(now[r])
        y[r] = mx_ref.matmul(mx_ref.quantize(v[r]), q)
        oa[r] = a[r]
        oc[r], osc[r] = emit(q)
    return {"y": y, "oa": oa, "oc": oc, "osc": osc}

@@ -1,0 +1,578 @@
+import math
+from concourse.mybir import dt, AluOpType, ActivationFunctionType
+
+S, Z, E, C, A, R = 24, 16, 6, 384, 144, 3
+ZO = 16
+PW = ZO + C + A
+RW = ZO + A
+TP, MID = 160, 240
+NC = 7 * S
+TOPK = S * (S - 1)
+AT_RECEIVER = (True, True, True)
+SPLIT = ("C", "A", "C")
+EARLY = (0, 96)
+LAST = ((0, 256), (256, C))
+X4 = "float8_e4m3fn_x4"
+
+SCRATCH = {"ps": ("psum", [128, 4096], "float32")}
+
+
+def _sb(name, n, dtype):
+    SCRATCH[name] = ("sbuf", [128, n], dtype)
+
+
+def _mx(name, n):
+    _sb("q" + name, n, X4)
+    _sb("s" + name, n, "uint8")
+
+
+for _n, _w in (("xin", 4 * C), ("uin", 512), ("vin", 512), ("eb", 516), ("c64", 128), ("c1k", 16), ("cm", 4 * NC), ("sg", 512),
+               ("x1", 4 * C), ("x2", 4 * C), ("x3", 4 * C)):
+    _sb(_n, _w, "bfloat16")
+for _n, _w in (("x", C), ("u", 128), ("up", 128), ("v", 128), ("w", 512), ("e", 512), ("cone", NC), ("sign", 128), ("m", 128), ("fin", C)):
+    _mx(_n, _w)
+for _t in range(R):
+    _mx("t%d" % _t, C)
+    _mx("r%d" % _t, A)
+    _mx("k%d" % _t, A)
+    _sb("win%d" % _t, 4 * PW, "bfloat16")
+    _sb("bt%d" % _t, 4 * A, "bfloat16")
+    if AT_RECEIVER[_t]:
+        _sb("rw%d" % _t, 4 * RW, "bfloat16")
+    _sb("lst%d" % _t, 48, "uint16")
+    _sb("ml%d" % _t, 24, "uint16")
+    _sb("bl%d" % _t, 24, "uint16")
+    _sb("tg%d" % _t, 72, "float32")
+for _n, _w in (("cr", S), ("far", S), ("room", 8), ("pj", 25), ("kf", 25), ("kq", 25), ("mf", 1), ("tau", 4), ("j25", S), ("j16", S),
+               ("u1", S), ("u2", S), ("u3", S), ("u4", 32), ("sc", 8), ("cl", 42), ("dec", 72), ("cap", NC), ("h", NC),
+               ("d0", 28), ("d1", 28), ("so", 28), ("n0", 48), ("n1", 48), ("no", 48),
+               ("fw", S), ("gn", S), ("g32", S), ("yn", S), ("mn", S), ("lc", S), ("m48", S), ("o1", S), ("o2", S), ("ysb", C)):
+    _sb(_n, _w, "float32")
+for _n, _w in (("pi", 1), ("mi", 1), ("ki", 25)):
+    _sb(_n, _w, "int32")
+for _n, _w in (("ul", 8), ("xl", S)):
+    _sb(_n, _w, "uint16")
+
+SEMAPHORES = ["cV", "cS", "cT", "cG", "sent", "lx0", "lx1", "lu", "lv", "lwc", "lws", "st",
+              "ac0", "ac1", "ac2", "al0", "al1", "al2", "an"]
+
+ADD, SUB, MUL, MAX, MIN = AluOpType.add, AluOpType.subtract, AluOpType.mult, AluOpType.max, AluOpType.min
+GT, LE, LT = AluOpType.is_gt, AluOpType.is_le, AluOpType.is_lt
+AF = ActivationFunctionType
+HOP, SAME = 130, 60
+FAR_BIG, FAR_SMALL, FIRST, LOAD, STORE, CALL = 3000, 2300, 1500, 2600, 2000, 400
+CASES = ((1, 1, 1, 1, 130), (0.85, 0.7, 0.7, 1.3, 200), (1.15, 1.3, 1.3, 0.8, 80))
+PASSES, NOISE, PULL, TRIES, HEAT, SEED = 60, 400.0, 0.1, 24000, 30.0, 1
+BULK, CHAIN = (0, 1, 2, 3, 4), (5, 6, 7)
+_PLAN = {}
+
+
+def build(g, core, T, topo):
+    rank = T.rank_of(core)
+    n_ranks = len(T.cores)
+    V, ACT, PE, SY = g.vector, g.scalar, g.tensor, g.sync
+    ops = []
+
+    def op(alts, reads, writes, **kw):
+        ops.append(dict(alts=alts, reads=list(reads), writes=list(writes), **kw))
+        return len(ops) - 1
+
+    def bank(i):
+        return 512 * ops[i]["bank"]
+
+    def small(n):
+        return max(75, 45 + int(1.04 * n))
+
+    def vop(n, fn, reads, writes, **kw):
+        return op({"V": (small(n), fn)}, reads, writes, **kw)
+
+    def ts(out, in0, s1, s2, o0, o1, n, reads, writes):
+        if o1 is None:
+            return vop(n, lambda: V.tensor_scalar(out, in0, s1, None, o0), reads, writes)
+        return vop(n, lambda: V.tensor_scalar(out, in0, s1, s2, o0, o1), reads, writes)
+
+    def lin(out, in_, scale, bias, n, reads, writes):
+        return op({"V": (small(n), lambda: V.tensor_scalar(out, in_, scale, bias, MUL, ADD)),
+                   "S": (small(n) + 20, lambda: ACT.activation(out, in_, AF.Identity, bias=bias, scale=scale))}, reads, writes)
+
+    def tt(out, a, b, o, n, reads, writes):
+        return vop(2 * n, lambda: V.tensor_tensor(out, a, b, o), reads, writes)
+
+    def cp(out, a, n, reads, writes):
+        return vop(n, lambda: V.tensor_copy(out, a), reads, writes)
+
+    def const(ap, val, n, writes):
+        return op({"V": (small(n // 2), lambda: V.memset(ap, float(val))),
+                   "G": (170 + int(2.1 * n), lambda: g.iota(ap, [[0, n]], val, 0, allow_small_or_imprecise_dtypes=True))}, [], writes)
+
+    def zero(ap, n, writes):
+        return op({"V": (small(n // 2), lambda: V.memset(ap, 0.0)),
+                   "S": (small(n) + 20, lambda: ACT.activation(ap, T.cap[:, 0:n], AF.Copy, scale=0.0))}, ["cap"], writes)
+
+    def scan(out, d0, d1, init, o0, o1, n, reads, writes):
+        return vop(n, lambda: V.tensor_tensor_scan(out, d0, d1, init, o0, o1), reads, writes)
+
+    def iota(out, pat, base, cmul, n, writes, flag=True):
+        if flag:
+            fn = lambda: g.iota(out, pat, base, cmul, allow_small_or_imprecise_dtypes=True)
+        else:
+            fn = lambda: g.iota(out, pat, base, cmul)
+        return op({"G": (170 + int(2.1 * n), fn)}, [], writes)
+
+    def quant(nm, a, b, src, reads, writes):
+        return op({"V": (30 + int(1.1 * (b - a)), lambda: V.quantize_mx(T["q" + nm][:, a:b], T["s" + nm][:, a:b], src))}, reads, writes)
+
+    def side(nm, a, b):
+        return T["q" + nm][:, a:b], T["s" + nm][:, a:b]
+
+    def mm(pairs, n, reads, banks):
+        me = len(ops)
+
+        def fn():
+            last = None
+            for i, (l, r) in enumerate(pairs):
+                last = PE.matmul_mx(T.ps[:, bank(me):bank(me) + n], l[0], l[1], r[0], r[1], i == 0, i == len(pairs) - 1)
+            return last
+        return op({"T": (len(pairs) * int(0.65 * (n + 16)) + 40, fn)}, reads, ["mm%d" % me], banks=banks)
+
+    def evac(src, a, b, out, scale, writes):
+        def view():
+            return T.ps[:, bank(src) + a:bank(src) + b]
+        n = b - a
+        return op({"V": (small(n), lambda: V.tensor_scalar(out, view(), scale, None, MUL)),
+                   "S": (small(n) + 20, lambda: ACT.activation(out, view(), AF.Copy, scale=scale))}, ["mm%d" % src], writes, frees=src)
+
+    def gather(out, win, off, n, reads, writes):
+        return op({"V": (62 + int(1.62 * n), lambda: V.tensor_copy(out, win.indirect(off))),
+                   "S": (82 + int(1.62 * n), lambda: ACT.activation(out, win.indirect(off), AF.Copy))}, reads, writes, kind=1)
+
+    def pick(dst, a, src, w, off, n, reads, tag):
+        op({"V": (62 + int(1.62 * n), lambda: V.tensor_copy(T["q" + dst][:, a:a + n].bitcast(dt.uint32),
+                                                            T["q" + src][:, 0:w].bitcast(dt.uint32).indirect(off)))}, reads, ["q" + tag], kind=1)
+        op({"V": (62 + int(1.62 * n), lambda: V.tensor_copy(T["s" + dst][:, a:a + n], T["s" + src][:, 0:w].indirect(off))),
+            "S": (82 + int(1.62 * n), lambda: ACT.activation(T["s" + dst][:, a:a + n], T["s" + src][:, 0:w].indirect(off), AF.Copy))},
+           reads, ["s" + tag], kind=1)
+
+    def dma(queues, out, in_, sem, lat, reads, writes):
+        alts = {"Y": (100, lambda: SY.dma_start(out, in_)), "S": (100, lambda: ACT.dma_start(out, in_))}
+        return op({q: alts[q] for q in queues}, reads, writes, dsem=sem, lat=lat)
+
+    def send(t, parts, sem, lat, reads, writes):
+        dst, src = T.cores[(rank + 1 + t) % n_ranks], T.cores[(rank - 1 - t) % n_ranks]
+        rid, pid, _ = topo.addr(dst)
+
+        def fn():
+            for o, i in parts:
+                g.remote_dma(o, i, T.sem[sem], T.sem.sent, pid, rid, topo.mask(core, dst))
+            return None
+        return op({"G": (CALL * len(parts), fn)}, reads, writes, rsem=sem, lat=lat,
+                  got=len(parts) * len(topo.engines(src, core)), gone=len(parts) * len(topo.engines(core, dst)))
+
+    dma("S", T.xin[:, 0:768], T.x[:, 0:768], "lx0", LOAD, [], ["xin0"])
+    dma("Y", T.uin[:], T.u[:], "lu", LOAD - 500, [], ["uin"])
+    dma("Y", T.xin[:, 768:1536], T.x[:, 768:1536], "lx1", LOAD, [], ["xin1"])
+    dma("Y", T.qw[:].bitcast(dt.uint8), T.wc[:], "lwc", LOAD, ["xin1"], ["qw"])
+    dma("Y", T.sw[:], T.ws[:], "lws", LOAD, ["xin1"], ["sw"])
+    dma("Y", T.vin[:], T.v[:], "lv", LOAD, ["xin1"], ["vin"])
+
+    J, KQ = T.pj, T.kq
+    iota(T.pi[:], [[0, 1]], 0, 1, 1, ["pi"], False)
+    iota(T.cr[:], [[1, S]], 0, 0, S, ["cr"])
+    iota(J[:, S:S + 1], [[0, 1]], 0, 1, 1, ["pp"])
+    iota(T.cap[:], [[-S, S], [S, 7]], TOPK, 0, NC, ["cap"])
+    for b in range(3):
+        zero(T.eb[:, b:516:4], 129, ["eb%d" % b])
+    const(T.c64[:], 64, 128, ["c64"])
+    op({"G": (480, lambda: g.affine_select(T.eb[:, 3:515:4], T.c64[:], [[-1, 128]], AluOpType.is_equal, 0.0, 0, 1))}, ["c64"], ["eb"])
+    for b in range(4):
+        quant("e", 128 * b, 128 * b + 128, T.eb[:, 3 - b:515 - b], ["eb", "eb0", "eb1", "eb2"], ["e%d" % b])
+    ts(T.mi[:], T.pi[:], Z - 1, None, AluOpType.bitwise_and, None, 1, ["pi"], ["mi"])
+    cp(T.mf[:], T.mi[:], 1, ["mi"], ["mf"])
+    ts(T.ul[:], T.cr[:, 0:8], 16.0, None, MUL, None, 8, ["cr"], ["ul"])
+    lin(J[:, 0:S], T.cr[:], 16.0, T.mf[:], S, ["cr", "mf"], ["pj"])
+    ts(T.kf[:], J[:], -11.5, 1.0 / S, ADD, MUL, 25, ["pj", "pp"], ["kf"])
+    cp(T.ki[:], T.kf[:], 25, ["kf"], ["ki"])
+    cp(KQ[:], T.ki[:], 25, ["ki"], ["kq"])
+    lin(T.j16[:], J[:, 0:S], 16.0, 0.0, S, ["pj"], ["j16"])
+    lin(T.u1[:], KQ[:, 0:S], 1.0 - C, 0.0, S, ["kq"], ["u1"])
+    tt(T.u2[:], T.u1[:], T.j16[:], ADD, S, ["u1", "j16"], ["u2"])
+    cp(T.xl[:], T.u2[:], S, ["u2"], ["xl"])
+    lin(T.sc[:, 0:1], KQ[:, S:S + 1], -float(S), J[:, S:S + 1], 1, ["kq", "pp"], ["sc0"])
+    op({"S": (100, lambda: ACT.activation(T.far[:], T.cr[:], AF.Abs, bias=T.sc[:, 0:1], scale=-1.0))}, ["cr", "sc0"], ["far"])
+    ts(T.room[:], T.cr[:, 0:8], KQ[:, S:S + 1], None, SUB, None, 8, ["cr", "kq"], ["room"])
+    for b in range(1, 4):
+        zero(T.cm[:, b:4 * NC:4], NC, ["cz%d" % b])
+    const(T.c1k[:], 1024, 16, ["c1k"])
+    for e in range(7):
+        ts(T.cm[:, 4 * e:4 * NC:28], T.far[:], T.room[:, e:e + 1], 2048.0, LT, MUL, S, ["far", "room"], ["cm%d" % e])
+    op({"G": (250, lambda: g.affine_select(T.cm[:, 249:4 * NC:28], T.c1k[:], [[-1, 16]], AluOpType.is_equal, 0.0, -112, 1))},
+       ["c1k", "cz1"], ["cz1"])
+    quant("cone", 0, NC, T.cm[:], ["cm%d" % e for e in range(7)] + ["cz1", "cz2", "cz3"], ["cone"])
+    zero(T.sg[:, 2:512:4], 128, ["sg2"])
+    zero(T.sg[:, 3:512:4], 128, ["sg3"])
+    for i in range(3):
+        lin(T.tau[:, i:i + 1], KQ[:, i:i + 1], -float(S), J[:, i:i + 1], 1, ["kq", "pj"], ["tau%d" % i])
+        ts(T.dec[:, S * i:S * i + S], T.cr[:], T.tau[:, i:i + 1], -48.0, LE, MUL, S, ["cr", "tau%d" % i], ["dec%d" % i])
+    lin(T.j25[:], J[:, 0:S], 25.0, 0.0, S, ["pj"], ["j25"])
+    lin(T.u3[:], KQ[:, 0:S], -576.0, -float(TOPK), S, ["kq"], ["u3"])
+    tt(T.cl[:, 0:24], T.u3[:], T.j25[:], ADD, S, ["u3", "j25"], ["cl0"])
+    lin(T.u4[:, 0:9], KQ[:, 0:9], -624.0, float(ZO - S - TOPK), 9, ["kq"], ["u4a"])
+    tt(T.cl[:, 24:33], T.u4[:, 0:9], T.j25[:, 0:9], ADD, 9, ["u4a", "j25"], ["cl1"])
+    lin(T.cl[:, 33:42], KQ[:, 0:9], -24.0, float(A), 9, ["kq"], ["cl2"])
+    lin(T.u4[:, 16:25], KQ[:, 0:9], -48.0, 120.0, 9, ["kq"], ["u4b"])
+    const(T.d1[:, 1:10:2], 0, 5, ["d1m"])
+    const(T.d0[:, 1:10:2], 4096, 5, ["d0m"])
+    tt(T.d1[:, 11:28:2], T.u4[:, 16:25], J[:, 0:9], ADD, 9, ["u4b", "pj"], ["d1o"])
+    const(T.d0[:, 0:28:2], -1, 14, ["d0e"])
+    const(T.n0[:, 0:48:2], -1, S, ["n0e"])
+    const(T.m48[:], -48, S, ["m48"])
+    lin(T.sc[:, 2:3], T.mf[:], 24.0, -float(TOPK), 1, ["mf"], ["sc2"])
+    lin(T.sc[:, 3:4], T.mf[:], -24.0, 360.0, 1, ["mf"], ["sc3"])
+    lin(T.sc[:, 4:5], T.mf[:], -768.0, 32.0 * C, 1, ["mf"], ["sc4"])
+    ts(T.sc[:, 5:6], T.mf[:], 24.0, T.sc[:, 3:4], MUL, MIN, 1, ["mf", "sc3"], ["sc5"])
+    lin(T.lc[:], T.cr[:], 25.0, T.sc[:, 2:3], S, ["cr", "sc2"], ["lc"])
+    lin(T.n1[:, 1:48:2], T.cr[:], 1.0, T.sc[:, 5:6], S, ["cr", "sc5"], ["n1o"])
+    for t in range(R):
+        buf, w = (T["rw%d" % t], RW) if AT_RECEIVER[t] else (T["win%d" % t], PW)
+        for b in range(4):
+            const(buf[:, b * w:b * w + ZO], 0, ZO, ["z%d_%d" % (t, b)])
+    CL = ["cl0", "cl1", "cl2"]
+
+    quant("u", 0, 128, T.uin[:], ["uin"], ["u"])
+    pick("up", 0, "u", 128, T.ul[:], 128, ["u", "ul"], "up")
+    quant("v", 0, 128, T.vin[:], ["vin"], ["v"])
+    quant("x", 0, 192, T.xin[:, 0:768], ["xin0"], ["xa"])
+    quant("x", 192, C, T.xin[:, 768:1536], ["xin1"], ["xb"])
+    pick("t0", 0, "x", C, T.xl[:, 0:10], TP, ["xa", "xb", "xl"], "t0")
+    pick("t0", TP, "x", C, T.xl[:, 10:24], C - TP, ["xa", "xb", "xl"], "b0")
+
+    def unpack(nm, c0, n, a, dst, width, at, need, tags):
+        for p in range(4):
+            m = mm([(side("e", 128 * p, 128 * p + 128), side(nm, c0, c0 + n))], n, ["e%d" % p] + [x + y for x in "qs" for y in need], BULK)
+            o = p * width + at
+            evac(m, a, n, dst[:, o:o + n - a], 0.015625, ["%s_%d" % (x, p) for x in tags])
+
+    for t in range(R):
+        win, lst, ml, bl, tg = (T[n + str(t)] for n in ("win", "lst", "ml", "bl", "tg"))
+        top, rr, kk = "t%d" % t, "r%d" % t, "k%d" % t
+        codes = lambda nm: [(T["q" + rr][:].bitcast(dt.uint8), T["q" + nm][:, 0:A].bitcast(dt.uint8)), (T["s" + rr][:], T["s" + nm][:, 0:A])]
+        big = FAR_BIG + (FIRST if t == 0 else 0)
+        if AT_RECEIVER[t]:
+            send(t, codes(top), "ac%d" % t, big, ["q" + top, "s" + top], ["q" + rr, "s" + rr])
+        p0 = mm([(side(top, 0, 128), side("up", 0, 128))], 128, ["q" + top, "s" + top, "qup", "sup"], CHAIN)
+        p1 = mm([(side(top, 16, A), side("up", 0, 128))], 128, ["q" + top, "s" + top, "qup", "sup"], CHAIN)
+        vop(128, lambda p0=p0: V.tensor_scalar(T.sg[:, 0:512:4], T.ps[:, bank(p0):bank(p0) + 128], 0.0, 0.5, GT, SUB),
+            ["mm%d" % p0], ["sg0"], frees=p0)
+        op({"S": (200, lambda p1=p1: ACT.activation(T.sg[:, 1:512:4], T.ps[:, bank(p1):bank(p1) + 128], AF.Sign, bias=-1e-37))},
+           ["mm%d" % p1], ["sg1"], frees=p1)
+        quant("sign", 0, 128, T.sg[:], ["sg0", "sg1", "sg2", "sg3"], ["sign"])
+        pc = mm([(side("sign", 0, 128), side("cone", 0, NC))], NC, ["sign", "cone"], CHAIN)
+        vop(NC, lambda pc=pc: V.tensor_tensor_scan(T.h[:], T.ps[:, bank(pc):bank(pc) + NC], T.cap[:], float(TOPK), MAX, MIN),
+            ["mm%d" % pc, "cap"], ["h"], frees=pc)
+        lo, hi = (24, 33) if t == R - 1 else (0, 42)
+        for i in range(3):
+            scan(tg[:, S * i:S * i + S], T.dec[:, S * i:S * i + S], T.h[:, 6:NC:7], 0.0, ADD, MAX, S, ["h", "dec%d" % i], ["tg%d_%d" % (t, i)])
+            ts(lst[:, lo + i:hi:3], T.cl[:, lo + i:hi:3], tg[:, S * i + S - 1:S * i + S], 0.0, ADD, MAX, 14, CL + ["tg%d_%d" % (t, i)], ["l%d_%d" % (t, i)])
+        L = ["l%d_%d" % (t, i) for i in range(3)]
+        first = 24 if AT_RECEIVER[t] else 33
+        if first < hi:
+            send(t, [(ml[:, first - 24:hi - 24], lst[:, first:hi])], "al%d" % t, FAR_SMALL, L, ["ml%d" % t])
+        ta, tm, tb, low = "Ta%d" % t, "Tm%d" % t, "Tb%d" % t, "b%d" % t
+        if SPLIT[t] == "C":
+            unpack(top, 0, C, 0, win, PW, ZO, [top, low], [ta, tm, tb])
+        else:
+            unpack(top, 0, TP, 0, win, PW, ZO, [top], [ta])
+        if SPLIT[t] == "B":
+            unpack(top, TP, C - TP, 0, win, PW, ZO + TP, [low], [tm, tb])
+        if SPLIT[t] == "A":
+            unpack("m", 0, 128, 128 - (MID - TP), win, PW, ZO + TP, ["m"], [tm])
+            unpack(top, MID, A, 0, win, PW, ZO + MID, [low], [tb])
+        Tn = lambda b: ["%s_%d" % (x, b) for x in (ta, tm, tb)]
+        bt = T["bt%d" % t]
+        if AT_RECEIVER[t]:
+            rw = T["rw%d" % t]
+            unpack(rr, 0, A, 0, rw, RW, ZO, [rr], ["Ra%d" % t])
+            for b in range(4):
+                gather(bt[:, b:4 * A:4], rw[:, b * RW:b * RW + RW], ml[:, 0:9], A, ["Ra%d_%d" % (t, b), "z%d_%d" % (t, b), "ml%d" % t], ["bt%d_%d" % (t, b)])
+            use = kk
+        else:
+            for b in range(4):
+                gather(bt[:, b:4 * A:4], win[:, b * PW:b * PW + RW], lst[:, 24:33], A, ["Ta%d_%d" % (t, b), "z%d_%d" % (t, b)] + L, ["bt%d_%d" % (t, b)])
+            use = rr
+        quant(kk, 0, A, bt[:], ["bt%d_%d" % (t, b) for b in range(4)], ["q" + kk, "s" + kk])
+        if not AT_RECEIVER[t]:
+            send(t, codes(kk), "ac%d" % t, big, ["q" + kk, "s" + kk], ["q" + rr, "s" + rr])
+        for b in range(4):
+            m = mm([(side("w", 128 * b, 128 * b + 128), side(use, 0, A)), (side("e", 128 * b, 128 * b + 128), side(use, 0, A))], A,
+                   ["qw", "sw", "e%d" % b, "q" + use, "s" + use], BULK)
+            evac(m, 0, A, win[:, b * PW + ZO + C:b * PW + PW], 0.015625, ["H%d_%d" % (t, b)])
+        xn = T["x%d" % (t + 1)]
+        if t < R - 1:
+            cp(T.d1[:, 0:28:2], lst[:, 10:24], 14, L, ["d1e"])
+            for i in range(3):
+                ts(T.d0[:, 11 + 2 * i:28:6], ml[:, 9 + i:18:3], tg[:, S * i + S - 1:S * i + S], 4096.0, GT, MUL, 3,
+                   ["ml%d" % t, "tg%d_%d" % (t, i)], ["d0o%d" % i])
+            scan(T.so[:], T.d0[:], T.d1[:], 0.0, MIN, MAX, 28, ["d0m", "d1m", "d0e", "d0o0", "d0o1", "d0o2", "d1e", "d1o"], ["so"])
+            apart = SPLIT[t + 1] == "A"
+            if apart:
+                cp(bl[:, 0:9], T.so[:, 11:28:2], 9, ["so"], ["bl%d" % t])
+            else:
+                cp(bl[:, 0:14], T.so[:, 1:28:2], 14, ["so"], ["bl%d" % t])
+            c0, c1 = MID if apart else TP, EARLY[t]
+            for b in range(4):
+                w = win[:, b * PW + ZO:b * PW + ZO + C]
+                if c1:
+                    gather(xn[:, b:4 * c1:4], win[:, b * PW + ZO:b * PW + ZO + MID], lst[:, 0:c1 // 16], c1, Tn(b)[:2] + L, ["xe%d_%d" % (t, b)])
+                gather(xn[:, 4 * c1 + b:4 * TP:4], w, lst[:, c1 // 16:10], TP - c1, Tn(b) + L, ["xt%d_%d" % (t, b)])
+                if apart:
+                    gather(xn[:, 4 * TP + b:4 * MID:4], w, lst[:, 10:15], MID - TP, Tn(b) + L, ["xm%d_%d" % (t, b)])
+                gather(xn[:, 4 * c0 + b:4 * C:4], win[:, b * PW + ZO:b * PW + PW], bl[:, 0:(C - c0) // 16], C - c0,
+                       Tn(b) + ["H%d_%d" % (t, b), "bl%d" % t], ["xb%d_%d" % (t, b)])
+            four = lambda s: ["%s%d_%d" % (s, t, b) for b in range(4)]
+            nt = "t%d" % (t + 1)
+            quant(nt, 0, TP, xn[:, 0:4 * TP], four("xt") + (four("xe") if c1 else []), ["q" + nt, "s" + nt])
+            if apart:
+                quant("m", 0, 128, xn[:, 4 * (MID - 128):4 * MID], four("xt") + four("xm"), ["qm", "sm"])
+            quant(nt, c0, C, xn[:, 4 * c0:4 * C], four("xb"), ["qb%d" % (t + 1), "sb%d" % (t + 1)])
+        else:
+            scan(T.fw[:], T.m48[:], T.h[:, 6:NC:7], 0.0, ADD, MAX, S, ["h", "m48"], ["fw"])
+            scan(T.gn[:, ::-1], T.fw[:, ::-1], T.fw[:, ::-1], 0.0, MAX, MAX, S, ["fw"], ["gn"])
+            lin(T.yn[:], T.gn[:], 32.0, T.sc[:, 4:5], S, ["gn", "sc4"], ["yn"])
+            send(t, [(T.mn[:], T.yn[:])], "an", FAR_SMALL, ["yn"] + L, ["mn"])
+            lin(T.g32[:], T.gn[:], 32.0, 0.0, S, ["gn"], ["g32"])
+            tt(T.n1[:, 0:48:2], T.gn[:], T.lc[:], ADD, S, ["gn", "lc"], ["n1e"])
+            tt(T.o1[:], T.gn[:], T.cap[:, 0:NC:7], SUB, S, ["gn", "cap"], ["oa1"])
+            lin(T.o2[:], T.o1[:], 1.0 / S, 0.0, S, ["oa1"], ["oa2"])
+            dma("Y", T.oa[:], T.o2[0:128:16, :], "st", STORE, ["oa2"], ["oa"])
+            tt(T.n0[:, 1:48:2], T.mn[:], T.g32[:], SUB, S, ["mn", "g32"], ["n0o"])
+            scan(T.no[:], T.n0[:], T.n1[:], 0.0, MIN, MAX, 48, ["n0e", "n0o", "n1e", "n1o"], ["no"])
+            cp(bl[:], T.no[:, 1:48:2], S, ["no"], ["bl%d" % t])
+            for hh, (a, z) in enumerate(LAST):
+                for b in range(4):
+                    gather(xn[:, 4 * a + b:4 * z:4], win[:, b * PW + ZO:b * PW + PW], bl[:, a // Z:z // Z], z - a,
+                           Tn(b) + ["H%d_%d" % (t, b), "bl%d" % t], ["xf%d_%d" % (hh, b)])
+                quant("fin", a, z, xn[:, 4 * a:4 * z], ["xf%d_%d" % (hh, b) for b in range(4)], ["o%d" % hh])
+                dma("Y", T.oc[:, 4 * a:4 * z], T.qfin[:, a:z].bitcast(dt.uint8), "st", STORE, ["o%d" % hh], ["oc%d" % hh])
+                m = mm([(side("v", 0, 128), side("fin", a, z))], z - a, ["v", "o%d" % hh], BULK)
+                evac(m, 0, z - a, T.ysb[:, a:z], 1.0, ["ysb%d" % hh])
+                dma("YS", T.y[:, a:z], T.ysb[:, a:z], "st", STORE, ["ysb%d" % hh], ["y%d" % hh])
+            for k in range(4):
+                dma("YS", T.osc[4 * k:4 * k + 4, :], T.sfin[32 * k:32 * k + 4, :], "st", STORE, ["o0", "o1"], ["osc%d" % k])
+    writer, readers = {}, {}
+    for i, o in enumerate(ops):
+        d = set(writer[r] for r in o["reads"])
+        for w in o["writes"]:
+            if w in writer:
+                d.add(writer[w])
+            d.update(readers.get(w, []))
+        d.discard(i)
+        o["deps"] = d
+        for r in o["reads"]:
+            readers.setdefault(r, []).append(i)
+        for w in o["writes"]:
+            writer[w] = i
+            readers[w] = []
+    late = [i for i, o in enumerate(ops) if "qr0" in o["reads"] and "banks" in o]
+    for i in late:
+        ops[i]["soft"] = [k for k, o in enumerate(ops) if "qt1" in o["reads"] and "qup" in o["reads"]]
+    return ops
+
+
+def place(rows, links, seq, back):
+    busy = dict(V=[], S=[], T=[], G=[], Y=[])
+    start, done, where, held = {}, {}, {}, {BULK: [], CHAIN: []}
+
+    def gap(e, t, d):
+        for s, f in busy[e]:
+            if s >= t + d:
+                break
+            if f > t:
+                t = f
+        return t
+
+    def best(i, t0):
+        c = None
+        for e, d in rows[i][5].items():
+            t = t0
+            for k in links[i]:
+                lat = rows[i][1] if back else rows[k][1]
+                t = max(t, done[k] + lat + (HOP if where[k] != e or lat else SAME))
+            t = gap(e, t, d)
+            if c is None or t + d < c[0]:
+                c = (t + d, t, e)
+        return c
+
+    def put(i, c):
+        done[i], start[i], where[i] = c
+        busy[c[2]].append((c[1], c[0]))
+        busy[c[2]].sort()
+
+    for i in seq:
+        if i in done:
+            continue
+        c = best(i, rows[i][1] if back else 0)
+        pool = rows[i][2]
+        if pool and not back:
+            k = rows[i][6]
+            while True:
+                done[i], where[i] = c[0], c[2]
+                r = best(k, 0)
+                over = sorted(f for s, f in held[pool] if s < r[0] + HOP and f + HOP > c[1])
+                if len(over) < len(pool):
+                    break
+                c = best(i, over[0] + HOP + 1)
+            put(i, c)
+            put(k, r)
+            held[pool].append((c[1], r[0]))
+        else:
+            put(i, c)
+    return start, done, where
+
+
+def replay(rows, order, where):
+    banks, extra, holder, total, first, tight = {}, {}, {}, 0, None, []
+    for fc, fg, ft, fl, hop in CASES:
+        free = dict(V=0, S=0, T=0, G=0, Y=0)
+        done, start, why, last = [0] * len(rows), [0] * len(rows), [None] * len(rows), {}
+        for i in order:
+            deps, lat, pool, frees, picks, alts, _ = rows[i]
+            e = where[i]
+            t = free[e]
+            why[i] = last.get(e)
+            last[e] = i
+            for d in deps:
+                u = done[d] + (hop if where[d] != e or rows[d][1] else hop / 2)
+                if u > t:
+                    t, why[i] = u, d
+            if pool:
+                if first is None:
+                    ok = [(done[holder[x]] if x in holder else 0, x) for x in pool if holder.get(x, 0) is not None]
+                    if not ok:
+                        return None
+                    b = min(ok)[1]
+                    if b in holder:
+                        extra[i] = holder[b]
+                    holder[b], banks[i] = None, b
+                if i in extra and done[extra[i]] + hop > t:
+                    t, why[i] = done[extra[i]] + hop, extra[i]
+            elif frees is not None and first is None:
+                holder[banks[frees]] = i
+            start[i] = t
+            t += alts[e] * (ft if e == "T" else fg if picks else fc)
+            free[e], done[i] = t, t + fl * lat
+        if first is None:
+            first = (max(done), start)
+        i = done.index(max(done))
+        while why[i] is not None:
+            if why[i] not in rows[i][0]:
+                tight.append((why[i], i))
+            i = why[i]
+        total += max(done) + PULL * sum(done) / len(done)
+    return total / len(CASES), first[0], banks, extra, first[1], tight
+
+
+def plan(ops):
+    if _PLAN:
+        return _PLAN["best"]
+    n, seed = len(ops), [SEED]
+
+    def rnd():
+        seed[0] = (seed[0] * 1103515245 + 12345) % 2147483648
+        return seed[0] / 2147483648
+    users = [[] for _ in ops]
+    for i, o in enumerate(ops):
+        for d in o["deps"] | set(o.get("soft", [])):
+            users[d].append(i)
+    rows = [[sorted(o["deps"] | set(o.get("soft", []))), o.get("lat", 0), o.get("banks"), o.get("frees"), "kind" in o,
+             {e: a[0] for e, a in o["alts"].items()}, ([k for k in users[i] if ops[k].get("frees") == i] + [None])[0]] for i, o in enumerate(ops)]
+    deps = [r[0] for r in rows]
+
+    def ranked(key, links, outs):
+        left = [len(x) for x in links]
+        ready, seq = [i for i in range(n) if not left[i]], []
+        while ready:
+            i = min(ready, key=lambda k: key[k])
+            ready.remove(i)
+            seq.append(i)
+            for k in outs[i]:
+                left[k] -= 1
+                if not left[k]:
+                    ready.append(k)
+        return seq
+    dep2 = [sorted(set(r[0]) | (set(rows[r[6]][0]) - {i} if r[2] else set())) for i, r in enumerate(rows)]
+    use2 = [[k for k in range(n) if i in dep2[k]] for i in range(n)]
+    now, key = None, list(range(n))
+    for step in range(PASSES):
+        _, done, _ = place(rows, users, ranked([-x for x in key], users, deps), True)
+        start, done, w = place(rows, deps, ranked([-done[i] + NOISE * rnd() for i in range(n)], dep2, use2), False)
+        o2, w2 = sorted(range(n), key=lambda k: (start[k], k)), [w[i] for i in range(n)]
+        c = replay(rows, o2, w2)
+        if c is not None and (now is None or c[0] < now[0]):
+            now, order, where, keep = c, o2, w2, done
+        key = [(keep if now and step % 3 == 2 else done)[i] + rows[i][1] + NOISE * rnd() for i in range(n)]
+    best = (now, order, where)
+    for step in range(TRIES):
+        o2, w2 = order, where
+        i, aim = int(rnd() * n), None
+        if now[5] and rnd() < 0.6:
+            i, aim = now[5][int(rnd() * len(now[5]))]
+            if rnd() < 0.5:
+                i, aim = aim, i
+        if len(rows[i][5]) > 1 and rnd() < 0.3:
+            w2 = list(where)
+            w2[i] = [e for e in sorted(rows[i][5]) if e != where[i]][0]
+        if w2 is where or rnd() < 0.5:
+            o2 = list(order)
+            at = o2.index(i)
+            del o2[at]
+            lo = max([o2.index(d) + 1 for d in rows[i][0]] + [0])
+            hi = min([o2.index(d) for d in users[i]] + [n - 1])
+            to = at + int((rnd() - 0.5) * 2 * 60 * rnd() ** 2)
+            if aim is not None:
+                to = o2.index(aim)
+                to = to + 1 + int(20 * rnd() ** 3) if to >= at else to - int(20 * rnd() ** 3)
+            o2.insert(min(hi, max(lo, to)), i)
+        c = replay(rows, o2, w2)
+        if c is not None and c[0] <= now[0] - HEAT * (1.0 - step / TRIES) ** 2 * math.log(rnd() + 1e-9):
+            now, order, where = c, o2, w2
+            if c[0] < best[0][0]:
+                best = (c, o2, w2)
+    _PLAN["best"] = (best[0][1], best[1], best[2]) + best[0][2:5]
+    _PLAN["cost"] = best[0][0]
+    return _PLAN["best"]
+
+
+def rank_program(g, core, T, topo):
+    if T.rank_of(core) is None:
+        return
+    ops = build(g, core, T, topo)
+    _, order, where, banks, extra, _ = plan(ops)
+    for i, b in banks.items():
+        ops[i]["bank"] = b
+    for i, d in extra.items():
+        ops[i]["deps"].add(d)
+    queue = dict(V=g.vector, S=g.scalar, T=g.tensor, G=g, Y=g.sync)
+    count, mark, seen = {}, {}, {}
+    for i in order:
+        o, e = ops[i], where[i]
+        need = {}
+        for d in o["deps"]:
+            s, v = mark[d]
+            need[s] = max(need.get(s, 0), v)
+        for s, v in sorted(need.items()):
+            if seen.get((e, s), 0) < v:
+                queue[e].wait_ge(T.sem[s], v)
+                seen[(e, s)] = v
+        ins = o["alts"][e][1]()
+        if "rsem" in o:
+            s = o["rsem"]
+            count[s] = count.get(s, 0) + o["got"]
+            count["sent"] = count.get("sent", 0) + o["gone"]
+        else:
+            s, inc = (o["dsem"], 16) if "dsem" in o else ("c" + e, 1)
+            ins.then_inc(T.sem[s], inc)
+            count[s] = count.get(s, 0) + inc
+        mark[i] = (s, count[s])
+    for s, v in sorted(count.items()):
+        if max([w for (e, s2), w in seen.items() if s2 == s] + [0]) < v:
+            g.sync.wait_ge(T.sem[s], v)

@@ -1,578 +1,389 @@
-import math
 from concourse.mybir import dt, AluOpType, ActivationFunctionType
 
-S, Z, E, C, A, R = 24, 16, 6, 384, 144, 3
-ZO = 16
-PW = ZO + C + A
-RW = ZO + A
-TP, MID = 160, 240
+S, C, A, R = 24, 384, 144, 3
+ROW = 4 * S
+ZP = ROW
+MID = 10 * S
+E2 = 2 * S
 NC = 7 * S
-TOPK = S * (S - 1)
-AT_RECEIVER = (True, True, True)
-SPLIT = ("C", "A", "C")
-EARLY = (0, 96)
-LAST = ((0, 256), (256, C))
+TOPV = ROW * (S - 1)
+BIG = 8192.0
 X4 = "float8_e4m3fn_x4"
+SPLIT = True
+LAST = ((0, 128), (128, 256), (256, C))
 
 SCRATCH = {"ps": ("psum", [128, 4096], "float32")}
-
-
-def _sb(name, n, dtype):
-    SCRATCH[name] = ("sbuf", [128, n], dtype)
-
-
-def _mx(name, n):
-    _sb("q" + name, n, X4)
-    _sb("s" + name, n, "uint8")
-
-
-for _n, _w in (("xin", 4 * C), ("uin", 512), ("vin", 512), ("eb", 516), ("c64", 128), ("c1k", 16), ("cm", 4 * NC), ("sg", 512),
-               ("x1", 4 * C), ("x2", 4 * C), ("x3", 4 * C)):
-    _sb(_n, _w, "bfloat16")
-for _n, _w in (("x", C), ("u", 128), ("up", 128), ("v", 128), ("w", 512), ("e", 512), ("cone", NC), ("sign", 128), ("m", 128), ("fin", C)):
-    _mx(_n, _w)
-for _t in range(R):
-    _mx("t%d" % _t, C)
-    _mx("r%d" % _t, A)
-    _mx("k%d" % _t, A)
-    _sb("win%d" % _t, 4 * PW, "bfloat16")
-    _sb("bt%d" % _t, 4 * A, "bfloat16")
-    if AT_RECEIVER[_t]:
-        _sb("rw%d" % _t, 4 * RW, "bfloat16")
-    _sb("lst%d" % _t, 48, "uint16")
-    _sb("ml%d" % _t, 24, "uint16")
-    _sb("bl%d" % _t, 24, "uint16")
-    _sb("tg%d" % _t, 72, "float32")
-for _n, _w in (("cr", S), ("far", S), ("room", 8), ("pj", 25), ("kf", 25), ("kq", 25), ("mf", 1), ("tau", 4), ("j25", S), ("j16", S),
-               ("u1", S), ("u2", S), ("u3", S), ("u4", 32), ("sc", 8), ("cl", 42), ("dec", 72), ("cap", NC), ("h", NC),
-               ("d0", 28), ("d1", 28), ("so", 28), ("n0", 48), ("n1", 48), ("no", 48),
-               ("fw", S), ("gn", S), ("g32", S), ("yn", S), ("mn", S), ("lc", S), ("m48", S), ("o1", S), ("o2", S), ("ysb", C)):
-    _sb(_n, _w, "float32")
-for _n, _w in (("pi", 1), ("mi", 1), ("ki", 25)):
-    _sb(_n, _w, "int32")
-for _n, _w in (("ul", 8), ("xl", S)):
-    _sb(_n, _w, "uint16")
+for _d, _bufs in (
+        ("bfloat16", dict(xin=4 * (E2 + C), uin=512, vin=512, eb=516, c64=NC, cw=16, cm=4 * NC, sg=512, x1=4 * C, x2=4 * C, x3=4 * C,
+                          w0=ZP + 4 * (C + A), w1=ZP + 4 * (C + A), w2=4 * (C + A), rw0=ZP + 4 * A, rw2=ZP + 4 * A,
+                          bt0=4 * A, bt1=4 * A, bt2=4 * A)),
+        ("float32", dict(cr=S, crp=S, crm=S, xv=S, far=S, room=8, pj=8, kf=8, kq=2, ku=6, kv=6, mf=4, sc=8, cap=NC, h=NC, fw=S, v24=S, dec=6 * S,
+                         df=S, cl=96, tg0=6 * S, tg1=6 * S, tg2=6 * S, th=8, mn=S, dd=S, o1=S, o2=S,
+                         g3=36, g4=96, g5=96, g6=48, cf=96, cg=96, b0=96, b1=96, bo=72, f0=192, f1=192, fo=192, ysb=C)),
+        ("int32", dict(pi=2, mi=4, ki=8)),
+        ("uint16", dict(ul=8, xl=S, rth=4, rp4=6, ls0=132, ls1=132, ls2=72, lf=96, ml0=42, ml1=8, ml2=36))):
+    for _n, _w in _bufs.items():
+        SCRATCH[_n] = ("sbuf", [128, _w], _d)
+for _n, _w in dict(x=C, u=128, up=128, v=128, w=512, e=512, cone=NC, sign=128, t0=C, t1=A, m1=MID, n1=A, o1=128, t2=C, fin=C,
+                   r0=A, r1=A, r2=A, ke=128, k0=A, k1=A, k2=A).items():
+    SCRATCH["q" + _n] = ("sbuf", [128, _w], X4)
+    SCRATCH["s" + _n] = ("sbuf", [128, _w], "uint8")
 
 SEMAPHORES = ["cV", "cS", "cT", "cG", "sent", "lx0", "lx1", "lu", "lv", "lwc", "lws", "st",
               "ac0", "ac1", "ac2", "al0", "al1", "al2", "an"]
 
 ADD, SUB, MUL, MAX, MIN = AluOpType.add, AluOpType.subtract, AluOpType.mult, AluOpType.max, AluOpType.min
-GT, LE, LT = AluOpType.is_gt, AluOpType.is_le, AluOpType.is_lt
+GT, GE, LT, LE = AluOpType.is_gt, AluOpType.is_ge, AluOpType.is_lt, AluOpType.is_le
+AND, SHR = AluOpType.bitwise_and, AluOpType.logical_shift_right
 AF = ActivationFunctionType
-HOP, SAME = 130, 60
-FAR_BIG, FAR_SMALL, FIRST, LOAD, STORE, CALL = 3000, 2300, 1500, 2600, 2000, 400
-CASES = ((1, 1, 1, 1, 130), (0.85, 0.7, 0.7, 1.3, 200), (1.15, 1.3, 1.3, 0.8, 80))
-PASSES, NOISE, PULL, TRIES, HEAT, SEED = 60, 400.0, 0.1, 24000, 30.0, 1
-BULK, CHAIN = (0, 1, 2, 3, 4), (5, 6, 7)
-_PLAN = {}
+BULK = 6
+
+ORDER = {'Y': 'lu lx0 lx1 lws lwc lv oc2 oc1 os3 os2 y2 os0 y0', 'G': 'pi pp pi16 cr xv eb crp cw cz0 cm0 sz3 cap cla clb clc sc0s zw0 g3 bz g5 g6 g4 sl0 fz df sl1 sc1s sc2s sl2 sn', 'T': 'pb0 p0 mT2 mT3 pc0 mT0 mT1 mRa3 mRa2 mRa1 mRa0 pb1 p1 mU2 mU0 pc1 mHe2 mHe3 mHe1 mHe0 mU1 mU3 mH2 mH1 mH3 mH0 mV1 mV2 mV3 mV0 pb2 p2 mW3 mW2 mW1 mW0 pc2 mI2 mI1 mI0 mI3 mRc0 mRc3 mRc1 mRc2 mX2 mX1 mX0 mX3 mJ2 mJ3 mJ1 mJ0 my2 my1 my0', 'V': 'c64 fz1 mi0 ez1 mi2 mi1 mi3 ki0 mf ul kq k24 xl2 crm xl0 room qu xl1 qe2 upq cm2 qx0 qx1 cm3 cm1 cm4 taq cm6 tbq cm5 qe3 sa0 qcone qs0 qe0 dec2 dec4 dec5 qe1 dec1 h0 dec0 dec3 ki1 tg02 tg00 tg05 tg03 tg04 tg01 ls00 ls05 ls03 ls02 ls01 ls04 ku xa0 kv e0 cg qt1 Ra3 Ra1 qm1 sa1 be0 th0 qs1 qke rth U2 f0 h1 cf bo0 tg12 tg13 tg10 tg15 lb0 qk0 tg11 ls12 ls15 ls13 tg14 ls10 U1 ls14 ls11 qn1 H2 bb1 V1 V2 V3 V0 qk1 xe0 H3 own2 qt2 xh0 e1 qo1 sa2 th1 rp4 qs2 f1 W2 W1 bo1 h2 lb1 tg22 tg20 tg24 tg25 tg21 ls22 tg23 ls24 ls20 ls25 ls21 ls23 fw v24 xf1 Rc3 qn2 e2 o1 bc0 o2 dd qk2 f2 fo X3 lf J0 qv xg20 xg10 qf2 xg00 qf1 qf0 ys2 ys1 ys0', 'S': 'ez0 kf0 fz3 ez2 cz1 sc4 sc3 sc0 cz3 sc2 far sz2 j1 ups zrw2 cz2 tas tbs zw1 sb0 kf1 cl T2 T3 T0 T1 zrw0 xa1 xb0 Ra2 Ra0 sb1 be1 sc1 own1 ba1 U0 ba0 He2 He3 He1 He0 xc0 xc1 U3 H1 bb0 xd0 xe1 H0 xh1 own3 sb2 W3 W0 I2 I1 I0 I3 xf0 Rc0 Rc2 Rc1 bc1 X2 X1 X0 J2 J3 J1 xg21 xg11 xg01 oa oc0 os1 y1'}
 
 
-def build(g, core, T, topo):
-    rank = T.rank_of(core)
-    n_ranks = len(T.cores)
+def steps(g, core, T, topo):
+    rank, n_ranks = T.rank_of(core), len(T.cores)
     V, ACT, PE, SY = g.vector, g.scalar, g.tensor, g.sync
-    ops = []
+    ops, bank = {}, {}
 
-    def op(alts, reads, writes, **kw):
-        ops.append(dict(alts=alts, reads=list(reads), writes=list(writes), **kw))
-        return len(ops) - 1
+    def op(name, alts, reads, writes=None, **kw):
+        ops[name] = dict(alts=alts, reads=reads.split(), writes=(name if writes is None else writes).split(), **kw)
 
-    def bank(i):
-        return 512 * ops[i]["bank"]
+    def psum(name, a, z):
+        return T.ps[:, 512 * bank[name] + a:512 * bank[name] + z]
 
-    def small(n):
-        return max(75, 45 + int(1.04 * n))
-
-    def vop(n, fn, reads, writes, **kw):
-        return op({"V": (small(n), fn)}, reads, writes, **kw)
-
-    def ts(out, in0, s1, s2, o0, o1, n, reads, writes):
+    def ts(name, out, in0, s1, s2, o0, o1, reads, writes=None):
         if o1 is None:
-            return vop(n, lambda: V.tensor_scalar(out, in0, s1, None, o0), reads, writes)
-        return vop(n, lambda: V.tensor_scalar(out, in0, s1, s2, o0, o1), reads, writes)
-
-    def lin(out, in_, scale, bias, n, reads, writes):
-        return op({"V": (small(n), lambda: V.tensor_scalar(out, in_, scale, bias, MUL, ADD)),
-                   "S": (small(n) + 20, lambda: ACT.activation(out, in_, AF.Identity, bias=bias, scale=scale))}, reads, writes)
-
-    def tt(out, a, b, o, n, reads, writes):
-        return vop(2 * n, lambda: V.tensor_tensor(out, a, b, o), reads, writes)
-
-    def cp(out, a, n, reads, writes):
-        return vop(n, lambda: V.tensor_copy(out, a), reads, writes)
-
-    def const(ap, val, n, writes):
-        return op({"V": (small(n // 2), lambda: V.memset(ap, float(val))),
-                   "G": (170 + int(2.1 * n), lambda: g.iota(ap, [[0, n]], val, 0, allow_small_or_imprecise_dtypes=True))}, [], writes)
-
-    def zero(ap, n, writes):
-        return op({"V": (small(n // 2), lambda: V.memset(ap, 0.0)),
-                   "S": (small(n) + 20, lambda: ACT.activation(ap, T.cap[:, 0:n], AF.Copy, scale=0.0))}, ["cap"], writes)
-
-    def scan(out, d0, d1, init, o0, o1, n, reads, writes):
-        return vop(n, lambda: V.tensor_tensor_scan(out, d0, d1, init, o0, o1), reads, writes)
-
-    def iota(out, pat, base, cmul, n, writes, flag=True):
-        if flag:
-            fn = lambda: g.iota(out, pat, base, cmul, allow_small_or_imprecise_dtypes=True)
+            op(name, {"V": lambda: V.tensor_scalar(out, in0, s1, None, o0)}, reads, writes)
         else:
-            fn = lambda: g.iota(out, pat, base, cmul)
-        return op({"G": (170 + int(2.1 * n), fn)}, [], writes)
+            op(name, {"V": lambda: V.tensor_scalar(out, in0, s1, s2, o0, o1)}, reads, writes)
 
-    def quant(nm, a, b, src, reads, writes):
-        return op({"V": (30 + int(1.1 * (b - a)), lambda: V.quantize_mx(T["q" + nm][:, a:b], T["s" + nm][:, a:b], src))}, reads, writes)
+    def lin(name, out, in_, scale, bias, reads):
+        op(name, {"V": lambda: V.tensor_scalar(out, in_, scale, bias, MUL, ADD),
+                  "S": lambda: ACT.activation(out, in_, AF.Identity, bias=bias, scale=scale)}, reads)
+
+    def tt(name, out, a, b, o, reads, writes=None):
+        op(name, {"V": lambda: V.tensor_tensor(out, a, b, o)}, reads, writes)
+
+    def cp(name, out, a, reads):
+        op(name, {"V": lambda: V.tensor_copy(out, a)}, reads)
+
+    def scan(name, out, d0, d1, init, o0, o1, reads, writes=None):
+        op(name, {"V": lambda: V.tensor_tensor_scan(out, d0, d1, init, o0, o1)}, reads, writes)
+
+    def iota(name, out, pat, base, cmul=0):
+        op(name, {"G": lambda: g.iota(out, pat, base, cmul, allow_small_or_imprecise_dtypes=True)}, "")
+
+    def const(name, ap, val):
+        n = ap.shape[1]
+        alts = {"V": lambda: V.memset(ap, float(val)), "G": lambda: g.iota(ap, [[0, n]], val, 0, allow_small_or_imprecise_dtypes=True)}
+        if name != "c64":
+            alts["S"] = lambda: ACT.activation(ap, T.c64[:, 0:n], AF.Copy, scale=val / 64.0)
+        op(name, alts, "c64" if "S" in alts else "")
+
+    def quant(name, nm, a, b, src, reads):
+        op(name, {"V": lambda: V.quantize_mx(T["q" + nm][:, a:b], T["s" + nm][:, a:b], src)}, reads)
 
     def side(nm, a, b):
         return T["q" + nm][:, a:b], T["s" + nm][:, a:b]
 
-    def mm(pairs, n, reads, banks):
-        me = len(ops)
-
+    def mm(name, pairs, n, reads, fixed=None):
         def fn():
             last = None
             for i, (l, r) in enumerate(pairs):
-                last = PE.matmul_mx(T.ps[:, bank(me):bank(me) + n], l[0], l[1], r[0], r[1], i == 0, i == len(pairs) - 1)
+                last = PE.matmul_mx(psum(name, 0, n), l[0], l[1], r[0], r[1], i == 0, i == len(pairs) - 1)
             return last
-        return op({"T": (len(pairs) * int(0.65 * (n + 16)) + 40, fn)}, reads, ["mm%d" % me], banks=banks)
+        op(name, {"T": fn}, reads, fixed=fixed)
 
-    def evac(src, a, b, out, scale, writes):
-        def view():
-            return T.ps[:, bank(src) + a:bank(src) + b]
-        n = b - a
-        return op({"V": (small(n), lambda: V.tensor_scalar(out, view(), scale, None, MUL)),
-                   "S": (small(n) + 20, lambda: ACT.activation(out, view(), AF.Copy, scale=scale))}, ["mm%d" % src], writes, frees=src)
+    def evac(name, src, a, z, out, scale):
+        op(name, {"V": lambda: V.tensor_scalar(out, psum(src, a, z), scale, None, MUL),
+                  "S": lambda: ACT.activation(out, psum(src, a, z), AF.Copy, scale=scale)}, src, frees=src)
 
-    def gather(out, win, off, n, reads, writes):
-        return op({"V": (62 + int(1.62 * n), lambda: V.tensor_copy(out, win.indirect(off))),
-                   "S": (82 + int(1.62 * n), lambda: ACT.activation(out, win.indirect(off), AF.Copy))}, reads, writes, kind=1)
+    def gather(name, tile, c0, win, lst, l0, cuts, reads):
+        for i in range(len(cuts) - 1):
+            a, b = cuts[i], cuts[i + 1]
+            out, off = tile[:, 4 * c0 + 16 * a:4 * c0 + 16 * b], lst[:, l0 + a:l0 + b]
+            op("%s%d" % (name, i), {"V": lambda out=out, off=off: V.tensor_copy(out, win.indirect(off)),
+                                    "S": lambda out=out, off=off: ACT.activation(out, win.indirect(off), AF.Copy)}, reads)
+        return " ".join("%s%d" % (name, i) for i in range(len(cuts) - 1))
 
-    def pick(dst, a, src, w, off, n, reads, tag):
-        op({"V": (62 + int(1.62 * n), lambda: V.tensor_copy(T["q" + dst][:, a:a + n].bitcast(dt.uint32),
-                                                            T["q" + src][:, 0:w].bitcast(dt.uint32).indirect(off)))}, reads, ["q" + tag], kind=1)
-        op({"V": (62 + int(1.62 * n), lambda: V.tensor_copy(T["s" + dst][:, a:a + n], T["s" + src][:, 0:w].indirect(off))),
-            "S": (82 + int(1.62 * n), lambda: ACT.activation(T["s" + dst][:, a:a + n], T["s" + src][:, 0:w].indirect(off), AF.Copy))},
-           reads, ["s" + tag], kind=1)
+    def pick(name, dst, a, z, src, w, off, reads):
+        q, s = "q", "s"
+        op(name + q, {"V": lambda: V.tensor_copy(T[q + dst][:, a:z].bitcast(dt.uint32), T[q + src][:, 0:w].bitcast(dt.uint32).indirect(off))}, reads)
+        op(name + s, {"V": lambda: V.tensor_copy(T[s + dst][:, a:z], T[s + src][:, 0:w].indirect(off)),
+                      "S": lambda: ACT.activation(T[s + dst][:, a:z], T[s + src][:, 0:w].indirect(off), AF.Copy)}, reads)
+        return name + q + " " + name + s
 
-    def dma(queues, out, in_, sem, lat, reads, writes):
-        alts = {"Y": (100, lambda: SY.dma_start(out, in_)), "S": (100, lambda: ACT.dma_start(out, in_))}
-        return op({q: alts[q] for q in queues}, reads, writes, dsem=sem, lat=lat)
+    def dma(name, out, in_, sem, reads):
+        op(name, {"Y": lambda: SY.dma_start(out, in_), "S": lambda: ACT.dma_start(out, in_)}, reads, dsem=sem)
 
-    def send(t, parts, sem, lat, reads, writes):
-        dst, src = T.cores[(rank + 1 + t) % n_ranks], T.cores[(rank - 1 - t) % n_ranks]
+    def send(name, t, parts, sem, reads):
+        dst = T.cores[(rank + 1 + t) % n_ranks]
         rid, pid, _ = topo.addr(dst)
+        width = min(len(topo.engines(core, c)) for c in T.cores if c != core)
+        mask = sum(1 << e for e in topo.engines(core, dst)[:width])
 
         def fn():
             for o, i in parts:
-                g.remote_dma(o, i, T.sem[sem], T.sem.sent, pid, rid, topo.mask(core, dst))
-            return None
-        return op({"G": (CALL * len(parts), fn)}, reads, writes, rsem=sem, lat=lat,
-                  got=len(parts) * len(topo.engines(src, core)), gone=len(parts) * len(topo.engines(core, dst)))
+                g.remote_dma(o, i, T.sem[sem], T.sem.sent, pid, rid, mask)
+        op(name, {"G": fn}, reads, rsem=sem, inc=len(parts) * width)
 
-    dma("S", T.xin[:, 0:768], T.x[:, 0:768], "lx0", LOAD, [], ["xin0"])
-    dma("Y", T.uin[:], T.u[:], "lu", LOAD - 500, [], ["uin"])
-    dma("Y", T.xin[:, 768:1536], T.x[:, 768:1536], "lx1", LOAD, [], ["xin1"])
-    dma("Y", T.qw[:].bitcast(dt.uint8), T.wc[:], "lwc", LOAD, ["xin1"], ["qw"])
-    dma("Y", T.sw[:], T.ws[:], "lws", LOAD, ["xin1"], ["sw"])
-    dma("Y", T.vin[:], T.v[:], "lv", LOAD, ["xin1"], ["vin"])
+    def codes(dst, src):
+        return [(T["q" + dst][:].bitcast(dt.uint8), T["q" + src][:, 0:A].bitcast(dt.uint8)), (T["s" + dst][:], T["s" + src][:, 0:A])]
 
-    J, KQ = T.pj, T.kq
-    iota(T.pi[:], [[0, 1]], 0, 1, 1, ["pi"], False)
-    iota(T.cr[:], [[1, S]], 0, 0, S, ["cr"])
-    iota(J[:, S:S + 1], [[0, 1]], 0, 1, 1, ["pp"])
-    iota(T.cap[:], [[-S, S], [S, 7]], TOPK, 0, NC, ["cap"])
+    def product(name, left, nm, n, a, z, dst, at, reads):
+        for b in range(4):
+            mm("m%s%d" % (name, b), [(side(k, 128 * b, 128 * b + 128), side(nm, 0, n)) for k in left], n,
+               "qe%d %s %s" % (b, reads, "lwc lws" if "w" in left else ""))
+            evac(name + str(b), "m%s%d" % (name, b), a, z, dst[:, at + b:at + 4 * (z - a):4], 0.015625)
+        return " ".join(name + str(b) for b in range(4))
+
+    X0 = 4 * E2
+    dma("lx0", T.xin[:, X0:X0 + 768], T.x[:, 0:768], "lx0", "")
+    dma("lx1", T.xin[:, X0 + 768:X0 + 1536], T.x[:, 768:1536], "lx1", "")
+    dma("lu", T.uin[:], T.u[:], "lu", "")
+    dma("lwc", T.qw[:].bitcast(dt.uint8), T.wc[:], "lwc", "lu")
+    dma("lws", T.sw[:], T.ws[:], "lws", "lu")
+    dma("lv", T.vin[:], T.v[:], "lv", "lu")
+
+    sc = T.sc
+    m, mq, hi, m16 = (T.mf[:, i:i + 1] for i in range(4))
+    op("pi", {"G": lambda: g.iota(T.pi[:, 0:1], [[0, 1]], 0, 1)}, "")
+    op("pi16", {"G": lambda: g.iota(T.pi[:, 1:2], [[0, 1]], 0, 16)}, "")
+    iota("xv", T.xv[:], [[129, 3], [2, 8]], 0)
+    iota("cr", T.cr[:], [[1, S]], 0)
+    iota("crp", T.crp[:], [[1, S]], 0, -1)
+    iota("pp", T.pj[:, 6:8], [[0, 2]], 0, 1)
+    iota("cap", T.cap[:], [[-ROW, S], [ROW, 7]], TOPV)
+    const("c64", T.c64[:], 64)
     for b in range(3):
-        zero(T.eb[:, b:516:4], 129, ["eb%d" % b])
-    const(T.c64[:], 64, 128, ["c64"])
-    op({"G": (480, lambda: g.affine_select(T.eb[:, 3:515:4], T.c64[:], [[-1, 128]], AluOpType.is_equal, 0.0, 0, 1))}, ["c64"], ["eb"])
+        const("ez%d" % b, T.eb[:, b:516:4], 0)
+    op("eb", {"G": lambda: g.affine_select(T.eb[:, 3:515:4], T.c64[:, 0:128], [[-1, 128]], AluOpType.is_equal, 0.0, 0, 1)}, "c64")
     for b in range(4):
-        quant("e", 128 * b, 128 * b + 128, T.eb[:, 3 - b:515 - b], ["eb", "eb0", "eb1", "eb2"], ["e%d" % b])
-    ts(T.mi[:], T.pi[:], Z - 1, None, AluOpType.bitwise_and, None, 1, ["pi"], ["mi"])
-    cp(T.mf[:], T.mi[:], 1, ["mi"], ["mf"])
-    ts(T.ul[:], T.cr[:, 0:8], 16.0, None, MUL, None, 8, ["cr"], ["ul"])
-    lin(J[:, 0:S], T.cr[:], 16.0, T.mf[:], S, ["cr", "mf"], ["pj"])
-    ts(T.kf[:], J[:], -11.5, 1.0 / S, ADD, MUL, 25, ["pj", "pp"], ["kf"])
-    cp(T.ki[:], T.kf[:], 25, ["kf"], ["ki"])
-    cp(KQ[:], T.ki[:], 25, ["ki"], ["kq"])
-    lin(T.j16[:], J[:, 0:S], 16.0, 0.0, S, ["pj"], ["j16"])
-    lin(T.u1[:], KQ[:, 0:S], 1.0 - C, 0.0, S, ["kq"], ["u1"])
-    tt(T.u2[:], T.u1[:], T.j16[:], ADD, S, ["u1", "j16"], ["u2"])
-    cp(T.xl[:], T.u2[:], S, ["u2"], ["xl"])
-    lin(T.sc[:, 0:1], KQ[:, S:S + 1], -float(S), J[:, S:S + 1], 1, ["kq", "pp"], ["sc0"])
-    op({"S": (100, lambda: ACT.activation(T.far[:], T.cr[:], AF.Abs, bias=T.sc[:, 0:1], scale=-1.0))}, ["cr", "sc0"], ["far"])
-    ts(T.room[:], T.cr[:, 0:8], KQ[:, S:S + 1], None, SUB, None, 8, ["cr", "kq"], ["room"])
+        quant("qe%d" % b, "e", 128 * b, 128 * b + 128, T.eb[:, 3 - b:515 - b], "eb ez0 ez1 ez2")
+    ts("mi0", T.mi[:, 0:1], T.pi[:, 0:1], 15, None, AND, None, "pi")
+    ts("mi1", T.mi[:, 1:2], T.pi[:, 0:1], 2, 3, SHR, AND, "pi")
+    ts("mi2", T.mi[:, 2:3], T.pi[:, 0:1], 3, 1, SHR, AND, "pi")
+    ts("mi3", T.mi[:, 3:4], T.pi[:, 1:2], 255, None, AND, None, "pi16")
+    cp("mf", T.mf[:], T.mi[:], "mi0 mi1 mi2 mi3")
+    for i, f in enumerate((ROW, 92, -100)):
+        lin("sc%d" % i, sc[:, i:i + 1], mq, float(f), m, "mf")
+    lin("sc3", sc[:, 3:4], mq, float(ROW), -16.0 * ROW, "mf")
+    ts("ul", T.ul[:], T.cr[:, 0:8], 16.0, None, MUL, None, "cr")
+    ts("rp4", T.rp4[:], T.cr[:, 0:6], 4.0, mq, MUL, ADD, "cr mf")
+    lin("sc4", sc[:, 4:5], hi, 1.0 - C, m16, "mf")
+    ts("xl0", T.xl[:, 0:S:3], T.xv[:, 0:8], m16, None, ADD, None, "xv mf")
+    ts("xl1", T.xl[:, 1:S:3], T.xv[:, 16:24], sc[:, 4:5], -2.0, ADD, ADD, "xv sc4")
+    ts("xl2", T.xl[:, 2:S:3], T.xv[:, 8:16], m16, None, ADD, None, "xv mf")
+    lin("j1", T.pj[:, 0:6], T.cr[:, 0:6], 16.0, m, "cr mf")
+    lin("kf0", T.kf[:, 6:8], T.pj[:, 6:8], 1.0 / S, -11.5 / S, "pp")
+    lin("kf1", T.kf[:, 0:6], T.pj[:, 0:6], 1.0 / 6, -2.5 / 6, "j1")
+    cp("ki0", T.ki[:, 6:8], T.kf[:, 6:8], "kf0")
+    cp("ki1", T.ki[:, 0:6], T.kf[:, 0:6], "kf1")
+    ts("ku", T.ku[:], T.ki[:, 0:6], -6.0, None, MUL, None, "ki1")
+    tt("kv", T.kv[:], T.ku[:], T.pj[:, 0:6], ADD, "ku j1")
+    cp("rth", T.rth[:], T.kv[:, 0:4], "kv")
+    cp("kq", T.kq[:, 0:1], T.ki[:, 6:7], "ki0")
+    ts("k24", T.kq[:, 1:2], T.ki[:, 6:7], float(S), None, MUL, None, "ki0")
+    op("far", {"S": lambda: ACT.activation(T.far[:], T.crp[:], AF.Abs, bias=T.kq[:, 1:2])}, "crp k24")
+    ts("room", T.room[:], T.cr[:, 0:8], T.kq[:, 0:1], None, SUB, None, "cr kq")
+    const("cz0", T.cm[:, 0:4 * NC:28], 0)
     for b in range(1, 4):
-        zero(T.cm[:, b:4 * NC:4], NC, ["cz%d" % b])
-    const(T.c1k[:], 1024, 16, ["c1k"])
-    for e in range(7):
-        ts(T.cm[:, 4 * e:4 * NC:28], T.far[:], T.room[:, e:e + 1], 2048.0, LT, MUL, S, ["far", "room"], ["cm%d" % e])
-    op({"G": (250, lambda: g.affine_select(T.cm[:, 249:4 * NC:28], T.c1k[:], [[-1, 16]], AluOpType.is_equal, 0.0, -112, 1))},
-       ["c1k", "cz1"], ["cz1"])
-    quant("cone", 0, NC, T.cm[:], ["cm%d" % e for e in range(7)] + ["cz1", "cz2", "cz3"], ["cone"])
-    zero(T.sg[:, 2:512:4], 128, ["sg2"])
-    zero(T.sg[:, 3:512:4], 128, ["sg3"])
-    for i in range(3):
-        lin(T.tau[:, i:i + 1], KQ[:, i:i + 1], -float(S), J[:, i:i + 1], 1, ["kq", "pj"], ["tau%d" % i])
-        ts(T.dec[:, S * i:S * i + S], T.cr[:], T.tau[:, i:i + 1], -48.0, LE, MUL, S, ["cr", "tau%d" % i], ["dec%d" % i])
-    lin(T.j25[:], J[:, 0:S], 25.0, 0.0, S, ["pj"], ["j25"])
-    lin(T.u3[:], KQ[:, 0:S], -576.0, -float(TOPK), S, ["kq"], ["u3"])
-    tt(T.cl[:, 0:24], T.u3[:], T.j25[:], ADD, S, ["u3", "j25"], ["cl0"])
-    lin(T.u4[:, 0:9], KQ[:, 0:9], -624.0, float(ZO - S - TOPK), 9, ["kq"], ["u4a"])
-    tt(T.cl[:, 24:33], T.u4[:, 0:9], T.j25[:, 0:9], ADD, 9, ["u4a", "j25"], ["cl1"])
-    lin(T.cl[:, 33:42], KQ[:, 0:9], -24.0, float(A), 9, ["kq"], ["cl2"])
-    lin(T.u4[:, 16:25], KQ[:, 0:9], -48.0, 120.0, 9, ["kq"], ["u4b"])
-    const(T.d1[:, 1:10:2], 0, 5, ["d1m"])
-    const(T.d0[:, 1:10:2], 4096, 5, ["d0m"])
-    tt(T.d1[:, 11:28:2], T.u4[:, 16:25], J[:, 0:9], ADD, 9, ["u4b", "pj"], ["d1o"])
-    const(T.d0[:, 0:28:2], -1, 14, ["d0e"])
-    const(T.n0[:, 0:48:2], -1, S, ["n0e"])
-    const(T.m48[:], -48, S, ["m48"])
-    lin(T.sc[:, 2:3], T.mf[:], 24.0, -float(TOPK), 1, ["mf"], ["sc2"])
-    lin(T.sc[:, 3:4], T.mf[:], -24.0, 360.0, 1, ["mf"], ["sc3"])
-    lin(T.sc[:, 4:5], T.mf[:], -768.0, 32.0 * C, 1, ["mf"], ["sc4"])
-    ts(T.sc[:, 5:6], T.mf[:], 24.0, T.sc[:, 3:4], MUL, MIN, 1, ["mf", "sc3"], ["sc5"])
-    lin(T.lc[:], T.cr[:], 25.0, T.sc[:, 2:3], S, ["cr", "sc2"], ["lc"])
-    lin(T.n1[:, 1:48:2], T.cr[:], 1.0, T.sc[:, 5:6], S, ["cr", "sc5"], ["n1o"])
-    for t in range(R):
-        buf, w = (T["rw%d" % t], RW) if AT_RECEIVER[t] else (T["win%d" % t], PW)
-        for b in range(4):
-            const(buf[:, b * w:b * w + ZO], 0, ZO, ["z%d_%d" % (t, b)])
-    CL = ["cl0", "cl1", "cl2"]
+        const("cz%d" % b, T.cm[:, b:4 * NC:4], 0)
+    const("cw", T.cw[:], int(BIG / 2))
+    for e in range(1, 7):
+        ts("cm%d" % e, T.cm[:, 4 * e:4 * NC:28], T.far[:], T.room[:, e:e + 1], BIG, LT, MUL, "far room")
+    op("cm0", {"G": lambda: g.affine_select(T.cm[:, 249:4 * NC:28], T.cw[:], [[-1, 16]], AluOpType.is_equal, 0.0, -112, 1)}, "cw cz1")
+    quant("qcone", "cone", 0, NC, T.cm[:], "cz0 cz2 cz3 " + " ".join("cm%d" % e for e in range(7)))
+    const("sz2", T.sg[:, 2:512:4], 0)
+    const("sz3", T.sg[:, 3:512:4], 0)
+    const("df", T.df[:], -2 * ROW)
+    ts("crm", T.crm[:], T.cr[:], mq, None, SUB, None, "cr mf")
+    for j in range(6):
+        ts("dec%d" % j, T.dec[:, S * j:S * j + S], T.crm[:], 4.0 * j, -2.0 * ROW, LE, MUL, "crm")
+    per = 16 + 4 * ROW
+    iota("cla", T.cl[:, 0:36], [[ROW, 6], [per, 6]], ZP - TOPV)
+    iota("clb", T.cl[:, 36:72], [[-ROW, 6], [per, 6]], ZP - ROW - TOPV)
+    iota("clc", T.cl[:, 72:96], [[ROW, 4], [per, 6]], ZP + 6 * ROW - TOPV)
+    lin("cl", T.cl[:], T.cl[:], 1.0, sc[:, 0:1], "cla clb clc sc0")
+    iota("g3", T.g3[:], [[-ROW, 6], [16, 6]], ZP + 5 * ROW)
+    lin("own1", T.b1[:, 1:72:2], T.g3[:], 1.0, m, "g3 mf")
+    iota("g4", T.g4[:], [[ROW + 4, S], [4 * ROW, 4]], -TOPV)
+    lin("cf", T.cf[:], T.g4[:], 1.0, sc[:, 1:2], "g4 sc1")
+    iota("g5", T.g5[:], [[0, S], [4 * ROW, 4]], 0)
+    lin("cg", T.cg[:], T.g5[:], 1.0, sc[:, 3:4], "g5 sc3")
+    iota("g6", T.g6[:], [[-4 * ROW, 2], [4, S]], 7 * ROW)
+    lin("own2", T.f1[:, 5:192:8], T.g6[:, 0:S], 1.0, sc[:, 2:3], "g6 sc2")
+    lin("own3", T.f1[:, 7:192:8], T.g6[:, S:48], 1.0, sc[:, 2:3], "g6 sc2")
+    const("fz1", T.f1[:, 1:192:8], 0)
+    const("fz3", T.f1[:, 3:192:8], 0)
+    const("bz", T.b0[:, 0:72:2], 0)
+    const("fz", T.f0[:, 0:192:2], 0)
+    for n in ("w0", "rw0", "w1", "rw2"):
+        const("z" + n, T[n][:, 0:ZP], 0)
 
-    quant("u", 0, 128, T.uin[:], ["uin"], ["u"])
-    pick("up", 0, "u", 128, T.ul[:], 128, ["u", "ul"], "up")
-    quant("v", 0, 128, T.vin[:], ["vin"], ["v"])
-    quant("x", 0, 192, T.xin[:, 0:768], ["xin0"], ["xa"])
-    quant("x", 192, C, T.xin[:, 768:1536], ["xin1"], ["xb"])
-    pick("t0", 0, "x", C, T.xl[:, 0:10], TP, ["xa", "xb", "xl"], "t0")
-    pick("t0", TP, "x", C, T.xl[:, 10:24], C - TP, ["xa", "xb", "xl"], "b0")
+    def cuts(t, top, reads):
+        n = str(t)
+        mm("p" + n, [(side(top, 0, 128), side("up", 0, 128))], 128, reads + " upq ups", fixed=6)
+        mm("pb" + n, [(side(top, 16, A), side("up", 0, 128))], 128, reads + " upq ups", fixed=7)
+        op("sa" + n, {"V": lambda: V.tensor_scalar(T.sg[:, 0:512:4], psum("p" + n, 0, 128), 0.0, 0.5, GT, SUB)}, "p" + n, "sga", frees="p" + n)
+        op("sb" + n, {"S": lambda: ACT.activation(T.sg[:, 1:512:4], psum("pb" + n, 0, 128), AF.Sign, bias=-1e-37)}, "pb" + n, "sgb", frees="pb" + n)
+        op("qs" + n, {"V": lambda: V.quantize_mx(T.qsign[:], T.ssign[:], T.sg[:])}, "sga sgb sz2 sz3", "sign")
+        mm("pc" + n, [(side("sign", 0, 128), side("cone", 0, NC))], NC, "sign qcone", fixed=6)
+        op("h" + n, {"V": lambda: V.tensor_tensor_scan(T.h[:], psum("pc" + n, 0, NC), T.cap[:], float(TOPV), MAX, MIN)}, "pc%d cap" % t, "h", frees="pc" + n)
+        lo, hi = (36, 72) if t == R - 1 else (0, 96)
+        tg = T["tg" + n]
+        for j in range(6):
+            scan("tg%d%d" % (t, j), tg[:, S * j:S * j + S], T.dec[:, S * j:S * j + S], T.h[:, 6:NC:7], 0.0, ADD, MAX, "h dec%d" % j)
+            ts("ls%d%d" % (t, j), T["ls" + n][:, lo + j:hi:6], T.cl[:, lo + j:hi:6], tg[:, S * j + S - 1:S * j + S], None, ADD, None, "cl tg%d%d" % (t, j))
+        return " ".join("ls%d%d" % (t, j) for j in range(6))
 
-    def unpack(nm, c0, n, a, dst, width, at, need, tags):
-        for p in range(4):
-            m = mm([(side("e", 128 * p, 128 * p + 128), side(nm, c0, c0 + n))], n, ["e%d" % p] + [x + y for x in "qs" for y in need], BULK)
-            o = p * width + at
-            evac(m, a, n, dst[:, o:o + n - a], 0.015625, ["%s_%d" % (x, p) for x in tags])
+    def bottom(t, ls):
+        n = str(t)
+        ts("e" + n, T.b1[:, 0:96:2], T["ls" + n][:, 0:48], 10.0 * ROW, None, ADD, None, ls, "e")
+        ts("th" + n, T.th[:], T["ml" + n][:, 0:8], 10.0 * ROW, None, ADD, None, "sl" + n, "th")
+        tt("f" + n, T.b0[:, 1:96:2], T.th[:].indirect(T.rth[:, 0:3]), T.b1[:, 0:96:2], GE, "th rth e", "f")
+        scan("bo" + n, T.bo[:], T.b0[:, 0:72], T.b1[:, 0:72], 0.0, MUL, MAX, "bz f e own1", "bo")
+        cp("lb" + n, T["ls" + n][:, 96:132], T.bo[:, 1:72:2], "bo")
 
-    for t in range(R):
-        win, lst, ml, bl, tg = (T[n + str(t)] for n in ("win", "lst", "ml", "bl", "tg"))
-        top, rr, kk = "t%d" % t, "r%d" % t, "k%d" % t
-        codes = lambda nm: [(T["q" + rr][:].bitcast(dt.uint8), T["q" + nm][:, 0:A].bitcast(dt.uint8)), (T["s" + rr][:], T["s" + nm][:, 0:A])]
-        big = FAR_BIG + (FIRST if t == 0 else 0)
-        if AT_RECEIVER[t]:
-            send(t, codes(top), "ac%d" % t, big, ["q" + top, "s" + top], ["q" + rr, "s" + rr])
-        p0 = mm([(side(top, 0, 128), side("up", 0, 128))], 128, ["q" + top, "s" + top, "qup", "sup"], CHAIN)
-        p1 = mm([(side(top, 16, A), side("up", 0, 128))], 128, ["q" + top, "s" + top, "qup", "sup"], CHAIN)
-        vop(128, lambda p0=p0: V.tensor_scalar(T.sg[:, 0:512:4], T.ps[:, bank(p0):bank(p0) + 128], 0.0, 0.5, GT, SUB),
-            ["mm%d" % p0], ["sg0"], frees=p0)
-        op({"S": (200, lambda p1=p1: ACT.activation(T.sg[:, 1:512:4], T.ps[:, bank(p1):bank(p1) + 128], AF.Sign, bias=-1e-37))},
-           ["mm%d" % p1], ["sg1"], frees=p1)
-        quant("sign", 0, 128, T.sg[:], ["sg0", "sg1", "sg2", "sg3"], ["sign"])
-        pc = mm([(side("sign", 0, 128), side("cone", 0, NC))], NC, ["sign", "cone"], CHAIN)
-        vop(NC, lambda pc=pc: V.tensor_tensor_scan(T.h[:], T.ps[:, bank(pc):bank(pc) + NC], T.cap[:], float(TOPK), MAX, MIN),
-            ["mm%d" % pc, "cap"], ["h"], frees=pc)
-        lo, hi = (24, 33) if t == R - 1 else (0, 42)
-        for i in range(3):
-            scan(tg[:, S * i:S * i + S], T.dec[:, S * i:S * i + S], T.h[:, 6:NC:7], 0.0, ADD, MAX, S, ["h", "dec%d" % i], ["tg%d_%d" % (t, i)])
-            ts(lst[:, lo + i:hi:3], T.cl[:, lo + i:hi:3], tg[:, S * i + S - 1:S * i + S], 0.0, ADD, MAX, 14, CL + ["tg%d_%d" % (t, i)], ["l%d_%d" % (t, i)])
-        L = ["l%d_%d" % (t, i) for i in range(3)]
-        first = 24 if AT_RECEIVER[t] else 33
-        if first < hi:
-            send(t, [(ml[:, first - 24:hi - 24], lst[:, first:hi])], "al%d" % t, FAR_SMALL, L, ["ml%d" % t])
-        ta, tm, tb, low = "Ta%d" % t, "Tm%d" % t, "Tb%d" % t, "b%d" % t
-        if SPLIT[t] == "C":
-            unpack(top, 0, C, 0, win, PW, ZO, [top, low], [ta, tm, tb])
-        else:
-            unpack(top, 0, TP, 0, win, PW, ZO, [top], [ta])
-        if SPLIT[t] == "B":
-            unpack(top, TP, C - TP, 0, win, PW, ZO + TP, [low], [tm, tb])
-        if SPLIT[t] == "A":
-            unpack("m", 0, 128, 128 - (MID - TP), win, PW, ZO + TP, ["m"], [tm])
-            unpack(top, MID, A, 0, win, PW, ZO + MID, [low], [tb])
-        Tn = lambda b: ["%s_%d" % (x, b) for x in (ta, tm, tb)]
-        bt = T["bt%d" % t]
-        if AT_RECEIVER[t]:
-            rw = T["rw%d" % t]
-            unpack(rr, 0, A, 0, rw, RW, ZO, [rr], ["Ra%d" % t])
-            for b in range(4):
-                gather(bt[:, b:4 * A:4], rw[:, b * RW:b * RW + RW], ml[:, 0:9], A, ["Ra%d_%d" % (t, b), "z%d_%d" % (t, b), "ml%d" % t], ["bt%d_%d" % (t, b)])
-            use = kk
-        else:
-            for b in range(4):
-                gather(bt[:, b:4 * A:4], win[:, b * PW:b * PW + RW], lst[:, 24:33], A, ["Ta%d_%d" % (t, b), "z%d_%d" % (t, b)] + L, ["bt%d_%d" % (t, b)])
-            use = rr
-        quant(kk, 0, A, bt[:], ["bt%d_%d" % (t, b) for b in range(4)], ["q" + kk, "s" + kk])
-        if not AT_RECEIVER[t]:
-            send(t, codes(kk), "ac%d" % t, big, ["q" + kk, "s" + kk], ["q" + rr, "s" + rr])
-        for b in range(4):
-            m = mm([(side("w", 128 * b, 128 * b + 128), side(use, 0, A)), (side("e", 128 * b, 128 * b + 128), side(use, 0, A))], A,
-                   ["qw", "sw", "e%d" % b, "q" + use, "s" + use], BULK)
-            evac(m, 0, A, win[:, b * PW + ZO + C:b * PW + PW], 0.015625, ["H%d_%d" % (t, b)])
-        xn = T["x%d" % (t + 1)]
-        if t < R - 1:
-            cp(T.d1[:, 0:28:2], lst[:, 10:24], 14, L, ["d1e"])
-            for i in range(3):
-                ts(T.d0[:, 11 + 2 * i:28:6], ml[:, 9 + i:18:3], tg[:, S * i + S - 1:S * i + S], 4096.0, GT, MUL, 3,
-                   ["ml%d" % t, "tg%d_%d" % (t, i)], ["d0o%d" % i])
-            scan(T.so[:], T.d0[:], T.d1[:], 0.0, MIN, MAX, 28, ["d0m", "d1m", "d0e", "d0o0", "d0o1", "d0o2", "d1e", "d1o"], ["so"])
-            apart = SPLIT[t + 1] == "A"
-            if apart:
-                cp(bl[:, 0:9], T.so[:, 11:28:2], 9, ["so"], ["bl%d" % t])
-            else:
-                cp(bl[:, 0:14], T.so[:, 1:28:2], 14, ["so"], ["bl%d" % t])
-            c0, c1 = MID if apart else TP, EARLY[t]
-            for b in range(4):
-                w = win[:, b * PW + ZO:b * PW + ZO + C]
-                if c1:
-                    gather(xn[:, b:4 * c1:4], win[:, b * PW + ZO:b * PW + ZO + MID], lst[:, 0:c1 // 16], c1, Tn(b)[:2] + L, ["xe%d_%d" % (t, b)])
-                gather(xn[:, 4 * c1 + b:4 * TP:4], w, lst[:, c1 // 16:10], TP - c1, Tn(b) + L, ["xt%d_%d" % (t, b)])
-                if apart:
-                    gather(xn[:, 4 * TP + b:4 * MID:4], w, lst[:, 10:15], MID - TP, Tn(b) + L, ["xm%d_%d" % (t, b)])
-                gather(xn[:, 4 * c0 + b:4 * C:4], win[:, b * PW + ZO:b * PW + PW], bl[:, 0:(C - c0) // 16], C - c0,
-                       Tn(b) + ["H%d_%d" % (t, b), "bl%d" % t], ["xb%d_%d" % (t, b)])
-            four = lambda s: ["%s%d_%d" % (s, t, b) for b in range(4)]
-            nt = "t%d" % (t + 1)
-            quant(nt, 0, TP, xn[:, 0:4 * TP], four("xt") + (four("xe") if c1 else []), ["q" + nt, "s" + nt])
-            if apart:
-                quant("m", 0, 128, xn[:, 4 * (MID - 128):4 * MID], four("xt") + four("xm"), ["qm", "sm"])
-            quant(nt, c0, C, xn[:, 4 * c0:4 * C], four("xb"), ["qb%d" % (t + 1), "sb%d" % (t + 1)])
-        else:
-            scan(T.fw[:], T.m48[:], T.h[:, 6:NC:7], 0.0, ADD, MAX, S, ["h", "m48"], ["fw"])
-            scan(T.gn[:, ::-1], T.fw[:, ::-1], T.fw[:, ::-1], 0.0, MAX, MAX, S, ["fw"], ["gn"])
-            lin(T.yn[:], T.gn[:], 32.0, T.sc[:, 4:5], S, ["gn", "sc4"], ["yn"])
-            send(t, [(T.mn[:], T.yn[:])], "an", FAR_SMALL, ["yn"] + L, ["mn"])
-            lin(T.g32[:], T.gn[:], 32.0, 0.0, S, ["gn"], ["g32"])
-            tt(T.n1[:, 0:48:2], T.gn[:], T.lc[:], ADD, S, ["gn", "lc"], ["n1e"])
-            tt(T.o1[:], T.gn[:], T.cap[:, 0:NC:7], SUB, S, ["gn", "cap"], ["oa1"])
-            lin(T.o2[:], T.o1[:], 1.0 / S, 0.0, S, ["oa1"], ["oa2"])
-            dma("Y", T.oa[:], T.o2[0:128:16, :], "st", STORE, ["oa2"], ["oa"])
-            tt(T.n0[:, 1:48:2], T.mn[:], T.g32[:], SUB, S, ["mn", "g32"], ["n0o"])
-            scan(T.no[:], T.n0[:], T.n1[:], 0.0, MIN, MAX, 48, ["n0e", "n0o", "n1e", "n1o"], ["no"])
-            cp(bl[:], T.no[:, 1:48:2], S, ["no"], ["bl%d" % t])
-            for hh, (a, z) in enumerate(LAST):
-                for b in range(4):
-                    gather(xn[:, 4 * a + b:4 * z:4], win[:, b * PW + ZO:b * PW + PW], bl[:, a // Z:z // Z], z - a,
-                           Tn(b) + ["H%d_%d" % (t, b), "bl%d" % t], ["xf%d_%d" % (hh, b)])
-                quant("fin", a, z, xn[:, 4 * a:4 * z], ["xf%d_%d" % (hh, b) for b in range(4)], ["o%d" % hh])
-                dma("Y", T.oc[:, 4 * a:4 * z], T.qfin[:, a:z].bitcast(dt.uint8), "st", STORE, ["o%d" % hh], ["oc%d" % hh])
-                m = mm([(side("v", 0, 128), side("fin", a, z))], z - a, ["v", "o%d" % hh], BULK)
-                evac(m, 0, z - a, T.ysb[:, a:z], 1.0, ["ysb%d" % hh])
-                dma("YS", T.y[:, a:z], T.ysb[:, a:z], "st", STORE, ["ysb%d" % hh], ["y%d" % hh])
-            for k in range(4):
-                dma("YS", T.osc[4 * k:4 * k + 4, :], T.sfin[32 * k:32 * k + 4, :], "st", STORE, ["o0", "o1"], ["osc%d" % k])
+    quant("qu", "u", 0, 128, T.uin[:], "lu")
+    pick("up", "up", 0, 128, "u", 128, T.ul[:], "qu ul")
+    quant("qv", "v", 0, 128, T.vin[:], "lv")
+    quant("qx0", "x", 0, 192, T.xin[:, X0:X0 + 768], "lx0")
+    quant("qx1", "x", 192, C, T.xin[:, X0 + 768:X0 + 1536], "lx1")
+    top0 = pick("ta", "t0", 0, 160, "x", C, T.xl[:, 0:10], "qx0 qx1 xl0 xl1 xl2")
+    low0 = pick("tb", "t0", 160, C, "x", C, T.xl[:, 10:S], "qx0 qx1 xl0 xl1 xl2")
+
+    send("sc0s", 0, codes("r0", "t0"), "ac0", top0)
+    t0 = product("T", "e", "t0", C, 0, C, T.w0, ZP, top0 + " " + low0)
+    ls0 = cuts(0, "t0", top0)
+    t0 += " zw0 " + ls0
+    send("sl0", 0, [(T.ml0[:], T.ls0[:, 30:72])], "al0", ls0)
+    held = T.w0[:, 0:ZP + 4 * C]
+    ra = "sl0 zrw0 " + product("Ra", "e", "r0", A, 0, A, T.rw0, ZP, "sc0s")
+    x1t = gather("xa", T.x1, 0, held, T.ls0, 0, (0, 18, 36), t0)
+    quant("qt1", "t1", 0, A, T.x1[:, 0:4 * A], x1t)
+    x1m = gather("xb", T.x1, A, held, T.ls0, 72, (0, 24), t0)
+    quant("qm1", "m1", 0, MID, T.x1[:, 0:4 * MID], x1t + " " + x1m)
+    t1a = "zw1 " + product("U", "e", "m1", MID, 0, MID, T.w1, ZP, "qm1")
+    bottom(0, ls0)
+    if SPLIT:
+        be = gather("be", T.xin, 0, T.rw0[:], T.ml0, 6, (0, 6, 12), ra)
+        quant("qke", "ke", 0, 128, T.xin[:, 0:512], be + " lx0")
+        he = product("He", "we", "ke", 128, 0, E2, T.w0, ZP + 4 * C, "qke")
+        xc = gather("xc", T.x1, MID, T.w0[:, 0:ZP + 4 * (C + E2)], T.ls0, 96, (0, 6, 12), "lb0 %s %s" % (t0, he))
+        quant("qn1", "n1", 0, 128, T.x1[:, 4 * (MID + E2 - 128):4 * (MID + E2)], xc + " " + x1m)
+        t1b = product("V", "e", "n1", 128, 128 - E2, 128, T.w1, ZP + 4 * MID, "qn1")
+        b0 = gather("ba", T.bt0, 0, T.rw0[:], T.ml0, 10, (0, 16, 32), ra)
+        quant("qk0", "k0", 0, 128, T.bt0[:, 0:512], b0)
+        h0 = product("H", "we", "k0", 128, 32, 128, T.w0, ZP + 4 * (C + E2), "qk0")
+        xh = gather("xh", T.x1, MID + E2, T.w0[:], T.ls0, 108, (0, 12, 24), "lb0 %s %s %s" % (t0, he, h0))
+        quant("qo1", "o1", 0, 128, T.x1[:, 4 * (C - 128):4 * C], xh + " " + xc)
+        t1c = product("W", "e", "o1", 128, 32, 128, T.w1, ZP + 4 * (MID + E2), "qo1")
+        reach = MID + E2
+    else:
+        b0 = gather("ba", T.bt0, 0, T.rw0[:], T.ml0, 6, (0, 18, 36), ra)
+        quant("qk0", "k0", 0, A, T.bt0[:], b0)
+        h0 = product("H", "we", "k0", A, 0, A, T.w0, ZP + 4 * C, "qk0")
+        xc = gather("xc", T.x1, MID, T.w0[:], T.ls0, 96, (0, 18, 36), "lb0 %s %s" % (t0, h0))
+        quant("qn1", "n1", 0, A, T.x1[:, 4 * MID:4 * C], xc)
+        t1b = product("W", "e", "n1", A, 0, A, T.w1, ZP + 4 * MID, "qn1")
+        t1c, reach = "", C
+
+    upper = T.w1[:, 0:ZP + 4 * MID]
+    ls1 = cuts(1, "t1", "qt1")
+    t1a += " " + ls1
+    send("sl1", 1, [(T.ml1[:], T.ls1[:, 30:38])], "al1", ls1)
+    b1 = gather("bb", T.bt1, 0, upper, T.ls1, 36, (0, 18, 36), t1a)
+    quant("qk1", "k1", 0, A, T.bt1[:], b1)
+    send("sc1s", 1, codes("r1", "k1"), "ac1", "qk1")
+    h1 = product("I", "we", "r1", A, 0, A, T.w1, ZP + 4 * C, "sc1s")
+    x2e = gather("xd", T.x2, 0, upper, T.ls1, 0, (0, 24), t1a)
+    x2l = gather("xe", T.x2, ROW, T.w1[:, 0:ZP + 4 * reach], T.ls1, 24, (0, 6, 12), t1a + " " + t1b)
+    quant("qt2", "t2", 0, A, T.x2[:, 0:4 * A], x2e + " " + x2l)
+    bottom(1, ls1)
+    x2r = gather("xf", T.x2, A, T.w1[:], T.ls1, 72, (0, 30, 60), "lb1 %s %s %s %s" % (t1a, t1b, t1c, h1))
+    quant("qn2", "t2", A, C, T.x2[:, 4 * A:4 * C], x2r)
+
+    send("sc2s", 2, codes("r2", "t2"), "ac2", "qt2")
+    ls2 = cuts(2, "t2", "qt2")
+    send("sl2", 2, [(T.ml2[:], T.ls2[:, 36:72])], "al2", ls2)
+    scan("fw", T.fw[:], T.df[:], T.h[:, 6:NC:7], 0.0, ADD, MAX, "h df")
+    scan("v24", T.v24[:, ::-1], T.fw[:, ::-1], T.fw[:, ::-1], 0.0, MAX, MAX, "fw")
+    send("sn", 2, [(T.mn[:], T.v24[:])], "an", "v24 sl2s" if False else "v24")
+    t2 = product("X", "e", "t2", C, 0, C, T.w2, 0, "qt2 qn2")
+    rc = product("Rc", "e", "r2", A, 0, A, T.rw2, ZP, "sc2s")
+    b2 = gather("bc", T.bt2, 0, T.rw2[:], T.ml2, 0, (0, 18, 36), "sl2 zrw2 " + rc)
+    quant("qk2", "k2", 0, A, T.bt2[:], b2)
+    h2 = product("J", "we", "k2", A, 0, A, T.w2, 4 * C, "qk2")
+    tt("o1", T.o1[:], T.v24[:], T.cap[:, 0:NC:7], SUB, "v24 cap")
+    lin("o2", T.o2[:], T.o1[:], 1.0 / ROW, 0.0, "o1")
+    dma("oa", T.oa[:], T.o2[0:128:16, :], "st", "o2")
+    tt("e2", T.f1[:, 0:192:2], T.v24[:].indirect(T.rp4[:]), T.cf[:], ADD, "v24 rp4 cf")
+    tt("dd", T.dd[:], T.mn[:], T.v24[:], SUB, "sn v24")
+    tt("f2", T.f0[:, 1:192:2], T.dd[:].indirect(T.rp4[:]), T.cg[:], GT, "dd rp4 cg")
+    scan("fo", T.fo[:], T.f0[:], T.f1[:], 0.0, MUL, MAX, "fz f2 e2 own2 own3 fz1 fz3")
+    cp("lf", T.lf[:], T.fo[:, 1:192:2], "fo")
+    for p, (a, z) in enumerate(LAST):
+        n = str(p)
+        xg = gather("xg" + n, T.x3, a, T.w2[:], T.lf, a // 4, (0, (z - a) // 8, (z - a) // 4), "lf %s %s" % (t2, h2))
+        quant("qf" + n, "fin", a, z, T.x3[:, 4 * a:4 * z], xg)
+        dma("oc" + n, T.oc[:, 4 * a:4 * z], T.qfin[:, a:z].bitcast(dt.uint8), "st", "qf" + n)
+        mm("my" + n, [(side("v", 0, 128), side("fin", a, z))], z - a, "qv qf" + n)
+        evac("ys" + n, "my" + n, 0, z - a, T.ysb[:, a:z], 1.0)
+        dma("y" + n, T.y[:, a:z], T.ysb[:, a:z], "st", "ys" + n)
+    for k in range(4):
+        dma("os%d" % k, T.osc[4 * k:4 * k + 4, :], T.sfin[32 * k:32 * k + 4, :], "st", " ".join("qf%d" % p for p in range(len(LAST))))
+
     writer, readers = {}, {}
-    for i, o in enumerate(ops):
-        d = set(writer[r] for r in o["reads"])
+    for n, o in ops.items():
+        o["deps"] = set(writer[r] for r in o["reads"])
         for w in o["writes"]:
-            if w in writer:
-                d.add(writer[w])
-            d.update(readers.get(w, []))
-        d.discard(i)
-        o["deps"] = d
+            o["deps"].update(readers.pop(w, []))
+            writer[w] = n
         for r in o["reads"]:
-            readers.setdefault(r, []).append(i)
-        for w in o["writes"]:
-            writer[w] = i
-            readers[w] = []
-    late = [i for i, o in enumerate(ops) if "qr0" in o["reads"] and "banks" in o]
-    for i in late:
-        ops[i]["soft"] = [k for k, o in enumerate(ops) if "qt1" in o["reads"] and "qup" in o["reads"]]
-    return ops
-
-
-def place(rows, links, seq, back):
-    busy = dict(V=[], S=[], T=[], G=[], Y=[])
-    start, done, where, held = {}, {}, {}, {BULK: [], CHAIN: []}
-
-    def gap(e, t, d):
-        for s, f in busy[e]:
-            if s >= t + d:
-                break
-            if f > t:
-                t = f
-        return t
-
-    def best(i, t0):
-        c = None
-        for e, d in rows[i][5].items():
-            t = t0
-            for k in links[i]:
-                lat = rows[i][1] if back else rows[k][1]
-                t = max(t, done[k] + lat + (HOP if where[k] != e or lat else SAME))
-            t = gap(e, t, d)
-            if c is None or t + d < c[0]:
-                c = (t + d, t, e)
-        return c
-
-    def put(i, c):
-        done[i], start[i], where[i] = c
-        busy[c[2]].append((c[1], c[0]))
-        busy[c[2]].sort()
-
-    for i in seq:
-        if i in done:
-            continue
-        c = best(i, rows[i][1] if back else 0)
-        pool = rows[i][2]
-        if pool and not back:
-            k = rows[i][6]
-            while True:
-                done[i], where[i] = c[0], c[2]
-                r = best(k, 0)
-                over = sorted(f for s, f in held[pool] if s < r[0] + HOP and f + HOP > c[1])
-                if len(over) < len(pool):
-                    break
-                c = best(i, over[0] + HOP + 1)
-            put(i, c)
-            put(k, r)
-            held[pool].append((c[1], r[0]))
-        else:
-            put(i, c)
-    return start, done, where
-
-
-def replay(rows, order, where):
-    banks, extra, holder, total, first, tight = {}, {}, {}, 0, None, []
-    for fc, fg, ft, fl, hop in CASES:
-        free = dict(V=0, S=0, T=0, G=0, Y=0)
-        done, start, why, last = [0] * len(rows), [0] * len(rows), [None] * len(rows), {}
-        for i in order:
-            deps, lat, pool, frees, picks, alts, _ = rows[i]
-            e = where[i]
-            t = free[e]
-            why[i] = last.get(e)
-            last[e] = i
-            for d in deps:
-                u = done[d] + (hop if where[d] != e or rows[d][1] else hop / 2)
-                if u > t:
-                    t, why[i] = u, d
-            if pool:
-                if first is None:
-                    ok = [(done[holder[x]] if x in holder else 0, x) for x in pool if holder.get(x, 0) is not None]
-                    if not ok:
-                        return None
-                    b = min(ok)[1]
-                    if b in holder:
-                        extra[i] = holder[b]
-                    holder[b], banks[i] = None, b
-                if i in extra and done[extra[i]] + hop > t:
-                    t, why[i] = done[extra[i]] + hop, extra[i]
-            elif frees is not None and first is None:
-                holder[banks[frees]] = i
-            start[i] = t
-            t += alts[e] * (ft if e == "T" else fg if picks else fc)
-            free[e], done[i] = t, t + fl * lat
-        if first is None:
-            first = (max(done), start)
-        i = done.index(max(done))
-        while why[i] is not None:
-            if why[i] not in rows[i][0]:
-                tight.append((why[i], i))
-            i = why[i]
-        total += max(done) + PULL * sum(done) / len(done)
-    return total / len(CASES), first[0], banks, extra, first[1], tight
-
-
-def plan(ops):
-    if _PLAN:
-        return _PLAN["best"]
-    n, seed = len(ops), [SEED]
-
-    def rnd():
-        seed[0] = (seed[0] * 1103515245 + 12345) % 2147483648
-        return seed[0] / 2147483648
-    users = [[] for _ in ops]
-    for i, o in enumerate(ops):
-        for d in o["deps"] | set(o.get("soft", [])):
-            users[d].append(i)
-    rows = [[sorted(o["deps"] | set(o.get("soft", []))), o.get("lat", 0), o.get("banks"), o.get("frees"), "kind" in o,
-             {e: a[0] for e, a in o["alts"].items()}, ([k for k in users[i] if ops[k].get("frees") == i] + [None])[0]] for i, o in enumerate(ops)]
-    deps = [r[0] for r in rows]
-
-    def ranked(key, links, outs):
-        left = [len(x) for x in links]
-        ready, seq = [i for i in range(n) if not left[i]], []
-        while ready:
-            i = min(ready, key=lambda k: key[k])
-            ready.remove(i)
-            seq.append(i)
-            for k in outs[i]:
-                left[k] -= 1
-                if not left[k]:
-                    ready.append(k)
-        return seq
-    dep2 = [sorted(set(r[0]) | (set(rows[r[6]][0]) - {i} if r[2] else set())) for i, r in enumerate(rows)]
-    use2 = [[k for k in range(n) if i in dep2[k]] for i in range(n)]
-    now, key = None, list(range(n))
-    for step in range(PASSES):
-        _, done, _ = place(rows, users, ranked([-x for x in key], users, deps), True)
-        start, done, w = place(rows, deps, ranked([-done[i] + NOISE * rnd() for i in range(n)], dep2, use2), False)
-        o2, w2 = sorted(range(n), key=lambda k: (start[k], k)), [w[i] for i in range(n)]
-        c = replay(rows, o2, w2)
-        if c is not None and (now is None or c[0] < now[0]):
-            now, order, where, keep = c, o2, w2, done
-        key = [(keep if now and step % 3 == 2 else done)[i] + rows[i][1] + NOISE * rnd() for i in range(n)]
-    best = (now, order, where)
-    for step in range(TRIES):
-        o2, w2 = order, where
-        i, aim = int(rnd() * n), None
-        if now[5] and rnd() < 0.6:
-            i, aim = now[5][int(rnd() * len(now[5]))]
-            if rnd() < 0.5:
-                i, aim = aim, i
-        if len(rows[i][5]) > 1 and rnd() < 0.3:
-            w2 = list(where)
-            w2[i] = [e for e in sorted(rows[i][5]) if e != where[i]][0]
-        if w2 is where or rnd() < 0.5:
-            o2 = list(order)
-            at = o2.index(i)
-            del o2[at]
-            lo = max([o2.index(d) + 1 for d in rows[i][0]] + [0])
-            hi = min([o2.index(d) for d in users[i]] + [n - 1])
-            to = at + int((rnd() - 0.5) * 2 * 60 * rnd() ** 2)
-            if aim is not None:
-                to = o2.index(aim)
-                to = to + 1 + int(20 * rnd() ** 3) if to >= at else to - int(20 * rnd() ** 3)
-            o2.insert(min(hi, max(lo, to)), i)
-        c = replay(rows, o2, w2)
-        if c is not None and c[0] <= now[0] - HEAT * (1.0 - step / TRIES) ** 2 * math.log(rnd() + 1e-9):
-            now, order, where = c, o2, w2
-            if c[0] < best[0][0]:
-                best = (c, o2, w2)
-    _PLAN["best"] = (best[0][1], best[1], best[2]) + best[0][2:5]
-    _PLAN["cost"] = best[0][0]
-    return _PLAN["best"]
+            readers.setdefault(r, []).append(n)
+    return ops, bank
 
 
 def rank_program(g, core, T, topo):
     if T.rank_of(core) is None:
         return
-    ops = build(g, core, T, topo)
-    _, order, where, banks, extra, _ = plan(ops)
-    for i, b in banks.items():
-        ops[i]["bank"] = b
-    for i, d in extra.items():
-        ops[i]["deps"].add(d)
-    queue = dict(V=g.vector, S=g.scalar, T=g.tensor, G=g, Y=g.sync)
-    count, mark, seen = {}, {}, {}
-    for i in order:
-        o, e = ops[i], where[i]
-        need = {}
-        for d in o["deps"]:
-            s, v = mark[d]
-            need[s] = max(need.get(s, 0), v)
-        for s, v in sorted(need.items()):
-            if seen.get((e, s), 0) < v:
-                queue[e].wait_ge(T.sem[s], v)
-                seen[(e, s)] = v
-        ins = o["alts"][e][1]()
-        if "rsem" in o:
-            s = o["rsem"]
-            count[s] = count.get(s, 0) + o["got"]
-            count["sent"] = count.get("sent", 0) + o["gone"]
-        else:
-            s, inc = (o["dsem"], 16) if "dsem" in o else ("c" + e, 1)
-            ins.then_inc(T.sem[s], inc)
+    ops, bank = steps(g, core, T, topo)
+    order = {e: names.split() for e, names in ORDER.items()}
+    reader = {o["frees"]: n for n, o in ops.items() if "frees" in o}
+    last, turn = {}, 0
+    for n in order["T"]:
+        b = ops[n]["fixed"]
+        if b is None:
+            b, turn = turn % BULK, turn + 1
+        if b in last:
+            ops[n]["deps"].add(reader[last[b]])
+        last[b], bank[n] = n, b
+    count, mark = {}, {}
+    for e, names in order.items():
+        for n in names:
+            o = ops[n]
+            s, inc = (o["rsem"], o["inc"]) if "rsem" in o else (o["dsem"], 16) if "dsem" in o else ("c" + e, 1)
             count[s] = count.get(s, 0) + inc
-        mark[i] = (s, count[s])
+            mark[n] = (s, count[s])
+            if "rsem" in o:
+                count["sent"] = count.get("sent", 0) + inc
+    queue = dict(V=g.vector, S=g.scalar, T=g.tensor, G=g, Y=g.sync)
+    seen = {}
+    for e, names in order.items():
+        for n in names:
+            o, need = ops[n], {}
+            for d in o["deps"]:
+                s, v = mark[d]
+                need[s] = max(need.get(s, 0), v)
+            for s, v in sorted(need.items()):
+                if seen.get((e, s), 0) < v:
+                    queue[e].wait_ge(T.sem[s], v)
+                    seen[(e, s)] = v
+            ins = o["alts"][e]()
+            if "rsem" not in o:
+                ins.then_inc(T.sem[mark[n][0]], 16 if "dsem" in o else 1)
     for s, v in sorted(count.items()):
         if max([w for (e, s2), w in seen.items() if s2 == s] + [0]) < v:
             g.sync.wait_ge(T.sem[s], v)

@@ -1,44 +1,63 @@
 from concourse.mybir import dt, AluOpType, ActivationFunctionType
 
 S, C, A, R = 24, 384, 144, 3
-ROW = 4 * S
-ZP = ROW
+ROW = 2 * S
 MID = 10 * S
 E2 = 2 * S
 NC = 7 * S
-TOPV = ROW * (S - 1)
+PAD = 35
+K = 16 * ROW
+OFF = K + 5 * (ROW - 2)
 BIG = 8192.0
 X4 = "float8_e4m3fn_x4"
-SPLIT = True
 LAST = ((0, 128), (128, 256), (256, C))
+X0 = 4 * A
+XCUT = (0, 256, C)
+T0CUT = 12 * S
+B2_AT_SENDER = False
+B1_AT_SENDER = False
+XSPLIT = True
+NATIVE = False
+SBV = False
+WIDE = True
+SPLITSEND = True
+OCS = ((0,), (1,), (2,))
+YS = ((0,), (1,), (2,))
 
 SCRATCH = {"ps": ("psum", [128, 4096], "float32")}
 for _d, _bufs in (
-        ("bfloat16", dict(xin=4 * (E2 + C), uin=512, vin=512, eb=516, c64=NC, cw=16, cm=4 * NC, sg=512, x1=4 * C, x2=4 * C, x3=4 * C,
-                          w0=ZP + 4 * (C + A), w1=ZP + 4 * (C + A), w2=4 * (C + A), rw0=ZP + 4 * A, rw2=ZP + 4 * A,
-                          bt0=4 * A, bt1=4 * A, bt2=4 * A)),
-        ("float32", dict(cr=S, crp=S, crm=S, xv=S, far=S, room=8, pj=8, kf=8, kq=2, ku=6, kv=6, mf=4, sc=8, cap=NC, h=NC, fw=S, v24=S, dec=6 * S,
-                         df=S, cl=96, tg0=6 * S, tg1=6 * S, tg2=6 * S, th=8, mn=S, dd=S, o1=S, o2=S,
-                         g3=36, g4=96, g5=96, g6=48, cf=96, cg=96, b0=96, b1=96, bo=72, f0=192, f1=192, fo=192, ysb=C)),
-        ("int32", dict(pi=2, mi=4, ki=8)),
-        ("uint16", dict(ul=8, xl=S, rth=4, rp4=6, ls0=132, ls1=132, ls2=72, lf=96, ml0=42, ml1=8, ml2=36))):
+        ("bfloat16", dict(xin=X0 + 4 * C, uin=512, vin=512, zz=NC, eb=516, cm=4 * NC, cn=4 * NC, sg=512, x1=4 * C, x2=4 * C, x3=4 * C, bt1=4 * A, bt2=4 * A,
+                          w00=2 * (C + A), w01=2 * (C + A), w10=ROW + 2 * (C + A), w11=ROW + 2 * (C + A),
+                          w20=ROW + 2 * (C + A), w21=ROW + 2 * (C + A),
+                          r00=ROW + 2 * A, r01=ROW + 2 * A, r10=ROW + 2 * A, r11=ROW + 2 * A, r20=ROW + 2 * A, r21=ROW + 2 * A)),
+        ("float32", dict(cr=S, room=7, r7=7, mf=2, sc=8, far=S, ins=NC, f0i=40, far0=40, r0e=7, in0=280, cap=NC, h=NC + 2 * PAD, dec0=18, dec=18, cl=22, tg0=54, tg1=54, tg2=54,
+                         th=18, g3=18, b0=48, b1=36, bo=48, f1=48, df=2 * S, fw=S, v24=S, mn=S, o1=S, o2=S, ysb=C)),
+        ("int32", dict(pi=1, mi=2, ki=1)),
+        ("uint16", dict(ul=8, xl=S, ls0=84, ls1=84, ls2=66, lf=48, ml0=36, ml1=36, ml2=18))):
     for _n, _w in _bufs.items():
         SCRATCH[_n] = ("sbuf", [128, _w], _d)
-for _n, _w in dict(x=C, u=128, up=128, v=128, w=512, e=512, cone=NC, sign=128, t0=C, t1=A, m1=MID, n1=A, o1=128, t2=C, fin=C,
-                   r0=A, r1=A, r2=A, ke=128, k0=A, k1=A, k2=A).items():
+for _n, _w in dict(x=C, u=128, up=128, v=128, w=512, e=512, cone=NC, cn=NC, sign=128, t0=C, t1=A + 128, n1=128, o1=128, t2=C, fin=C,
+                   r0=A, r1=A, r2=A, ke=128, k0=128, k1=A, k2=A).items():
     SCRATCH["q" + _n] = ("sbuf", [128, _w], X4)
     SCRATCH["s" + _n] = ("sbuf", [128, _w], "uint8")
 
-SEMAPHORES = ["cV", "cS", "cT", "cG", "sent", "lx0", "lx1", "lu", "lv", "lwc", "lws", "st",
+SEMAPHORES = ["cV", "cS", "cT", "cG", "sent", "lx0", "lx1", "lx2", "lu", "lv", "lwc", "lws", "st",
               "ac0", "ac1", "ac2", "al0", "al1", "al2", "an"]
 
 ADD, SUB, MUL, MAX, MIN = AluOpType.add, AluOpType.subtract, AluOpType.mult, AluOpType.max, AluOpType.min
-GT, GE, LT, LE = AluOpType.is_gt, AluOpType.is_ge, AluOpType.is_lt, AluOpType.is_le
-AND, SHR = AluOpType.bitwise_and, AluOpType.logical_shift_right
+GT, GE, LT, NE = AluOpType.is_gt, AluOpType.is_ge, AluOpType.is_lt, AluOpType.not_equal
+AND = AluOpType.bitwise_and
 AF = ActivationFunctionType
 BULK = 6
 
-ORDER = {'Y': 'lu lx0 lx1 lws lwc lv oc2 oc1 os3 os2 y2 os0 y0', 'G': 'pi pp pi16 cr xv eb crp cw cz0 cm0 sz3 cap cla clb clc sc0s zw0 g3 bz g5 g6 g4 sl0 fz df sl1 sc1s sc2s sl2 sn', 'T': 'pb0 p0 mT2 mT3 pc0 mT0 mT1 mRa3 mRa2 mRa1 mRa0 pb1 p1 mU2 mU0 pc1 mHe2 mHe3 mHe1 mHe0 mU1 mU3 mH2 mH1 mH3 mH0 mV1 mV2 mV3 mV0 pb2 p2 mW3 mW2 mW1 mW0 pc2 mI2 mI1 mI0 mI3 mRc0 mRc3 mRc1 mRc2 mX2 mX1 mX0 mX3 mJ2 mJ3 mJ1 mJ0 my2 my1 my0', 'V': 'c64 fz1 mi0 ez1 mi2 mi1 mi3 ki0 mf ul kq k24 xl2 crm xl0 room qu xl1 qe2 upq cm2 qx0 qx1 cm3 cm1 cm4 taq cm6 tbq cm5 qe3 sa0 qcone qs0 qe0 dec2 dec4 dec5 qe1 dec1 h0 dec0 dec3 ki1 tg02 tg00 tg05 tg03 tg04 tg01 ls00 ls05 ls03 ls02 ls01 ls04 ku xa0 kv e0 cg qt1 Ra3 Ra1 qm1 sa1 be0 th0 qs1 qke rth U2 f0 h1 cf bo0 tg12 tg13 tg10 tg15 lb0 qk0 tg11 ls12 ls15 ls13 tg14 ls10 U1 ls14 ls11 qn1 H2 bb1 V1 V2 V3 V0 qk1 xe0 H3 own2 qt2 xh0 e1 qo1 sa2 th1 rp4 qs2 f1 W2 W1 bo1 h2 lb1 tg22 tg20 tg24 tg25 tg21 ls22 tg23 ls24 ls20 ls25 ls21 ls23 fw v24 xf1 Rc3 qn2 e2 o1 bc0 o2 dd qk2 f2 fo X3 lf J0 qv xg20 xg10 qf2 xg00 qf1 qf0 ys2 ys1 ys0', 'S': 'ez0 kf0 fz3 ez2 cz1 sc4 sc3 sc0 cz3 sc2 far sz2 j1 ups zrw2 cz2 tas tbs zw1 sb0 kf1 cl T2 T3 T0 T1 zrw0 xa1 xb0 Ra2 Ra0 sb1 be1 sc1 own1 ba1 U0 ba0 He2 He3 He1 He0 xc0 xc1 U3 H1 bb0 xd0 xe1 H0 xh1 own3 sb2 W3 W0 I2 I1 I0 I3 xf0 Rc0 Rc2 Rc1 bc1 X2 X1 X0 J2 J3 J1 xg21 xg11 xg01 oa oc0 os1 y1'}
+ORDER = {'Y': 'lx1 lx0 lwc lws lv oc1 oc0 os1 y2', 'G': 'pi room cr ez2 cmb cz3 cz2 eb cap sc0s zx1 zx2 sl0 bz g3 sc1s zr10 sl1 sc2s sl2 zr21 sn zr20', 'T': 'pb0 p0 mT1 mT3 mTl1 pc0 mT0 mT2 mTl0 mTl2 mTl3 mRa1 mRa3 mRa0 mRa2 pb1 p1 mHe0 mHe2 mHe1 mHe3 mU0 mU3 pc1 mU2 mH1 mH0 mU1 mV0 mV1 mV2 mV3 mH2 mRb2 mH3 mRb3 mRb0 mRb1 pb2 p2 mW2 pc2 mW0 mW1 mW3 mI1 mI3 mI2 mRc3 mRc0 mRc2 mRc1 mI0 mX3 mX1 mX0 mX2 mJ1 mJ0 mJ3 mZ3 mZ1 mJ2 mZ2 mZ0 my1 my2 my0', 'V': 'zz mi1 mi0 ez1 ki mf df1 negc lo383 dec0 sz2 ul xl0 xl1 xl2 qx1 qu qx0 qx2 upq taq tbq qe1 qe3 sa0 qcone qs0 qe0 qe2 zr11 zr00 h0 Tl1 tg01 tg02 tg00 ls01 ls02 ls00 Tl0 Tl3 xa1 Ra1 df0 e0 Ra2 qt1 be0 th0 qke own1 f0 sa1 bo0 qm1 qs1 He0 lb0 He2 qv He1 qk0 U0 h1 qn1 H1 tg10 tg12 own2 tg11 ls10 ls12 ls11 V0 V3 xd1 xe1 qt2 e1 xh0 Rb0 sa2 qo1 qs2 th1 bb1 h2 qk1 tg22 tg21 tg20 ls22 ls21 ls20 f1 fw bo1 I1 v24 qm2 lb1 Rc0 I2 Rc1 I0 bc0 qk2 e2 X1 qn2 X2 f2 le fo o1 Z3 lf Z2 xg21 xg10 xg00 qf1 qf2 qf0 ys1 ys2 ys0', 'S': 'lu lx2 zr01 cz1 ez0 clb r7 m16 m16b clc far sz3 cm4 hz cm6 lane cm2 cm3 lane_o dec cm1 ups cm5 tas cm0 cla tbs cma sb0 T3 T1 T0 lane_e T2 Tl2 xa0 Ra3 Ra0 be1 xb0 xb1 sb1 ba1 ba0 He3 xc0 xc1 U3 U2 H0 U1 V1 V2 xd0 xe0 H2 H3 Rb2 Rb1 xh1 sb2 Rb3 bb0 W2 W0 W1 W3 xf0 xf1 I3 Rc3 Rc2 xi1 bc1 xi0 X3 X0 J1 J0 J3 Z1 J2 Z0 xg11 xg20 xg01 o2 oa oc2 os3 os0 y1 os2 y0'}
+ORDER = {'Y': 'lu lx0 lv lws lwc os3 os2 os1 oa', 'G': 'pi room f0i cr zr01 cz3 ez1 eb sz3 cap sc0s clb zr10 cz1 sl0 cmb zr21 zr00 bz g3 sc1s sl1 sc2s df1 sl2 sn zr20', 'T': 'pd0 pb0 pa0 pc0 mT1 mTl1 mT3 mTl3 mT0 mT2 mTl2 mRa0 mRa2 mRa3 mRa1 mTl0 pb1 pa1 mHe2 mHe0 mHe1 mHe3 mU3 mU0 pc1 mU2 mH1 mU1 mH0 mV2 mV3 mV0 mV1 mH2 mRb3 mH3 mRb0 mRb2 mRb1 pb2 pa2 mW0 pc2 mW3 mW2 mW1 mRc1 mRc2 mRc0 mI1 mI3 mI2 mI0 mRc3 mX2 mX0 mX3 mX1 mJ1 mJ3 mJ0 mZ1 mZ3 mJ2 mZ2 mZ0 my1 my2 my0', 'V': 'zz mi1 mi0 hz zr11 mf ki cz2 ez0 r0 lo383 lane_o zx1 ul dec0 qu xl2 negc xl0 qx1 upq qx0 xl1 qx2 cna1 taq qcn sa0 qe1 qs0 tbq qe3 qe0 h0 qe2 own2 tg02 tg01 tg00 Tl1 ls02 ls01 ls00 Tl3 T2 Tl2 xb1 e0 Ra0 Ra2 Ra1 cm1 qt1 be1 qv th0 qke own1 f0 sa1 qm1 bo0 qcone He2 lb0 qs1 He3 qk0 U3 h1 qn1 H1 tg11 tg12 tg10 ls11 ls12 ls10 V2 V0 V1 xd1 xe1 H2 qt2 e1 xh0 xh1 sa2 qo1 qs2 th1 zx2 bb0 h2 qk1 tg22 tg20 tg21 fw ls22 ls20 ls21 f1 xf0 bo1 v24 I1 lb1 qm2 le Rc0 Rc3 e2 bc0 X2 qk2 f2 X1 qn2 fo J1 J3 lf Z1 J0 Z2 xg21 xg10 xg00 qf1 qf2 qf0 o1 ys1 ys2 ys0', 'S': 'lx1 lx2 df0 cnz ez2 far0 m16 m16b cn0 cn6 cn5 cn1 cn2 cn3 cn4 ups cna2 cna0 tas sd0 sb0 far r7 tbs dec lane cm5 cla cm2 cm6 cm0 cm3 cm4 clc T1 T3 T0 xa1 xa0 Ra3 Tl0 be0 cma xb0 ba0 sb1 ba1 He0 He1 xc0 xc1 U0 U2 U1 H0 V3 xd0 xe0 Rb3 H3 Rb0 lane_e Rb2 sb2 Rb1 bb1 W0 W3 W2 W1 Rc1 Rc2 xf1 I3 I2 I0 xi1 bc1 xi0 X0 X3 Z3 J2 Z0 xg11 xg20 xg01 oc1 oc2 oc0 os0 o2 y1 y2 y0'}
+ORDER = {'Y': 'lx0 lu lws lwc lv oa os1 os0', 'G': 'pi room cr cap eb ez2 cmb zr11 clb sc0s sc0q g3 sl0 zr01 sc1s zr20 sl1 sc2s zr10 sl2 sn', 'T': 'pb0 pa0 mT2 mT0 mT1 pc0 mT3 mTl3 mTl0 mTl2 mTl1 mRa3 mRa2 mRa1 mRa0 pa1 pb1 mHe2 mHe0 mHe1 mHe3 mU3 mU0 pc1 mH1 mU2 mH0 mU1 mV3 mV1 mV0 mV2 mH2 mRb3 mH3 mRb0 mRb1 pb2 pa2 mRb2 pc2 mW0 mW2 mW1 mW3 mRc1 mI3 mI1 mRc0 mI0 mRc2 mRc3 mI2 mX2 mX3 mX0 mX1 mJ1 mJ0 mJ3 mZ1 mZ3 mJ2 mZ0 mZ2 my1 my2 my0', 'V': 'zz cz1 mi1 mi0 sz3 ki mf ul ez0 negc m16 lo383 m16b dec0 xl0 xl2 xl1 qx0 qx1 qe2 qu taq upq tbq qe0 qe1 sa0 qcone qs0 zx1 qe3 zx2 T1 h0 tg01 tg02 tg00 ls01 ls02 ls00 Tl3 own1 xa1 e0 xb0 Ra3 Ra1 Ra0 qt1 be0 qke th0 df1 sa1 f0 qm1 bo0 qs1 lane_e lb0 qk0 He1 He3 qv U3 h1 qn1 tg11 tg12 tg10 ls11 ls12 ls10 H0 V3 V1 e1 V0 V2 xd1 H2 qt2 Rb1 xh0 th1 sa2 qo1 qs2 bb1 h2 qk1 tg21 tg20 tg22 own2 ls21 ls20 ls22 f1 fw bo1 Rc1 I3 v24 lb1 qm2 Rc0 Rc2 Rc3 I2 le bc0 o1 e2 qk2 X2 f2 qn2 X1 J1 fo lf o2 Z3 Z0 xg21 xg10 xg00 qf1 qf2 qf0 ys1 ys2 ys0', 'S': 'lx1 cz2 ez1 sz2 cz3 clc r7 df0 far cm3 cm1 cm6 cm4 cm2 cm5 cm0 tas hz ups tbs cma sb0 bz dec lane T2 cla T0 zr21 T3 Tl1 zr00 Tl0 Tl2 xa0 Ra2 xb1 be1 lane_o ba0 sb1 ba1 He2 He0 xc0 xc1 U0 H1 U2 U1 xd0 xe1 xe0 H3 Rb0 xh1 Rb3 sb2 Rb2 bb0 W0 W1 W2 W3 xf0 xf1 I1 I0 xi1 bc1 xi0 X3 X0 J0 J3 Z1 J2 Z2 xg11 xg20 xg01 oc1 os2 oc0 os3 y1 y0'}
+ORDER = {'Y': 'lx0 lu lws lv lwc oa os2 os0 os1', 'G': 'pi room cr zx2 ez2 sz3 eb cmb cap sc0s sc0q sl0 g3 sc1s sl1 zr11 sc2s sl2 zr21 sn', 'T': 'pb0 pa0 mT2 mT0 pc0 mTl2 mT1 mTl0 mT3 mTl3 mTl1 mRa2 mRa0 mRa3 mRa1 pb1 pa1 mHe0 mHe2 mHe1 mHe3 mU3 pc1 mU0 mU2 mH1 mU1 mH0 mV3 mV1 mV0 mV2 mH2 mRb2 mRb3 mH3 mRb1 mRb0 pb2 pa2 mW0 pc2 mW2 mW1 mW3 mRc1 mI1 mRc3 mRc2 mRc0 mI3 mI0 mI2 mX1 mX2 mX3 mX0 mJ3 mJ1 mJ0 mZ1 mZ3 mJ2 mZ0 mZ2 my1 my2 my0', 'V': 'zz mi0 mi1 ki df1 r7 mf sz2 negc cz1 lo383 qx0 xl0 qx1 xl2 xl1 ul qu taq upq tbq qe2 qe0 sa0 qcone qs0 qe1 lane dec0 qe3 h0 zx1 tg01 tg00 tg02 ls01 ls00 ls02 Tl3 zr01 T3 zr10 zr00 xa1 Ra2 Ra1 qt1 be0 e0 th0 qke f0 sa1 bo0 qm1 qs1 He0 lb0 qk0 He3 xc0 U3 h1 qn1 tg11 H1 tg10 tg12 ls11 ls10 ls12 V3 V0 V2 xd1 xe1 Rb3 qt2 H2 Rb1 e1 xh0 sa2 qo1 qs2 th1 lane_o qv W0 f1 h2 qk1 tg21 tg22 tg20 ls21 ls22 ls20 fw bo1 xf0 lb1 I1 v24 qm2 Rc2 I0 Rc1 I2 bc0 own2 e2 qk2 X2 qn2 f2 X0 fo o1 J3 le lf Z1 J0 Z0 xg21 xg10 xg00 qf1 qf2 o2 qf0 ys1 ys2 ys0', 'S': 'lx1 cz2 cz3 ez0 ez1 m16 m16b far cm2 cm0 cm6 cm1 hz cm5 cm3 clb cm4 tas ups tbs cma sb0 clc df0 cla T2 T0 dec Tl2 lane_e T1 Tl1 Tl0 xa0 xb1 bz Ra3 Ra0 own1 be1 xb0 sb1 ba1 ba0 He2 He1 xc1 U0 U2 U1 H0 V1 xd0 xe0 H3 Rb0 xh1 Rb2 sb2 bb1 bb0 zr20 W2 W1 W3 xf1 Rc0 I3 Rc3 xi1 bc1 xi0 X1 X3 J1 Z3 J2 Z2 xg11 xg20 xg01 oc1 oc0 os3 y1 y0'}
+ORDER = {'Y': 'lx0 lu lv lws lwc os0 os1 os2 y0', 'G': 'pi room cr cap ez2 eb hz zr00 cmb zx1 sc0s sc0q sl0 g3 bz df0 sc1s sl1 sc2s sl2 sn', 'T': 'pb0 pa0 mT2 pc0 mT0 mT1 mT3 mTl1 mTl2 mTl0 mTl3 mRa2 mRa3 mRa1 mRa0 pb1 pa1 mHe2 mHe0 mHe1 mHe3 mU3 pc1 mU0 mH1 mU2 mU1 mH0 mV2 mV3 mV1 mV0 mH2 mH3 mRb1 mRb0 mRb3 mRb2 pb2 pa2 mW1 pc2 mW0 mW3 mW2 mI3 mI1 mI0 mRc0 mRc3 mRc1 mRc2 mI2 mX0 mX3 mX2 mX1 mJ1 mJ3 mJ0 mZ1 mZ3 mZ2 mZ0 mJ2 my1 my2 my0', 'V': 'zz cz1 mi0 ki mi1 sz3 negc mf ez1 cz2 m16 lo383 ul xl0 xl2 qx0 xl1 qx1 qu taq upq qe2 tbq dec0 qe3 sa0 qcone qs0 qe0 qe1 h0 lane zx2 tg00 tg02 tg01 ls00 ls02 ls01 T3 Tl3 Tl2 xa1 e0 lane_e Ra3 Ra0 qt1 be0 qke own1 th0 sa1 f0 qm1 bo0 qs1 lb0 He2 qk0 He3 U3 h1 qn1 tg12 tg11 tg10 ls12 ls10 ls11 V2 V3 xd1 xe1 xe0 H2 qt2 Rb0 zr21 xh0 Rb2 sa2 qo1 qs2 e1 qv th1 W1 h2 qk1 tg20 tg21 tg22 f1 ls20 ls21 ls22 zr20 bo1 xf0 fw lb1 qm2 lane_o v24 Rc3 Rc2 I2 bc0 own2 o1 qk2 e2 X2 qn2 f2 le o2 fo J1 J3 lf Z1 Z2 Z0 xg21 xg10 xg00 qf1 qf2 qf0 ys1 ys2 ys0', 'S': 'lx1 ez0 zr11 sz2 r7 far df1 m16b cm1 zr10 cz3 cm2 cm5 cm3 cm6 clb cm0 cm4 tas ups tbs cma sb0 T2 clc dec cla T0 T1 Tl1 Tl0 xa0 xb1 zr01 Ra2 Ra1 be1 xb0 ba0 sb1 ba1 He0 He1 xc0 xc1 U0 H1 U2 U1 H0 V1 V0 xd0 Rb1 H3 Rb3 xh1 sb2 bb1 bb0 W0 W3 W2 xf1 I3 I1 I0 Rc0 Rc1 xi1 bc1 xi0 X3 X0 X1 J0 Z3 oa J2 xg11 xg20 xg01 oc1 os3 oc0 y1'}
+ORDER = {'Y': 'lx0 lu lwc lws lv oa os2 os3 os1 y0', 'G': 'pi room cr ez2 eb sz3 cap cmb sc0s sc0q zx1 sl0 zx2 g3 sc1s sl1 sc2s sl2 zr20 sn', 'T': 'pb0 pa0 mT0 mT2 pc0 mT1 mTl3 mT3 mTl0 mTl1 mTl2 mRa3 mRa1 mRa2 mRa0 pb1 pa1 mHe0 mHe2 mHe1 mHe3 mU3 pc1 mU0 mU2 mH1 mU1 mH0 mV1 mV3 mV2 mV0 mH2 mH3 mRb1 mRb3 mRb2 mRb0 pb2 pa2 mW1 mW3 pc2 mW0 mW2 mI3 mI1 mI0 mRc2 mRc1 mRc0 mRc3 mI2 mX0 mX2 mX3 mX1 mJ0 mJ1 mJ3 mZ3 mZ1 mZ2 mZ0 mJ2 my1 my2 my0', 'V': 'zz mi1 mi0 ki cz2 mf cz3 m16 negc lo383 ul xl2 xl0 qx0 xl1 qx1 cla dec0 qu taq upq cm3 tbq qe0 qe2 sa0 qcone qs0 qe1 qe3 dec h0 tg01 tg00 tg02 ls01 ls00 ls02 T3 xa1 Tl2 e0 Ra3 Ra0 qt1 be0 df0 qke own1 th0 sa1 f0 qm1 bo0 qs1 lb0 He0 qk0 He3 lane_e U3 h1 qn1 tg11 tg10 tg12 H1 ls11 ls10 ls12 H0 xd1 xe1 xe0 H3 qt2 Rb0 xh0 e1 sa2 qo1 qs2 qv th1 bb0 h2 qk1 tg20 tg21 tg22 ls20 ls21 ls22 f1 fw xf0 bo1 v24 I1 qm2 lb1 I0 Rc0 Rc3 I2 bc0 o1 qk2 e2 X3 f2 qn2 le own2 fo J1 J0 lf Z1 Z2 xg21 xg10 xg00 qf1 qf2 qf0 ys2 ys0', 'S': 'lx1 ez1 sz2 hz r7 m16b ez0 far cz1 zr10 cm0 cm4 cm1 cm2 cm5 clb tas ups cm6 tbs cma lane sb0 T0 T2 clc zr01 T1 Tl0 Tl3 zr00 Tl1 xa0 xb1 Ra1 Ra2 bz be1 xb0 ba1 sb1 ba0 He2 He1 zr11 xc0 xc1 U0 U2 U1 V1 V3 V2 V0 xd0 df1 H2 Rb1 zr21 xh1 Rb2 sb2 Rb3 bb1 W1 W3 lane_o xf1 W0 W2 I3 Rc2 Rc1 xi1 bc1 xi0 X2 X0 X1 o2 J3 Z3 Z0 J2 xg11 xg20 xg01 oc1 ys1 oc0 y1 os0'}
+ORDER = {'Y': 'lx1 lu lwc lv lws os3 os1 y2 y0', 'G': 'pi room cr eb cmb clb cap cz3 hz g3 sc0s sc0q zr00 bz sl0 zx1 df1 zr11 sc1s sl1 sc2s sl2 sn', 'T': 'pb0 pa0 mTl1 mT3 mT1 mT2 pc0 mTl2 mTl0 mT0 mTl3 mRa3 mRa1 mRa0 mRa2 pb1 pa1 mU0 mU3 mU1 mU2 mHe1 mHe3 mHe2 mHe0 pc1 mH0 mH3 mH2 mH1 mV3 mV2 mV0 mV1 mRb0 mRb2 mRb3 mRb1 pb2 pa2 mW0 mW2 mW3 mW1 pc2 mI3 mI0 mI2 mRc2 mI1 mRc1 mRc3 mRc0 mX0 mX1 mZ0 mX3 mZ1 mZ3 mZ2 mX2 mJ0 mJ2 mJ3 mJ1 my2 my1 my0', 'V': 'zz cz1 mi0 mi1 ki zr10 mf ez1 ul lo383 negc qe1 xl2 xl0 qx1 xl1 cm3 qx0 cm1 qu taq upq qe2 tbq qe3 sa0 qcone qs0 own1 qe0 dec0 T3 h0 qv tg01 tg02 tg00 ls01 ls02 ls00 Tl0 xa1 xb0 qt1 Ra1 Ra2 qm1 e0 be0 th0 sa1 qke f0 U0 qs1 bo0 U1 He3 lb0 qk0 He0 h1 xc0 tg10 tg11 tg12 qn1 ls10 ls12 ls11 H2 xd1 V3 V0 V1 Rb0 xe1 Rb2 qt2 xh1 Rb1 qo1 sa2 th1 qs2 e1 lane_e W2 qk1 h2 f1 tg20 tg21 tg22 bo1 ls20 ls21 ls22 lb1 qm2 fw I2 I1 v24 Rc3 xi1 o1 e2 qn2 bc0 o2 le own2 qk2 f2 X3 fo lf J0 J2 J3 xg20 xg21 xg00 qf2 qf1 qf0 ys2 ys1 ys0', 'S': 'lx0 zr01 cz2 ez0 ez2 cla m16b m16 r7 zr20 far sz3 df0 cm2 cm6 sz2 cm0 cm5 cm4 tas ups tbs cma sb0 zx2 Tl1 clc lane T1 dec T2 T0 Tl2 Tl3 zr21 xa0 xb1 Ra3 Ra0 be1 sb1 ba0 U3 ba1 He1 U2 He2 xc1 H0 H3 H1 V2 xd0 xe0 xh0 Rb3 bb0 sb2 bb1 W0 W3 W1 xf0 lane_o xf1 I0 I3 Rc2 Rc1 xi0 Rc0 X0 bc1 X1 Z0 oa Z1 Z2 X2 Z3 J1 xg10 xg11 xg01 oc2 oc1 oc0 os2 y1 os0'}
+ORDER = {'Y': 'lx0 lu lwc lv lws oa os0 y2 y1 y0', 'G': 'pi room cr ez2 eb g3 zx2 bz cap cmb cz3 sc0s sc0q sl0 zx1 sc1s sl1 zr11 sc2s sl2 sn', 'T': 'pb0 pa0 mT3 mT2 mT1 pc0 mTl3 mTl2 mT0 mTl0 mTl1 mRa3 mRa0 mRa1 mRa2 pb1 pa1 mU3 mU0 mU1 mU2 pc1 mHe0 mHe1 mHe3 mHe2 mH3 mH0 mH2 mH1 mV3 mV1 mV0 mV2 mRb2 mRb0 mRb3 mRb1 pb2 pa2 mW2 mW0 mW1 mW3 pc2 mI2 mI0 mI1 mI3 mRc1 mRc3 mRc2 mRc0 mX1 mX0 mX3 mZ0 mZ3 mX2 mZ2 mZ1 mJ0 mJ2 mJ3 mJ1 my2 my1 my0', 'V': 'zz mi1 mi0 ki mf negc r7 m16 ul ez0 lo383 xl0 xl2 cm6 xl1 qx0 qx1 qe1 qu taq upq tbq qe3 qe2 sa0 qcone qs0 dec0 hz qe0 T2 dec h0 qv tg00 tg02 tg01 ls00 ls02 ls01 Tl1 zr00 xa1 xb1 qt1 e0 qm1 Ra0 Ra2 sa1 be1 qs1 th0 qke ba1 f0 h1 qk0 bo0 tg12 tg10 tg11 lb0 ls12 ls10 ls11 He2 df0 xc0 qn1 xd0 H2 H1 V3 V1 V0 V2 e1 zr21 xe0 Rb0 qt2 Rb1 Rb3 qo1 sa2 lane_o qs2 own2 th1 W2 qk1 f1 h2 bo1 tg20 tg22 tg21 ls20 ls22 ls21 fw qm2 lb1 v24 I3 zr20 Rc1 xi1 Rc3 lane_e qn2 bc0 qk2 e2 Z0 f2 o1 le fo Z3 lf J2 J3 xg20 xg21 xg00 qf2 qf1 qf0 ys2 ys1 ys0', 'S': 'lx1 ez1 sz2 sz3 lane far m16b cz2 cm0 cm4 clb cz1 cm1 cm3 cm2 tas ups cm5 tbs cma sb0 cla T3 T1 clc own1 Tl3 Tl2 T0 Tl0 xa0 xb0 zr01 Ra3 Ra1 sb1 be0 ba0 U3 U0 zr10 U1 He1 He0 He3 U2 xc1 H3 df1 H0 xd1 xh0 xe1 Rb2 xh1 bb0 sb2 bb1 W1 W3 W0 xf1 xf0 I2 I0 I1 xi0 Rc0 Rc2 X0 bc1 X1 X3 Z1 Z2 X2 J0 o2 J1 xg10 xg11 xg01 oc2 oc1 os1 oc0 os3 os2'}
 
 
 def steps(g, core, T, topo):
@@ -77,12 +96,12 @@ def steps(g, core, T, topo):
     def const(name, ap, val):
         n = ap.shape[1]
         alts = {"V": lambda: V.memset(ap, float(val)), "G": lambda: g.iota(ap, [[0, n]], val, 0, allow_small_or_imprecise_dtypes=True)}
-        if name != "c64":
-            alts["S"] = lambda: ACT.activation(ap, T.c64[:, 0:n], AF.Copy, scale=val / 64.0)
-        op(name, alts, "c64" if "S" in alts else "")
+        if name != "zz":
+            alts["S"] = lambda: ACT.activation(ap, T.zz[:, 0:n], AF.Identity, bias=float(val))
+        op(name, alts, "" if name == "zz" else "zz")
 
-    def quant(name, nm, a, b, src, reads):
-        op(name, {"V": lambda: V.quantize_mx(T["q" + nm][:, a:b], T["s" + nm][:, a:b], src)}, reads)
+    def quant(name, nm, a, b, src, reads, writes=None):
+        op(name, {"V": lambda: V.quantize_mx(T["q" + nm][:, a:b], T["s" + nm][:, a:b], src)}, reads, writes)
 
     def side(nm, a, b):
         return T["q" + nm][:, a:b], T["s" + nm][:, a:b]
@@ -99,13 +118,14 @@ def steps(g, core, T, topo):
         op(name, {"V": lambda: V.tensor_scalar(out, psum(src, a, z), scale, None, MUL),
                   "S": lambda: ACT.activation(out, psum(src, a, z), AF.Copy, scale=scale)}, src, frees=src)
 
-    def gather(name, tile, c0, win, lst, l0, cuts, reads):
-        for i in range(len(cuts) - 1):
-            a, b = cuts[i], cuts[i + 1]
-            out, off = tile[:, 4 * c0 + 16 * a:4 * c0 + 16 * b], lst[:, l0 + a:l0 + b]
-            op("%s%d" % (name, i), {"V": lambda out=out, off=off: V.tensor_copy(out, win.indirect(off)),
-                                    "S": lambda out=out, off=off: ACT.activation(out, win.indirect(off), AF.Copy)}, reads)
-        return " ".join("%s%d" % (name, i) for i in range(len(cuts) - 1))
+    def gather(name, tile, c0, n, win, a, z, off, reads, planes):
+        for h in range(2):
+            out, src = tile[:, 4 * c0 + h:4 * (c0 + n):2], T[win + str(h)][:, a:z]
+            need = " ".join(p + str(b) for p in planes.split() for b in (h, h + 2))
+            op(name + str(h), {"V": lambda out=out, src=src: V.tensor_copy(out, src.indirect(off)),
+                               "S": lambda out=out, src=src: ACT.activation(out, src.indirect(off), AF.Copy)},
+               reads.replace("#", str(h)) + " " + need)
+        return name + "0 " + name + "1"
 
     def pick(name, dst, a, z, src, w, off, reads):
         q, s = "q", "s"
@@ -131,207 +151,240 @@ def steps(g, core, T, topo):
     def codes(dst, src):
         return [(T["q" + dst][:].bitcast(dt.uint8), T["q" + src][:, 0:A].bitcast(dt.uint8)), (T["s" + dst][:], T["s" + src][:, 0:A])]
 
-    def product(name, left, nm, n, a, z, dst, at, reads):
+    def product(name, left, nm, c0, n, a, z, win, at, reads):
         for b in range(4):
-            mm("m%s%d" % (name, b), [(side(k, 128 * b, 128 * b + 128), side(nm, 0, n)) for k in left], n,
+            mm("m%s%d" % (name, b), [(side(k, 128 * b, 128 * b + 128), side(nm, c0, c0 + n)) for k in left], n,
                "qe%d %s %s" % (b, reads, "lwc lws" if "w" in left else ""))
-            evac(name + str(b), "m%s%d" % (name, b), a, z, dst[:, at + b:at + 4 * (z - a):4], 0.015625)
-        return " ".join(name + str(b) for b in range(4))
+            evac(name + str(b), "m%s%d" % (name, b), a, z, T[win + str(b % 2)][:, at + b // 2:at + 2 * (z - a):2], 0.015625)
 
-    X0 = 4 * E2
-    dma("lx0", T.xin[:, X0:X0 + 768], T.x[:, 0:768], "lx0", "")
-    dma("lx1", T.xin[:, X0 + 768:X0 + 1536], T.x[:, 768:1536], "lx1", "")
     dma("lu", T.uin[:], T.u[:], "lu", "")
-    dma("lwc", T.qw[:].bitcast(dt.uint8), T.wc[:], "lwc", "lu")
-    dma("lws", T.sw[:], T.ws[:], "lws", "lu")
-    dma("lv", T.vin[:], T.v[:], "lv", "lu")
+    for i, (a, z) in enumerate(zip(XCUT, XCUT[1:])):
+        dma("lx%d" % i, T.xin[:, X0 + 4 * a:X0 + 4 * z], T.x[:, 4 * a:4 * z], "lx%d" % i, "")
+    dma("lwc", T.qw[:].bitcast(dt.uint8), T.wc[:], "lwc", "")
+    dma("lws", T.sw[:], T.ws[:], "lws", "")
+    dma("lv", T.vin[:], T.v[:], "lv", "")
 
-    sc = T.sc
-    m, mq, hi, m16 = (T.mf[:, i:i + 1] for i in range(4))
-    op("pi", {"G": lambda: g.iota(T.pi[:, 0:1], [[0, 1]], 0, 1)}, "")
-    op("pi16", {"G": lambda: g.iota(T.pi[:, 1:2], [[0, 1]], 0, 16)}, "")
-    iota("xv", T.xv[:], [[129, 3], [2, 8]], 0)
-    iota("cr", T.cr[:], [[1, S]], 0)
-    iota("crp", T.crp[:], [[1, S]], 0, -1)
-    iota("pp", T.pj[:, 6:8], [[0, 2]], 0, 1)
-    iota("cap", T.cap[:], [[-ROW, S], [ROW, 7]], TOPV)
-    const("c64", T.c64[:], 64)
+    m, mh2 = T.mf[:, 0:1], T.mf[:, 1:2]
+    lane, m16, m16b, lo383, negc, lane_e, lane_o = (T.sc[:, i:i + 1] for i in range(7))
+    op("pi", {"G": lambda: g.iota(T.pi[:], [[0, 1]], 0, 1)}, "")
+    iota("cr", T.cr[:], [[2, S]], 0)
+    iota("room", T.room[:], [[S, 7]], -1, -1)
+    iota("cap", T.cap[:], [[-2, S], [ROW, 7]], K + 2 * (S - 1))
+    const("zz", T.zz[:], 0)
     for b in range(3):
         const("ez%d" % b, T.eb[:, b:516:4], 0)
-    op("eb", {"G": lambda: g.affine_select(T.eb[:, 3:515:4], T.c64[:, 0:128], [[-1, 128]], AluOpType.is_equal, 0.0, 0, 1)}, "c64")
+    op("eb", {"G": lambda: g.affine_select(T.eb[:, 3:515:4], T.zz[:, 0:128], [[-1, 128]], NE, 64.0, 0, 1)}, "zz")
     for b in range(4):
         quant("qe%d" % b, "e", 128 * b, 128 * b + 128, T.eb[:, 3 - b:515 - b], "eb ez0 ez1 ez2")
-    ts("mi0", T.mi[:, 0:1], T.pi[:, 0:1], 15, None, AND, None, "pi")
-    ts("mi1", T.mi[:, 1:2], T.pi[:, 0:1], 2, 3, SHR, AND, "pi")
-    ts("mi2", T.mi[:, 2:3], T.pi[:, 0:1], 3, 1, SHR, AND, "pi")
-    ts("mi3", T.mi[:, 3:4], T.pi[:, 1:2], 255, None, AND, None, "pi16")
-    cp("mf", T.mf[:], T.mi[:], "mi0 mi1 mi2 mi3")
-    for i, f in enumerate((ROW, 92, -100)):
-        lin("sc%d" % i, sc[:, i:i + 1], mq, float(f), m, "mf")
-    lin("sc3", sc[:, 3:4], mq, float(ROW), -16.0 * ROW, "mf")
-    ts("ul", T.ul[:], T.cr[:, 0:8], 16.0, None, MUL, None, "cr")
-    ts("rp4", T.rp4[:], T.cr[:, 0:6], 4.0, mq, MUL, ADD, "cr mf")
-    lin("sc4", sc[:, 4:5], hi, 1.0 - C, m16, "mf")
-    ts("xl0", T.xl[:, 0:S:3], T.xv[:, 0:8], m16, None, ADD, None, "xv mf")
-    ts("xl1", T.xl[:, 1:S:3], T.xv[:, 16:24], sc[:, 4:5], -2.0, ADD, ADD, "xv sc4")
-    ts("xl2", T.xl[:, 2:S:3], T.xv[:, 8:16], m16, None, ADD, None, "xv mf")
-    lin("j1", T.pj[:, 0:6], T.cr[:, 0:6], 16.0, m, "cr mf")
-    lin("kf0", T.kf[:, 6:8], T.pj[:, 6:8], 1.0 / S, -11.5 / S, "pp")
-    lin("kf1", T.kf[:, 0:6], T.pj[:, 0:6], 1.0 / 6, -2.5 / 6, "j1")
-    cp("ki0", T.ki[:, 6:8], T.kf[:, 6:8], "kf0")
-    cp("ki1", T.ki[:, 0:6], T.kf[:, 0:6], "kf1")
-    ts("ku", T.ku[:], T.ki[:, 0:6], -6.0, None, MUL, None, "ki1")
-    tt("kv", T.kv[:], T.ku[:], T.pj[:, 0:6], ADD, "ku j1")
-    cp("rth", T.rth[:], T.kv[:, 0:4], "kv")
-    cp("kq", T.kq[:, 0:1], T.ki[:, 6:7], "ki0")
-    ts("k24", T.kq[:, 1:2], T.ki[:, 6:7], float(S), None, MUL, None, "ki0")
-    op("far", {"S": lambda: ACT.activation(T.far[:], T.crp[:], AF.Abs, bias=T.kq[:, 1:2])}, "crp k24")
-    ts("room", T.room[:], T.cr[:, 0:8], T.kq[:, 0:1], None, SUB, None, "cr kq")
-    const("cz0", T.cm[:, 0:4 * NC:28], 0)
+    ts("mi0", T.mi[:, 0:1], T.pi[:], 15, None, AND, None, "pi")
+    ts("mi1", T.mi[:, 1:2], T.pi[:], 14, None, AND, None, "pi")
+    cp("mf", T.mf[:], T.mi[:], "mi0 mi1")
+    lin("lane", lane, mh2, -0.5 * ROW, m, "mf")
+    lin("lane_e", lane_e, mh2, 0.5 * ROW - 1, m, "mf")
+    lin("lane_o", lane_o, mh2, -0.5 * ROW - 1, m, "mf")
+    ts("ul", T.ul[:], T.cr[:, 0:8], 8.0, None, MUL, None, "cr")
+    lin("m16", m16, m, 16.0, 0.0, "mf")
+    lin("m16b", m16b, m, 16.0, 256.0 - (C - 1), "mf")
+    ts("lo383", lo383, m, 8.0, C - 1.0, LT, MUL, "mf")
+    ts("xl0", T.xl[:, 0:S:3], T.cr[:, 0:8], m16, None, ADD, None, "cr m16")
+    ts("xl1", T.xl[:, 1:S:3], T.cr[:, 0:8], m16b, lo383, ADD, ADD, "cr m16b lo383")
+    ts("xl2", T.xl[:, 2:S:3], T.cr[:, 0:8], m16, 129.0, ADD, ADD, "cr m16")
+    ts("ki", T.ki[:], T.room[:, 1:2], -1.0 / S, 11.5 / S, MUL, ADD, "room")
+    ts("negc", negc, T.ki[:], float(S), T.room[:, 1:2], MUL, ADD, "ki room")
+    op("far", {"S": lambda: ACT.activation(T.far[:], T.cr[:], AF.Abs, bias=negc, scale=-0.5)}, "cr negc")
+    lin("r7", T.r7[:], T.room[:], 1.0 / S, 0.5 / S, "room")
     for b in range(1, 4):
         const("cz%d" % b, T.cm[:, b:4 * NC:4], 0)
-    const("cw", T.cw[:], int(BIG / 2))
-    for e in range(1, 7):
-        ts("cm%d" % e, T.cm[:, 4 * e:4 * NC:28], T.far[:], T.room[:, e:e + 1], BIG, LT, MUL, "far room")
-    op("cm0", {"G": lambda: g.affine_select(T.cm[:, 249:4 * NC:28], T.cw[:], [[-1, 16]], AluOpType.is_equal, 0.0, -112, 1)}, "cw cz1")
-    quant("qcone", "cone", 0, NC, T.cm[:], "cz0 cz2 cz3 " + " ".join("cm%d" % e for e in range(7)))
-    const("sz2", T.sg[:, 2:512:4], 0)
+    for e in range(7):
+        op("cm%d" % e, {"S": lambda e=e: ACT.activation(T.ins[:, e:NC:7], T.far[:], AF.Sign, bias=T.r7[:, e:e + 1], scale=-1.0),
+                        "V": lambda e=e: V.tensor_scalar(T.ins[:, e:NC:7], T.far[:], T.r7[:, e:e + 1], None, LT)}, "far r7")
+    op("cma", {"S": lambda: ACT.activation(T.cm[:, 0:4 * NC:4], T.ins[:], AF.Relu, scale=BIG)}, " ".join("cm%d" % e for e in range(7)))
+    op("cmb", {"G": lambda: g.affine_select(T.cm[:, 25:25 + 28 * 16:28], T.zz[:, 0:16], [[1, 16]], NE, BIG if SBV else BIG / 2, -127, 1)}, "cz1")
+    quant("qcone", "cone", 0, NC, T.cm[:], "cz2 cz3 cma cmb")
+    if NATIVE:
+        iota("f0i", T.f0i[:], [[-16, 40]], 16 * (S - 1), -1)
+        op("far0", {"S": lambda: ACT.activation(T.far0[:], T.f0i[:], AF.Abs, bias=m)}, "f0i mf")
+        ts("r0", T.r0e[:], T.cr[:, 0:7], 0.5, m, MUL, SUB, "cr mf")
+        for e in range(7):
+            op("cn%d" % e, {"S": lambda e=e: ACT.activation(T.in0[:, e:280:7], T.far0[:], AF.Sign, bias=T.r0e[:, e:e + 1], scale=-1.0 / 16)}, "far0 r0")
+        for b in range(3):
+            w, src = BIG if b == 2 else BIG / 2, T.in0[:, 56 * b:56 * b + NC]
+            op("cna%d" % b, {"S": lambda b=b, w=w, src=src: ACT.activation(T.cn[:, b:4 * NC:4], src, AF.Relu, scale=w),
+                             "V": lambda b=b, w=w, src=src: V.tensor_scalar(T.cn[:, b:4 * NC:4], src, w, 0.0, MUL, MAX)},
+               " ".join("cn%d" % e for e in range(7)))
+        const("cnz", T.cn[:, 3:4 * NC:4], 0)
+        quant("qcn", "cn", 0, NC, T.cn[:], "cna0 cna1 cna2 cnz")
+    else:
+        const("sz2", T.sg[:, 2:512:4], 0)
     const("sz3", T.sg[:, 3:512:4], 0)
-    const("df", T.df[:], -2 * ROW)
-    ts("crm", T.crm[:], T.cr[:], mq, None, SUB, None, "cr mf")
-    for j in range(6):
-        ts("dec%d" % j, T.dec[:, S * j:S * j + S], T.crm[:], 4.0 * j, -2.0 * ROW, LE, MUL, "crm")
-    per = 16 + 4 * ROW
-    iota("cla", T.cl[:, 0:36], [[ROW, 6], [per, 6]], ZP - TOPV)
-    iota("clb", T.cl[:, 36:72], [[-ROW, 6], [per, 6]], ZP - ROW - TOPV)
-    iota("clc", T.cl[:, 72:96], [[ROW, 4], [per, 6]], ZP + 6 * ROW - TOPV)
-    lin("cl", T.cl[:], T.cl[:], 1.0, sc[:, 0:1], "cla clb clc sc0")
-    iota("g3", T.g3[:], [[-ROW, 6], [16, 6]], ZP + 5 * ROW)
-    lin("own1", T.b1[:, 1:72:2], T.g3[:], 1.0, m, "g3 mf")
-    iota("g4", T.g4[:], [[ROW + 4, S], [4 * ROW, 4]], -TOPV)
-    lin("cf", T.cf[:], T.g4[:], 1.0, sc[:, 1:2], "g4 sc1")
-    iota("g5", T.g5[:], [[0, S], [4 * ROW, 4]], 0)
-    lin("cg", T.cg[:], T.g5[:], 1.0, sc[:, 3:4], "g5 sc3")
-    iota("g6", T.g6[:], [[-4 * ROW, 2], [4, S]], 7 * ROW)
-    lin("own2", T.f1[:, 5:192:8], T.g6[:, 0:S], 1.0, sc[:, 2:3], "g6 sc2")
-    lin("own3", T.f1[:, 7:192:8], T.g6[:, S:48], 1.0, sc[:, 2:3], "g6 sc2")
-    const("fz1", T.f1[:, 1:192:8], 0)
-    const("fz3", T.f1[:, 3:192:8], 0)
-    const("bz", T.b0[:, 0:72:2], 0)
-    const("fz", T.f0[:, 0:192:2], 0)
-    for n in ("w0", "rw0", "w1", "rw2"):
-        const("z" + n, T[n][:, 0:ZP], 0)
+    const("hz", T.h[:, 6:NC + 2 * PAD:7], 0)
+    ts("dec0", T.dec0[:], T.cr[:, 0:18], mh2, 25.0, ADD, LT, "cr mf")
+    lin("dec", T.dec[:], T.dec0[:], -2.0 * ROW, ROW - 2.0, "dec0")
+    const("df0", T.df[:, 0:S], -ROW - 2)
+    const("df1", T.df[:, S:2 * S], -ROW + 2)
+    lin("cla", T.cl[:, 0:10], T.cr[:, 0:10], 0.5 * ROW, -float(OFF), "cr")
+    const("clb", T.cl[:, 10:16], K - OFF)
+    lin("clc", T.cl[:, 16:22], T.cr[:, 0:6], -0.5 * ROW, -float(OFF), "cr")
+    iota("g3", T.g3[:], [[-ROW, 6], [16, 3]], 5 * ROW)
+    lin("own1", T.b1[:, 1:36:2], T.g3[:], 1.0, m, "g3 mf")
+    ts("own2", T.f1[:, 1:48:2], T.cr[:], lane_o, 7.0 * ROW, ADD, ADD, "cr lane_o")
+    const("bz", T.b0[:, 0:48:2], 0)
+    for n in ("r0", "w1" if B1_AT_SENDER else "r1", "w2" if B2_AT_SENDER else "r2"):
+        for h in "01":
+            const("z" + n + h, T[n + h][:, 0:ROW], 0)
+    const("zx1", T.x1[:, 4 * MID:4 * A + 512], 0)
+    if XSPLIT:
+        const("zx2", T.x2[:, 4 * MID:4 * A + 512], 0)
 
     def cuts(t, top, reads):
         n = str(t)
-        mm("p" + n, [(side(top, 0, 128), side("up", 0, 128))], 128, reads + " upq ups", fixed=6)
-        mm("pb" + n, [(side(top, 16, A), side("up", 0, 128))], 128, reads + " upq ups", fixed=7)
-        op("sa" + n, {"V": lambda: V.tensor_scalar(T.sg[:, 0:512:4], psum("p" + n, 0, 128), 0.0, 0.5, GT, SUB)}, "p" + n, "sga", frees="p" + n)
-        op("sb" + n, {"S": lambda: ACT.activation(T.sg[:, 1:512:4], psum("pb" + n, 0, 128), AF.Sign, bias=-1e-37)}, "pb" + n, "sgb", frees="pb" + n)
-        op("qs" + n, {"V": lambda: V.quantize_mx(T.qsign[:], T.ssign[:], T.sg[:])}, "sga sgb sz2 sz3", "sign")
-        mm("pc" + n, [(side("sign", 0, 128), side("cone", 0, NC))], NC, "sign qcone", fixed=6)
-        op("h" + n, {"V": lambda: V.tensor_tensor_scan(T.h[:], psum("pc" + n, 0, NC), T.cap[:], float(TOPV), MAX, MIN)}, "pc%d cap" % t, "h", frees="pc" + n)
-        lo, hi = (36, 72) if t == R - 1 else (0, 96)
+        native = NATIVE and t == 0
+        parts = ((("a", 256, 2, "qx2", 6), ("b", 128, 1, "qx1", 7), ("d", 0, 0, "qx0", None)) if native else
+                 (("a", 0, 0, reads, 6), ("b", 16, 1, reads, 7)))
+        for k, c0, b, need, fixed in parts:
+            p = "p" + k + n
+            mm(p, [(side("x" if native else top, c0, c0 + 128), side("up", 0, 128))], 128, need + " upq ups", fixed=fixed)
+            if k == "a" or SBV:
+                op("s" + k + n, {"V": lambda p=p, b=b: V.tensor_scalar(T.sg[:, b:512:4], psum(p, 0, 128), 0.0, 0.5, GT, SUB)}, p, "sg%d" % b, frees=p)
+            else:
+                op("s" + k + n, {"S": lambda p=p, b=b: ACT.activation(T.sg[:, b:512:4], psum(p, 0, 128), AF.Sign, bias=-1e-37)}, p, "sg%d" % b, frees=p)
+        op("qs" + n, {"V": lambda: V.quantize_mx(T.qsign[:], T.ssign[:], T.sg[:])}, "sg0 sg1 sz3 " + ("sg2" if NATIVE else "sz2"), "sign")
+        cone = "cn" if native else "cone"
+        mm("pc" + n, [(side("sign", 0, 128), side(cone, 0, NC))], NC, "sign q" + cone, fixed=6)
+        op("h" + n, {"V": lambda: V.tensor_tensor_scan(T.h[:, PAD:PAD + NC], psum("pc" + n, 0, NC), T.cap[:], float(K + ROW), MAX, MIN)},
+           "pc%d cap hz" % t, "h", frees="pc" + n)
+        lo = 16 if t == R - 1 else 0
         tg = T["tg" + n]
-        for j in range(6):
-            scan("tg%d%d" % (t, j), tg[:, S * j:S * j + S], T.dec[:, S * j:S * j + S], T.h[:, 6:NC:7], 0.0, ADD, MAX, "h dec%d" % j)
-            ts("ls%d%d" % (t, j), T["ls" + n][:, lo + j:hi:6], T.cl[:, lo + j:hi:6], tg[:, S * j + S - 1:S * j + S], None, ADD, None, "cl tg%d%d" % (t, j))
-        return " ".join("ls%d%d" % (t, j) for j in range(6))
+        for j in range(3):
+            a = 6 + 7 * 8 * (2 - j)
+            scan("tg%d%d" % (t, j), tg[:, 18 * j:18 * j + 18], T.dec[:], T.h[:, a:a + 7 * 17 + 1:7], 0.0, ADD, MAX, "h dec")
+            ts("ls%d%d" % (t, j), T["ls" + n][:, 3 * lo + j:66:3], T.cl[:, lo:22], tg[:, 18 * j + 17:18 * j + 18], lane, ADD, ADD,
+               "cla clb clc lane tg%d%d" % (t, j))
+        return " ".join("ls%d%d" % (t, j) for j in range(3))
 
     def bottom(t, ls):
         n = str(t)
-        ts("e" + n, T.b1[:, 0:96:2], T["ls" + n][:, 0:48], 10.0 * ROW, None, ADD, None, ls, "e")
-        ts("th" + n, T.th[:], T["ml" + n][:, 0:8], 10.0 * ROW, None, ADD, None, "sl" + n, "th")
-        tt("f" + n, T.b0[:, 1:96:2], T.th[:].indirect(T.rth[:, 0:3]), T.b1[:, 0:96:2], GE, "th rth e", "f")
-        scan("bo" + n, T.bo[:], T.b0[:, 0:72], T.b1[:, 0:72], 0.0, MUL, MAX, "bz f e own1", "bo")
-        cp("lb" + n, T["ls" + n][:, 96:132], T.bo[:, 1:72:2], "bo")
+        ts("e" + n, T.b1[:, 0:36:2], T["ls" + n][:, 0:18], 10.0 * ROW, None, ADD, None, ls, "e")
+        op("th" + n, {"V": lambda: V.tensor_copy(T.th[:], T["ml" + n][:, 0:18])}, "sl" + n, "th")
+        tt("f" + n, T.b0[:, 1:36:2], T.th[:], T.b1[:, 0:36:2], GT, "th e", "f")
+        scan("bo" + n, T.bo[:, 0:36], T.b0[:, 0:36], T.b1[:], 0.0, MUL, MAX, "bz f e own1", "bo")
+        cp("lb" + n, T["ls" + n][:, 66:84], T.bo[:, 1:36:2], "bo")
 
     quant("qu", "u", 0, 128, T.uin[:], "lu")
     pick("up", "up", 0, 128, "u", 128, T.ul[:], "qu ul")
     quant("qv", "v", 0, 128, T.vin[:], "lv")
-    quant("qx0", "x", 0, 192, T.xin[:, X0:X0 + 768], "lx0")
-    quant("qx1", "x", 192, C, T.xin[:, X0 + 768:X0 + 1536], "lx1")
-    top0 = pick("ta", "t0", 0, 160, "x", C, T.xl[:, 0:10], "qx0 qx1 xl0 xl1 xl2")
-    low0 = pick("tb", "t0", 160, C, "x", C, T.xl[:, 10:S], "qx0 qx1 xl0 xl1 xl2")
+    for i, (a, z) in enumerate(zip(XCUT, XCUT[1:])):
+        quant("qx%d" % i, "x", a, z, T.xin[:, X0 + 4 * a:X0 + 4 * z], "lx%d" % i)
+    qx = " ".join("qx%d" % i for i in range(len(XCUT) - 1)) + " xl0 xl1 xl2"
+    top0 = pick("ta", "t0", 0, 160, "x", C, T.xl[:, 0:10], qx)
+    low0 = pick("tb", "t0", 160, C, "x", C, T.xl[:, 10:S], qx)
 
-    send("sc0s", 0, codes("r0", "t0"), "ac0", top0)
-    t0 = product("T", "e", "t0", C, 0, C, T.w0, ZP, top0 + " " + low0)
-    ls0 = cuts(0, "t0", top0)
-    t0 += " zw0 " + ls0
-    send("sl0", 0, [(T.ml0[:], T.ls0[:, 30:72])], "al0", ls0)
-    held = T.w0[:, 0:ZP + 4 * C]
-    ra = "sl0 zrw0 " + product("Ra", "e", "r0", A, 0, A, T.rw0, ZP, "sc0s")
-    x1t = gather("xa", T.x1, 0, held, T.ls0, 0, (0, 18, 36), t0)
-    quant("qt1", "t1", 0, A, T.x1[:, 0:4 * A], x1t)
-    x1m = gather("xb", T.x1, A, held, T.ls0, 72, (0, 24), t0)
-    quant("qm1", "m1", 0, MID, T.x1[:, 0:4 * MID], x1t + " " + x1m)
-    t1a = "zw1 " + product("U", "e", "m1", MID, 0, MID, T.w1, ZP, "qm1")
-    bottom(0, ls0)
-    if SPLIT:
-        be = gather("be", T.xin, 0, T.rw0[:], T.ml0, 6, (0, 6, 12), ra)
-        quant("qke", "ke", 0, 128, T.xin[:, 0:512], be + " lx0")
-        he = product("He", "we", "ke", 128, 0, E2, T.w0, ZP + 4 * C, "qke")
-        xc = gather("xc", T.x1, MID, T.w0[:, 0:ZP + 4 * (C + E2)], T.ls0, 96, (0, 6, 12), "lb0 %s %s" % (t0, he))
-        quant("qn1", "n1", 0, 128, T.x1[:, 4 * (MID + E2 - 128):4 * (MID + E2)], xc + " " + x1m)
-        t1b = product("V", "e", "n1", 128, 128 - E2, 128, T.w1, ZP + 4 * MID, "qn1")
-        b0 = gather("ba", T.bt0, 0, T.rw0[:], T.ml0, 10, (0, 16, 32), ra)
-        quant("qk0", "k0", 0, 128, T.bt0[:, 0:512], b0)
-        h0 = product("H", "we", "k0", 128, 32, 128, T.w0, ZP + 4 * (C + E2), "qk0")
-        xh = gather("xh", T.x1, MID + E2, T.w0[:], T.ls0, 108, (0, 12, 24), "lb0 %s %s %s" % (t0, he, h0))
-        quant("qo1", "o1", 0, 128, T.x1[:, 4 * (C - 128):4 * C], xh + " " + xc)
-        t1c = product("W", "e", "o1", 128, 32, 128, T.w1, ZP + 4 * (MID + E2), "qo1")
-        reach = MID + E2
+    if SPLITSEND:
+        send("sc0q", 0, codes("r0", "t0")[:1], "ac0", "taq")
+        send("sc0s", 0, codes("r0", "t0")[1:], "ac0", "tas")
     else:
-        b0 = gather("ba", T.bt0, 0, T.rw0[:], T.ml0, 6, (0, 18, 36), ra)
-        quant("qk0", "k0", 0, A, T.bt0[:], b0)
-        h0 = product("H", "we", "k0", A, 0, A, T.w0, ZP + 4 * C, "qk0")
-        xc = gather("xc", T.x1, MID, T.w0[:], T.ls0, 96, (0, 18, 36), "lb0 %s %s" % (t0, h0))
-        quant("qn1", "n1", 0, A, T.x1[:, 4 * MID:4 * C], xc)
-        t1b = product("W", "e", "n1", A, 0, A, T.w1, ZP + 4 * MID, "qn1")
-        t1c, reach = "", C
-
-    upper = T.w1[:, 0:ZP + 4 * MID]
+        send("sc0s", 0, codes("r0", "t0"), "ac0", top0)
+    if T0CUT < C:
+        product("T", "e", "t0", 0, T0CUT, 0, T0CUT, "w0", 0, top0 + " " + low0)
+        product("Tl", "e", "t0", C - 128, 128, T0CUT - (C - 128), 128, "w0", 2 * T0CUT, low0)
+        t0 = "T Tl"
+    else:
+        product("T", "e", "t0", 0, C, 0, C, "w0", 0, top0 + " " + low0)
+        t0 = "T"
+    ls0 = cuts(0, "t0", top0)
+    send("sl0", 0, [(T.ml0[:], T.ls0[:, 30:66])], "al0", ls0)
+    product("Ra", "e", "r0", 0, A, 0, A, "r0", ROW, "sc0s sc0q" if SPLITSEND else "sc0s")
+    x1t = gather("xa", T.x1, 0, A, "w0", 0, 2 * T0CUT, T.ls0[:, 0:18], ls0, "T")
+    quant("qt1", "t1", 0, A, T.x1[:, 0:4 * A], x1t)
     ls1 = cuts(1, "t1", "qt1")
-    t1a += " " + ls1
-    send("sl1", 1, [(T.ml1[:], T.ls1[:, 30:38])], "al1", ls1)
-    b1 = gather("bb", T.bt1, 0, upper, T.ls1, 36, (0, 18, 36), t1a)
-    quant("qk1", "k1", 0, A, T.bt1[:], b1)
-    send("sc1s", 1, codes("r1", "k1"), "ac1", "qk1")
-    h1 = product("I", "we", "r1", A, 0, A, T.w1, ZP + 4 * C, "sc1s")
-    x2e = gather("xd", T.x2, 0, upper, T.ls1, 0, (0, 24), t1a)
-    x2l = gather("xe", T.x2, ROW, T.w1[:, 0:ZP + 4 * reach], T.ls1, 24, (0, 6, 12), t1a + " " + t1b)
+    x1m = gather("xb", T.x1, A, MID - A, "w0", 0, 2 * C, T.ls0[:, 18:30], ls0, t0)
+    quant("qm1", "t1", A, A + 128, T.x1[:, 4 * A:4 * A + 512], x1m + " zx1")
+    product("U", "e", "t1", 0, MID, 0, MID, "w1", ROW, "qt1 qm1")
+    bottom(0, ls0)
+    be = gather("be", T.xin, A - E2, E2, "r0", 0, ROW + 2 * A, T.ml0[:, 18:24], "sl0 zr0#", "Ra")
+    quant("qke", "ke", 0, 128, T.xin[:, 4 * (A - E2):4 * (A - E2) + 512], be + " lx0")
+    product("He", "we", "ke", 0, 128, 0, E2, "w0", 2 * C, "qke")
+    xc = gather("xc", T.x1, MID, E2, "w0", 0, 2 * (C + E2), T.ls0[:, 66:72], "lb0 qm1", t0 + " He")
+    quant("qn1", "n1", 0, 128, T.x1[:, 4 * (MID + E2 - 128):4 * (MID + E2)], xc + " " + x1m)
+    product("V", "e", "n1", 0, 128, 128 - E2, 128, "w1", ROW + 2 * MID, "qn1")
+    b0 = gather("ba", T.xin, 0, A - E2, "r0", 0, ROW + 2 * A, T.ml0[:, 24:36], "sl0 zr0#", "Ra")
+    quant("qk0", "k0", 0, 128, T.xin[:, 0:512], b0 + " " + be)
+    product("H", "we", "k0", 0, 128, 0, A - E2, "w0", 2 * (C + E2), "qk0")
+    xh = gather("xh", T.x1, MID + E2, A - E2, "w0", 0, 2 * (C + A), T.ls0[:, 72:84], "lb0", t0 + " He H")
+    quant("qo1", "o1", 0, 128, T.x1[:, 4 * (C - 128):4 * C], xh + " " + xc)
+    product("W", "e", "o1", 0, 128, 128 - (A - E2), 128, "w1", ROW + 2 * (MID + E2), "qo1")
+
+    if B1_AT_SENDER:
+        send("sl1", 1, [(T.ml1[:, 0:18], T.ls1[:, 30:48])], "al1", ls1)
+        b1 = gather("bb", T.bt1, 0, A, "w1", 0, ROW + 2 * A, T.ls1[:, 48:66], ls1 + " zw1#", "U")
+        quant("qk1", "k1", 0, A, T.bt1[:], b1)
+        send("sc1s", 1, codes("r1", "k1"), "ac1", "qk1")
+        product("I", "we", "r1", 0, A, 0, A, "w1", ROW + 2 * C, "sc1s")
+    else:
+        send("sc1s", 1, codes("r1", "t1"), "ac1", "qt1")
+        send("sl1", 1, [(T.ml1[:], T.ls1[:, 30:66])], "al1", ls1)
+        product("Rb", "e", "r1", 0, A, 0, A, "r1", ROW, "sc1s")
+        b1 = gather("bb", T.bt1, 0, A, "r1", 0, ROW + 2 * A, T.ml1[:, 18:36], "sl1 zr1#", "Rb")
+        quant("qk1", "k1", 0, A, T.bt1[:], b1)
+        product("I", "we", "k1", 0, A, 0, A, "w1", ROW + 2 * C, "qk1")
+    x2e = gather("xd", T.x2, 0, 4 * S, "w1", ROW, ROW + 2 * MID, T.ls1[:, 0:12], ls1, "U")
+    x2l = gather("xe", T.x2, 4 * S, E2, "w1", ROW, ROW + 2 * (MID + E2), T.ls1[:, 12:18], ls1, "U V")
     quant("qt2", "t2", 0, A, T.x2[:, 0:4 * A], x2e + " " + x2l)
     bottom(1, ls1)
-    x2r = gather("xf", T.x2, A, T.w1[:], T.ls1, 72, (0, 30, 60), "lb1 %s %s %s %s" % (t1a, t1b, t1c, h1))
-    quant("qn2", "t2", A, C, T.x2[:, 4 * A:4 * C], x2r)
+    x2m = gather("xf", T.x2, A, MID - A, "w1", ROW, ROW + 2 * C, T.ls1[:, 18:30], ls1, "U V W")
+    if XSPLIT:
+        quant("qm2", "t2", A, A + 128, T.x2[:, 4 * A:4 * A + 512], x2m + " zx2")
+    x2r = gather("xi", T.x2, MID, A, "w1", ROW, ROW + 2 * (C + A), T.ls1[:, 66:84], "lb1 qm2" if XSPLIT else "lb1", "U V W I")
+    if XSPLIT:
+        quant("qn2", "t2", MID, C, T.x2[:, 4 * MID:4 * C], x2r)
+    else:
+        quant("qn2", "t2", A, C, T.x2[:, 4 * A:4 * C], x2m + " " + x2r)
 
-    send("sc2s", 2, codes("r2", "t2"), "ac2", "qt2")
     ls2 = cuts(2, "t2", "qt2")
-    send("sl2", 2, [(T.ml2[:], T.ls2[:, 36:72])], "al2", ls2)
-    scan("fw", T.fw[:], T.df[:], T.h[:, 6:NC:7], 0.0, ADD, MAX, "h df")
-    scan("v24", T.v24[:, ::-1], T.fw[:, ::-1], T.fw[:, ::-1], 0.0, MAX, MAX, "fw")
-    send("sn", 2, [(T.mn[:], T.v24[:])], "an", "v24 sl2s" if False else "v24")
-    t2 = product("X", "e", "t2", C, 0, C, T.w2, 0, "qt2 qn2")
-    rc = product("Rc", "e", "r2", A, 0, A, T.rw2, ZP, "sc2s")
-    b2 = gather("bc", T.bt2, 0, T.rw2[:], T.ml2, 0, (0, 18, 36), "sl2 zrw2 " + rc)
-    quant("qk2", "k2", 0, A, T.bt2[:], b2)
-    h2 = product("J", "we", "k2", A, 0, A, T.w2, 4 * C, "qk2")
-    tt("o1", T.o1[:], T.v24[:], T.cap[:, 0:NC:7], SUB, "v24 cap")
+    scan("fw", T.fw[:, ::-1], T.df[:, 0:S], T.h[:, PAD + 6:PAD + NC:7], 0.0, ADD, MAX, "h df0")
+    scan("v24", T.v24[:], T.df[:, S:2 * S], T.fw[:], 0.0, ADD, MAX, "fw df1")
+    send("sn", 2, [(T.mn[:], T.v24[:])], "an", "v24")
+    if B2_AT_SENDER:
+        product("Rc", "e", "t2", 0, A, 0, A, "w2", ROW, "qt2")
+        product("X", "e", "t2", A, C - A, 0, C - A, "w2", ROW + 2 * A, "qn2")
+        b2 = gather("bc", T.bt2, 0, A, "w2", 0, ROW + 2 * A, T.ls2[:, 48:66], ls2 + " zw2#", "Rc")
+        quant("qk2", "k2", 0, A, T.bt2[:], b2)
+        send("sc2s", 2, codes("r2", "k2"), "ac2", "qk2")
+        product("J", "we", "r2", 0, A, 0, A, "w2", ROW + 2 * C, "sc2s")
+        t2 = "Rc X J"
+    else:
+        send("sc2s", 2, codes("r2", "t2"), "ac2", "qt2")
+        send("sl2", 2, [(T.ml2[:], T.ls2[:, 48:66])], "al2", ls2)
+        if XSPLIT:
+            product("X", "e", "t2", 0, MID, 0, MID, "w2", ROW, "qt2 qm2")
+            product("Z", "e", "t2", MID, A, 0, A, "w2", ROW + 2 * MID, "qn2")
+        else:
+            product("X", "e", "t2", 0, C, 0, C, "w2", ROW, "qt2 qn2")
+        product("Rc", "e", "r2", 0, A, 0, A, "r2", ROW, "sc2s")
+        b2 = gather("bc", T.bt2, 0, A, "r2", 0, ROW + 2 * A, T.ml2[:], "sl2 zr2#", "Rc")
+        quant("qk2", "k2", 0, A, T.bt2[:], b2)
+        product("J", "we", "k2", 0, A, 0, A, "w2", ROW + 2 * C, "qk2")
+        t2 = "X Z J" if XSPLIT else "X J"
+    tt("o1", T.o1[:], T.v24[:], T.cap[:, NC - 7::-7], SUB, "v24 cap")
     lin("o2", T.o2[:], T.o1[:], 1.0 / ROW, 0.0, "o1")
     dma("oa", T.oa[:], T.o2[0:128:16, :], "st", "o2")
-    tt("e2", T.f1[:, 0:192:2], T.v24[:].indirect(T.rp4[:]), T.cf[:], ADD, "v24 rp4 cf")
-    tt("dd", T.dd[:], T.mn[:], T.v24[:], SUB, "sn v24")
-    tt("f2", T.f0[:, 1:192:2], T.dd[:].indirect(T.rp4[:]), T.cg[:], GT, "dd rp4 cg")
-    scan("fo", T.fo[:], T.f0[:], T.f1[:], 0.0, MUL, MAX, "fz f2 e2 own2 own3 fz1 fz3")
-    cp("lf", T.lf[:], T.fo[:, 1:192:2], "fo")
+    ts("le", T.lf[:, 0:48:2], T.v24[:], lane_e, -float(K), ADD, ADD, "v24 lane_e")
+    ts("e2", T.f1[:, 0:48:2], T.v24[:], lane_e, 8.0 * ROW - K, ADD, ADD, "v24 lane_e")
+    tt("f2", T.b0[:, 1:48:2], T.mn[:], T.f1[:, 0:48:2], GT, "sn e2", "f")
+    scan("fo", T.bo[:], T.b0[:], T.f1[:], 0.0, MUL, MAX, "bz f e2 own2", "bo")
+    cp("lf", T.lf[:, 1:48:2], T.bo[:, 1:48:2], "bo")
     for p, (a, z) in enumerate(LAST):
         n = str(p)
-        xg = gather("xg" + n, T.x3, a, T.w2[:], T.lf, a // 4, (0, (z - a) // 8, (z - a) // 4), "lf %s %s" % (t2, h2))
+        xg = gather("xg" + n, T.x3, a, z - a, "w2", ROW, ROW + 2 * (C + A), T.lf[:, a // 8:z // 8], "le lf", t2)
         quant("qf" + n, "fin", a, z, T.x3[:, 4 * a:4 * z], xg)
-        dma("oc" + n, T.oc[:, 4 * a:4 * z], T.qfin[:, a:z].bitcast(dt.uint8), "st", "qf" + n)
         mm("my" + n, [(side("v", 0, 128), side("fin", a, z))], z - a, "qv qf" + n)
         evac("ys" + n, "my" + n, 0, z - a, T.ysb[:, a:z], 1.0)
-        dma("y" + n, T.y[:, a:z], T.ysb[:, a:z], "st", "ys" + n)
+    for ps in OCS:
+        a, z = LAST[ps[0]][0], LAST[ps[-1]][1]
+        dma("oc%d" % ps[0], T.oc[:, 4 * a:4 * z], T.qfin[:, a:z].bitcast(dt.uint8), "st", " ".join("qf%d" % p for p in ps))
+    for ps in YS:
+        a, z = LAST[ps[0]][0], LAST[ps[-1]][1]
+        dma("y%d" % ps[0], T.y[:, a:z], T.ysb[:, a:z], "st", " ".join("ys%d" % p for p in ps))
     for k in range(4):
         dma("os%d" % k, T.osc[4 * k:4 * k + 4, :], T.sfin[32 * k:32 * k + 4, :], "st", " ".join("qf%d" % p for p in range(len(LAST))))
 
@@ -356,7 +409,7 @@ def rank_program(g, core, T, topo):
     for n in order["T"]:
         b = ops[n]["fixed"]
         if b is None:
-            b, turn = turn % BULK, turn + 1
+            b, turn = turn % (8 if WIDE and "pc2" in bank else BULK), turn + 1
         if b in last:
             ops[n]["deps"].add(reader[last[b]])
         last[b], bank[n] = n, b

from concourse.mybir import dt, AluOpType, ActivationFunctionType

S, C, A, R = 24, 384, 144, 3
ROW = 2 * S
MID = 10 * S
E2 = 2 * S
NC = 7 * S
PAD = 35
K = 16 * ROW
OFF = K + 5 * (ROW - 2)
BIG = 8192.0
X4 = "float8_e4m3fn_x4"
LAST = ((0, 128), (128, 256), (256, C))
X0 = 4 * A
XCUT = (0, 256, C)
T0CUT = 12 * S
B2_AT_SENDER = False
B1_AT_SENDER = False
XSPLIT = True
NATIVE = False
SBV = False
WIDE = True
SPLITSEND = True
OCS = ((0,), (1,), (2,))
YS = ((0,), (1,), (2,))

SCRATCH = {"ps": ("psum", [128, 4096], "float32")}
for _d, _bufs in (
        ("bfloat16", dict(xin=X0 + 4 * C, uin=512, vin=512, zz=NC, eb=516, cm=4 * NC, cn=4 * NC, sg=512, x1=4 * C, x2=4 * C, x3=4 * C, bt1=4 * A, bt2=4 * A,
                          w00=2 * (C + A), w01=2 * (C + A), w10=ROW + 2 * (C + A), w11=ROW + 2 * (C + A),
                          w20=ROW + 2 * (C + A), w21=ROW + 2 * (C + A),
                          r00=ROW + 2 * A, r01=ROW + 2 * A, r10=ROW + 2 * A, r11=ROW + 2 * A, r20=ROW + 2 * A, r21=ROW + 2 * A)),
        ("float32", dict(cr=S, room=7, r7=7, mf=2, sc=8, far=S, ins=NC, f0i=40, far0=40, r0e=7, in0=280, cap=NC, h=NC + 2 * PAD, dec0=18, dec=18, cl=22, tg0=54, tg1=54, tg2=54,
                         th=18, g3=18, b0=48, b1=36, bo=48, f1=48, df=2 * S, fw=S, v24=S, mn=S, o1=S, o2=S, ysb=C)),
        ("int32", dict(pi=1, mi=2, ki=1)),
        ("uint16", dict(ul=8, xl=S, ls0=84, ls1=84, ls2=66, lf=48, ml0=36, ml1=36, ml2=18))):
    for _n, _w in _bufs.items():
        SCRATCH[_n] = ("sbuf", [128, _w], _d)
for _n, _w in dict(x=C, u=128, up=128, v=128, w=512, e=512, cone=NC, cn=NC, sign=128, t0=C, t1=A + 128, n1=128, o1=128, t2=C, fin=C,
                   r0=A, r1=A, r2=A, ke=128, k0=128, k1=A, k2=A).items():
    SCRATCH["q" + _n] = ("sbuf", [128, _w], X4)
    SCRATCH["s" + _n] = ("sbuf", [128, _w], "uint8")

SEMAPHORES = ["cV", "cS", "cT", "cG", "sent", "lx0", "lx1", "lx2", "lu", "lv", "lwc", "lws", "st",
              "ac0", "ac1", "ac2", "al0", "al1", "al2", "an"]

ADD, SUB, MUL, MAX, MIN = AluOpType.add, AluOpType.subtract, AluOpType.mult, AluOpType.max, AluOpType.min
GT, GE, LT, NE = AluOpType.is_gt, AluOpType.is_ge, AluOpType.is_lt, AluOpType.not_equal
AND = AluOpType.bitwise_and
AF = ActivationFunctionType
BULK = 6

ORDER = {'Y': 'lx1 lx0 lwc lws lv oc1 oc0 os1 y2', 'G': 'pi room cr ez2 cmb cz3 cz2 eb cap sc0s zx1 zx2 sl0 bz g3 sc1s zr10 sl1 sc2s sl2 zr21 sn zr20', 'T': 'pb0 p0 mT1 mT3 mTl1 pc0 mT0 mT2 mTl0 mTl2 mTl3 mRa1 mRa3 mRa0 mRa2 pb1 p1 mHe0 mHe2 mHe1 mHe3 mU0 mU3 pc1 mU2 mH1 mH0 mU1 mV0 mV1 mV2 mV3 mH2 mRb2 mH3 mRb3 mRb0 mRb1 pb2 p2 mW2 pc2 mW0 mW1 mW3 mI1 mI3 mI2 mRc3 mRc0 mRc2 mRc1 mI0 mX3 mX1 mX0 mX2 mJ1 mJ0 mJ3 mZ3 mZ1 mJ2 mZ2 mZ0 my1 my2 my0', 'V': 'zz mi1 mi0 ez1 ki mf df1 negc lo383 dec0 sz2 ul xl0 xl1 xl2 qx1 qu qx0 qx2 upq taq tbq qe1 qe3 sa0 qcone qs0 qe0 qe2 zr11 zr00 h0 Tl1 tg01 tg02 tg00 ls01 ls02 ls00 Tl0 Tl3 xa1 Ra1 df0 e0 Ra2 qt1 be0 th0 qke own1 f0 sa1 bo0 qm1 qs1 He0 lb0 He2 qv He1 qk0 U0 h1 qn1 H1 tg10 tg12 own2 tg11 ls10 ls12 ls11 V0 V3 xd1 xe1 qt2 e1 xh0 Rb0 sa2 qo1 qs2 th1 bb1 h2 qk1 tg22 tg21 tg20 ls22 ls21 ls20 f1 fw bo1 I1 v24 qm2 lb1 Rc0 I2 Rc1 I0 bc0 qk2 e2 X1 qn2 X2 f2 le fo o1 Z3 lf Z2 xg21 xg10 xg00 qf1 qf2 qf0 ys1 ys2 ys0', 'S': 'lu lx2 zr01 cz1 ez0 clb r7 m16 m16b clc far sz3 cm4 hz cm6 lane cm2 cm3 lane_o dec cm1 ups cm5 tas cm0 cla tbs cma sb0 T3 T1 T0 lane_e T2 Tl2 xa0 Ra3 Ra0 be1 xb0 xb1 sb1 ba1 ba0 He3 xc0 xc1 U3 U2 H0 U1 V1 V2 xd0 xe0 H2 H3 Rb2 Rb1 xh1 sb2 Rb3 bb0 W2 W0 W1 W3 xf0 xf1 I3 Rc3 Rc2 xi1 bc1 xi0 X3 X0 J1 J0 J3 Z1 J2 Z0 xg11 xg20 xg01 o2 oa oc2 os3 os0 y1 os2 y0'}
ORDER = {'Y': 'lu lx0 lv lws lwc os3 os2 os1 oa', 'G': 'pi room f0i cr zr01 cz3 ez1 eb sz3 cap sc0s clb zr10 cz1 sl0 cmb zr21 zr00 bz g3 sc1s sl1 sc2s df1 sl2 sn zr20', 'T': 'pd0 pb0 pa0 pc0 mT1 mTl1 mT3 mTl3 mT0 mT2 mTl2 mRa0 mRa2 mRa3 mRa1 mTl0 pb1 pa1 mHe2 mHe0 mHe1 mHe3 mU3 mU0 pc1 mU2 mH1 mU1 mH0 mV2 mV3 mV0 mV1 mH2 mRb3 mH3 mRb0 mRb2 mRb1 pb2 pa2 mW0 pc2 mW3 mW2 mW1 mRc1 mRc2 mRc0 mI1 mI3 mI2 mI0 mRc3 mX2 mX0 mX3 mX1 mJ1 mJ3 mJ0 mZ1 mZ3 mJ2 mZ2 mZ0 my1 my2 my0', 'V': 'zz mi1 mi0 hz zr11 mf ki cz2 ez0 r0 lo383 lane_o zx1 ul dec0 qu xl2 negc xl0 qx1 upq qx0 xl1 qx2 cna1 taq qcn sa0 qe1 qs0 tbq qe3 qe0 h0 qe2 own2 tg02 tg01 tg00 Tl1 ls02 ls01 ls00 Tl3 T2 Tl2 xb1 e0 Ra0 Ra2 Ra1 cm1 qt1 be1 qv th0 qke own1 f0 sa1 qm1 bo0 qcone He2 lb0 qs1 He3 qk0 U3 h1 qn1 H1 tg11 tg12 tg10 ls11 ls12 ls10 V2 V0 V1 xd1 xe1 H2 qt2 e1 xh0 xh1 sa2 qo1 qs2 th1 zx2 bb0 h2 qk1 tg22 tg20 tg21 fw ls22 ls20 ls21 f1 xf0 bo1 v24 I1 lb1 qm2 le Rc0 Rc3 e2 bc0 X2 qk2 f2 X1 qn2 fo J1 J3 lf Z1 J0 Z2 xg21 xg10 xg00 qf1 qf2 qf0 o1 ys1 ys2 ys0', 'S': 'lx1 lx2 df0 cnz ez2 far0 m16 m16b cn0 cn6 cn5 cn1 cn2 cn3 cn4 ups cna2 cna0 tas sd0 sb0 far r7 tbs dec lane cm5 cla cm2 cm6 cm0 cm3 cm4 clc T1 T3 T0 xa1 xa0 Ra3 Tl0 be0 cma xb0 ba0 sb1 ba1 He0 He1 xc0 xc1 U0 U2 U1 H0 V3 xd0 xe0 Rb3 H3 Rb0 lane_e Rb2 sb2 Rb1 bb1 W0 W3 W2 W1 Rc1 Rc2 xf1 I3 I2 I0 xi1 bc1 xi0 X0 X3 Z3 J2 Z0 xg11 xg20 xg01 oc1 oc2 oc0 os0 o2 y1 y2 y0'}
ORDER = {'Y': 'lx0 lu lws lwc lv oa os1 os0', 'G': 'pi room cr cap eb ez2 cmb zr11 clb sc0s sc0q g3 sl0 zr01 sc1s zr20 sl1 sc2s zr10 sl2 sn', 'T': 'pb0 pa0 mT2 mT0 mT1 pc0 mT3 mTl3 mTl0 mTl2 mTl1 mRa3 mRa2 mRa1 mRa0 pa1 pb1 mHe2 mHe0 mHe1 mHe3 mU3 mU0 pc1 mH1 mU2 mH0 mU1 mV3 mV1 mV0 mV2 mH2 mRb3 mH3 mRb0 mRb1 pb2 pa2 mRb2 pc2 mW0 mW2 mW1 mW3 mRc1 mI3 mI1 mRc0 mI0 mRc2 mRc3 mI2 mX2 mX3 mX0 mX1 mJ1 mJ0 mJ3 mZ1 mZ3 mJ2 mZ0 mZ2 my1 my2 my0', 'V': 'zz cz1 mi1 mi0 sz3 ki mf ul ez0 negc m16 lo383 m16b dec0 xl0 xl2 xl1 qx0 qx1 qe2 qu taq upq tbq qe0 qe1 sa0 qcone qs0 zx1 qe3 zx2 T1 h0 tg01 tg02 tg00 ls01 ls02 ls00 Tl3 own1 xa1 e0 xb0 Ra3 Ra1 Ra0 qt1 be0 qke th0 df1 sa1 f0 qm1 bo0 qs1 lane_e lb0 qk0 He1 He3 qv U3 h1 qn1 tg11 tg12 tg10 ls11 ls12 ls10 H0 V3 V1 e1 V0 V2 xd1 H2 qt2 Rb1 xh0 th1 sa2 qo1 qs2 bb1 h2 qk1 tg21 tg20 tg22 own2 ls21 ls20 ls22 f1 fw bo1 Rc1 I3 v24 lb1 qm2 Rc0 Rc2 Rc3 I2 le bc0 o1 e2 qk2 X2 f2 qn2 X1 J1 fo lf o2 Z3 Z0 xg21 xg10 xg00 qf1 qf2 qf0 ys1 ys2 ys0', 'S': 'lx1 cz2 ez1 sz2 cz3 clc r7 df0 far cm3 cm1 cm6 cm4 cm2 cm5 cm0 tas hz ups tbs cma sb0 bz dec lane T2 cla T0 zr21 T3 Tl1 zr00 Tl0 Tl2 xa0 Ra2 xb1 be1 lane_o ba0 sb1 ba1 He2 He0 xc0 xc1 U0 H1 U2 U1 xd0 xe1 xe0 H3 Rb0 xh1 Rb3 sb2 Rb2 bb0 W0 W1 W2 W3 xf0 xf1 I1 I0 xi1 bc1 xi0 X3 X0 J0 J3 Z1 J2 Z2 xg11 xg20 xg01 oc1 os2 oc0 os3 y1 y0'}
ORDER = {'Y': 'lx0 lu lws lv lwc oa os2 os0 os1', 'G': 'pi room cr zx2 ez2 sz3 eb cmb cap sc0s sc0q sl0 g3 sc1s sl1 zr11 sc2s sl2 zr21 sn', 'T': 'pb0 pa0 mT2 mT0 pc0 mTl2 mT1 mTl0 mT3 mTl3 mTl1 mRa2 mRa0 mRa3 mRa1 pb1 pa1 mHe0 mHe2 mHe1 mHe3 mU3 pc1 mU0 mU2 mH1 mU1 mH0 mV3 mV1 mV0 mV2 mH2 mRb2 mRb3 mH3 mRb1 mRb0 pb2 pa2 mW0 pc2 mW2 mW1 mW3 mRc1 mI1 mRc3 mRc2 mRc0 mI3 mI0 mI2 mX1 mX2 mX3 mX0 mJ3 mJ1 mJ0 mZ1 mZ3 mJ2 mZ0 mZ2 my1 my2 my0', 'V': 'zz mi0 mi1 ki df1 r7 mf sz2 negc cz1 lo383 qx0 xl0 qx1 xl2 xl1 ul qu taq upq tbq qe2 qe0 sa0 qcone qs0 qe1 lane dec0 qe3 h0 zx1 tg01 tg00 tg02 ls01 ls00 ls02 Tl3 zr01 T3 zr10 zr00 xa1 Ra2 Ra1 qt1 be0 e0 th0 qke f0 sa1 bo0 qm1 qs1 He0 lb0 qk0 He3 xc0 U3 h1 qn1 tg11 H1 tg10 tg12 ls11 ls10 ls12 V3 V0 V2 xd1 xe1 Rb3 qt2 H2 Rb1 e1 xh0 sa2 qo1 qs2 th1 lane_o qv W0 f1 h2 qk1 tg21 tg22 tg20 ls21 ls22 ls20 fw bo1 xf0 lb1 I1 v24 qm2 Rc2 I0 Rc1 I2 bc0 own2 e2 qk2 X2 qn2 f2 X0 fo o1 J3 le lf Z1 J0 Z0 xg21 xg10 xg00 qf1 qf2 o2 qf0 ys1 ys2 ys0', 'S': 'lx1 cz2 cz3 ez0 ez1 m16 m16b far cm2 cm0 cm6 cm1 hz cm5 cm3 clb cm4 tas ups tbs cma sb0 clc df0 cla T2 T0 dec Tl2 lane_e T1 Tl1 Tl0 xa0 xb1 bz Ra3 Ra0 own1 be1 xb0 sb1 ba1 ba0 He2 He1 xc1 U0 U2 U1 H0 V1 xd0 xe0 H3 Rb0 xh1 Rb2 sb2 bb1 bb0 zr20 W2 W1 W3 xf1 Rc0 I3 Rc3 xi1 bc1 xi0 X1 X3 J1 Z3 J2 Z2 xg11 xg20 xg01 oc1 oc0 os3 y1 y0'}
ORDER = {'Y': 'lx0 lu lv lws lwc os0 os1 os2 y0', 'G': 'pi room cr cap ez2 eb hz zr00 cmb zx1 sc0s sc0q sl0 g3 bz df0 sc1s sl1 sc2s sl2 sn', 'T': 'pb0 pa0 mT2 pc0 mT0 mT1 mT3 mTl1 mTl2 mTl0 mTl3 mRa2 mRa3 mRa1 mRa0 pb1 pa1 mHe2 mHe0 mHe1 mHe3 mU3 pc1 mU0 mH1 mU2 mU1 mH0 mV2 mV3 mV1 mV0 mH2 mH3 mRb1 mRb0 mRb3 mRb2 pb2 pa2 mW1 pc2 mW0 mW3 mW2 mI3 mI1 mI0 mRc0 mRc3 mRc1 mRc2 mI2 mX0 mX3 mX2 mX1 mJ1 mJ3 mJ0 mZ1 mZ3 mZ2 mZ0 mJ2 my1 my2 my0', 'V': 'zz cz1 mi0 ki mi1 sz3 negc mf ez1 cz2 m16 lo383 ul xl0 xl2 qx0 xl1 qx1 qu taq upq qe2 tbq dec0 qe3 sa0 qcone qs0 qe0 qe1 h0 lane zx2 tg00 tg02 tg01 ls00 ls02 ls01 T3 Tl3 Tl2 xa1 e0 lane_e Ra3 Ra0 qt1 be0 qke own1 th0 sa1 f0 qm1 bo0 qs1 lb0 He2 qk0 He3 U3 h1 qn1 tg12 tg11 tg10 ls12 ls10 ls11 V2 V3 xd1 xe1 xe0 H2 qt2 Rb0 zr21 xh0 Rb2 sa2 qo1 qs2 e1 qv th1 W1 h2 qk1 tg20 tg21 tg22 f1 ls20 ls21 ls22 zr20 bo1 xf0 fw lb1 qm2 lane_o v24 Rc3 Rc2 I2 bc0 own2 o1 qk2 e2 X2 qn2 f2 le o2 fo J1 J3 lf Z1 Z2 Z0 xg21 xg10 xg00 qf1 qf2 qf0 ys1 ys2 ys0', 'S': 'lx1 ez0 zr11 sz2 r7 far df1 m16b cm1 zr10 cz3 cm2 cm5 cm3 cm6 clb cm0 cm4 tas ups tbs cma sb0 T2 clc dec cla T0 T1 Tl1 Tl0 xa0 xb1 zr01 Ra2 Ra1 be1 xb0 ba0 sb1 ba1 He0 He1 xc0 xc1 U0 H1 U2 U1 H0 V1 V0 xd0 Rb1 H3 Rb3 xh1 sb2 bb1 bb0 W0 W3 W2 xf1 I3 I1 I0 Rc0 Rc1 xi1 bc1 xi0 X3 X0 X1 J0 Z3 oa J2 xg11 xg20 xg01 oc1 os3 oc0 y1'}
ORDER = {'Y': 'lx0 lu lwc lws lv oa os2 os3 os1 y0', 'G': 'pi room cr ez2 eb sz3 cap cmb sc0s sc0q zx1 sl0 zx2 g3 sc1s sl1 sc2s sl2 zr20 sn', 'T': 'pb0 pa0 mT0 mT2 pc0 mT1 mTl3 mT3 mTl0 mTl1 mTl2 mRa3 mRa1 mRa2 mRa0 pb1 pa1 mHe0 mHe2 mHe1 mHe3 mU3 pc1 mU0 mU2 mH1 mU1 mH0 mV1 mV3 mV2 mV0 mH2 mH3 mRb1 mRb3 mRb2 mRb0 pb2 pa2 mW1 mW3 pc2 mW0 mW2 mI3 mI1 mI0 mRc2 mRc1 mRc0 mRc3 mI2 mX0 mX2 mX3 mX1 mJ0 mJ1 mJ3 mZ3 mZ1 mZ2 mZ0 mJ2 my1 my2 my0', 'V': 'zz mi1 mi0 ki cz2 mf cz3 m16 negc lo383 ul xl2 xl0 qx0 xl1 qx1 cla dec0 qu taq upq cm3 tbq qe0 qe2 sa0 qcone qs0 qe1 qe3 dec h0 tg01 tg00 tg02 ls01 ls00 ls02 T3 xa1 Tl2 e0 Ra3 Ra0 qt1 be0 df0 qke own1 th0 sa1 f0 qm1 bo0 qs1 lb0 He0 qk0 He3 lane_e U3 h1 qn1 tg11 tg10 tg12 H1 ls11 ls10 ls12 H0 xd1 xe1 xe0 H3 qt2 Rb0 xh0 e1 sa2 qo1 qs2 qv th1 bb0 h2 qk1 tg20 tg21 tg22 ls20 ls21 ls22 f1 fw xf0 bo1 v24 I1 qm2 lb1 I0 Rc0 Rc3 I2 bc0 o1 qk2 e2 X3 f2 qn2 le own2 fo J1 J0 lf Z1 Z2 xg21 xg10 xg00 qf1 qf2 qf0 ys2 ys0', 'S': 'lx1 ez1 sz2 hz r7 m16b ez0 far cz1 zr10 cm0 cm4 cm1 cm2 cm5 clb tas ups cm6 tbs cma lane sb0 T0 T2 clc zr01 T1 Tl0 Tl3 zr00 Tl1 xa0 xb1 Ra1 Ra2 bz be1 xb0 ba1 sb1 ba0 He2 He1 zr11 xc0 xc1 U0 U2 U1 V1 V3 V2 V0 xd0 df1 H2 Rb1 zr21 xh1 Rb2 sb2 Rb3 bb1 W1 W3 lane_o xf1 W0 W2 I3 Rc2 Rc1 xi1 bc1 xi0 X2 X0 X1 o2 J3 Z3 Z0 J2 xg11 xg20 xg01 oc1 ys1 oc0 y1 os0'}
ORDER = {'Y': 'lx1 lu lwc lv lws os3 os1 y2 y0', 'G': 'pi room cr eb cmb clb cap cz3 hz g3 sc0s sc0q zr00 bz sl0 zx1 df1 zr11 sc1s sl1 sc2s sl2 sn', 'T': 'pb0 pa0 mTl1 mT3 mT1 mT2 pc0 mTl2 mTl0 mT0 mTl3 mRa3 mRa1 mRa0 mRa2 pb1 pa1 mU0 mU3 mU1 mU2 mHe1 mHe3 mHe2 mHe0 pc1 mH0 mH3 mH2 mH1 mV3 mV2 mV0 mV1 mRb0 mRb2 mRb3 mRb1 pb2 pa2 mW0 mW2 mW3 mW1 pc2 mI3 mI0 mI2 mRc2 mI1 mRc1 mRc3 mRc0 mX0 mX1 mZ0 mX3 mZ1 mZ3 mZ2 mX2 mJ0 mJ2 mJ3 mJ1 my2 my1 my0', 'V': 'zz cz1 mi0 mi1 ki zr10 mf ez1 ul lo383 negc qe1 xl2 xl0 qx1 xl1 cm3 qx0 cm1 qu taq upq qe2 tbq qe3 sa0 qcone qs0 own1 qe0 dec0 T3 h0 qv tg01 tg02 tg00 ls01 ls02 ls00 Tl0 xa1 xb0 qt1 Ra1 Ra2 qm1 e0 be0 th0 sa1 qke f0 U0 qs1 bo0 U1 He3 lb0 qk0 He0 h1 xc0 tg10 tg11 tg12 qn1 ls10 ls12 ls11 H2 xd1 V3 V0 V1 Rb0 xe1 Rb2 qt2 xh1 Rb1 qo1 sa2 th1 qs2 e1 lane_e W2 qk1 h2 f1 tg20 tg21 tg22 bo1 ls20 ls21 ls22 lb1 qm2 fw I2 I1 v24 Rc3 xi1 o1 e2 qn2 bc0 o2 le own2 qk2 f2 X3 fo lf J0 J2 J3 xg20 xg21 xg00 qf2 qf1 qf0 ys2 ys1 ys0', 'S': 'lx0 zr01 cz2 ez0 ez2 cla m16b m16 r7 zr20 far sz3 df0 cm2 cm6 sz2 cm0 cm5 cm4 tas ups tbs cma sb0 zx2 Tl1 clc lane T1 dec T2 T0 Tl2 Tl3 zr21 xa0 xb1 Ra3 Ra0 be1 sb1 ba0 U3 ba1 He1 U2 He2 xc1 H0 H3 H1 V2 xd0 xe0 xh0 Rb3 bb0 sb2 bb1 W0 W3 W1 xf0 lane_o xf1 I0 I3 Rc2 Rc1 xi0 Rc0 X0 bc1 X1 Z0 oa Z1 Z2 X2 Z3 J1 xg10 xg11 xg01 oc2 oc1 oc0 os2 y1 os0'}
ORDER = {'Y': 'lx0 lu lwc lv lws oa os0 y2 y1 y0', 'G': 'pi room cr ez2 eb g3 zx2 bz cap cmb cz3 sc0s sc0q sl0 zx1 sc1s sl1 zr11 sc2s sl2 sn', 'T': 'pb0 pa0 mT3 mT2 mT1 pc0 mTl3 mTl2 mT0 mTl0 mTl1 mRa3 mRa0 mRa1 mRa2 pb1 pa1 mU3 mU0 mU1 mU2 pc1 mHe0 mHe1 mHe3 mHe2 mH3 mH0 mH2 mH1 mV3 mV1 mV0 mV2 mRb2 mRb0 mRb3 mRb1 pb2 pa2 mW2 mW0 mW1 mW3 pc2 mI2 mI0 mI1 mI3 mRc1 mRc3 mRc2 mRc0 mX1 mX0 mX3 mZ0 mZ3 mX2 mZ2 mZ1 mJ0 mJ2 mJ3 mJ1 my2 my1 my0', 'V': 'zz mi1 mi0 ki mf negc r7 m16 ul ez0 lo383 xl0 xl2 cm6 xl1 qx0 qx1 qe1 qu taq upq tbq qe3 qe2 sa0 qcone qs0 dec0 hz qe0 T2 dec h0 qv tg00 tg02 tg01 ls00 ls02 ls01 Tl1 zr00 xa1 xb1 qt1 e0 qm1 Ra0 Ra2 sa1 be1 qs1 th0 qke ba1 f0 h1 qk0 bo0 tg12 tg10 tg11 lb0 ls12 ls10 ls11 He2 df0 xc0 qn1 xd0 H2 H1 V3 V1 V0 V2 e1 zr21 xe0 Rb0 qt2 Rb1 Rb3 qo1 sa2 lane_o qs2 own2 th1 W2 qk1 f1 h2 bo1 tg20 tg22 tg21 ls20 ls22 ls21 fw qm2 lb1 v24 I3 zr20 Rc1 xi1 Rc3 lane_e qn2 bc0 qk2 e2 Z0 f2 o1 le fo Z3 lf J2 J3 xg20 xg21 xg00 qf2 qf1 qf0 ys2 ys1 ys0', 'S': 'lx1 ez1 sz2 sz3 lane far m16b cz2 cm0 cm4 clb cz1 cm1 cm3 cm2 tas ups cm5 tbs cma sb0 cla T3 T1 clc own1 Tl3 Tl2 T0 Tl0 xa0 xb0 zr01 Ra3 Ra1 sb1 be0 ba0 U3 U0 zr10 U1 He1 He0 He3 U2 xc1 H3 df1 H0 xd1 xh0 xe1 Rb2 xh1 bb0 sb2 bb1 W1 W3 W0 xf1 xf0 I2 I0 I1 xi0 Rc0 Rc2 X0 bc1 X1 X3 Z1 Z2 X2 J0 o2 J1 xg10 xg11 xg01 oc2 oc1 os1 oc0 os3 os2'}


def steps(g, core, T, topo):
    rank, n_ranks = T.rank_of(core), len(T.cores)
    V, ACT, PE, SY = g.vector, g.scalar, g.tensor, g.sync
    ops, bank = {}, {}

    def op(name, alts, reads, writes=None, **kw):
        ops[name] = dict(alts=alts, reads=reads.split(), writes=(name if writes is None else writes).split(), **kw)

    def psum(name, a, z):
        return T.ps[:, 512 * bank[name] + a:512 * bank[name] + z]

    def ts(name, out, in0, s1, s2, o0, o1, reads, writes=None):
        if o1 is None:
            op(name, {"V": lambda: V.tensor_scalar(out, in0, s1, None, o0)}, reads, writes)
        else:
            op(name, {"V": lambda: V.tensor_scalar(out, in0, s1, s2, o0, o1)}, reads, writes)

    def lin(name, out, in_, scale, bias, reads):
        op(name, {"V": lambda: V.tensor_scalar(out, in_, scale, bias, MUL, ADD),
                  "S": lambda: ACT.activation(out, in_, AF.Identity, bias=bias, scale=scale)}, reads)

    def tt(name, out, a, b, o, reads, writes=None):
        op(name, {"V": lambda: V.tensor_tensor(out, a, b, o)}, reads, writes)

    def cp(name, out, a, reads):
        op(name, {"V": lambda: V.tensor_copy(out, a)}, reads)

    def scan(name, out, d0, d1, init, o0, o1, reads, writes=None):
        op(name, {"V": lambda: V.tensor_tensor_scan(out, d0, d1, init, o0, o1)}, reads, writes)

    def iota(name, out, pat, base, cmul=0):
        op(name, {"G": lambda: g.iota(out, pat, base, cmul, allow_small_or_imprecise_dtypes=True)}, "")

    def const(name, ap, val):
        n = ap.shape[1]
        alts = {"V": lambda: V.memset(ap, float(val)), "G": lambda: g.iota(ap, [[0, n]], val, 0, allow_small_or_imprecise_dtypes=True)}
        if name != "zz":
            alts["S"] = lambda: ACT.activation(ap, T.zz[:, 0:n], AF.Identity, bias=float(val))
        op(name, alts, "" if name == "zz" else "zz")

    def quant(name, nm, a, b, src, reads, writes=None):
        op(name, {"V": lambda: V.quantize_mx(T["q" + nm][:, a:b], T["s" + nm][:, a:b], src)}, reads, writes)

    def side(nm, a, b):
        return T["q" + nm][:, a:b], T["s" + nm][:, a:b]

    def mm(name, pairs, n, reads, fixed=None):
        def fn():
            last = None
            for i, (l, r) in enumerate(pairs):
                last = PE.matmul_mx(psum(name, 0, n), l[0], l[1], r[0], r[1], i == 0, i == len(pairs) - 1)
            return last
        op(name, {"T": fn}, reads, fixed=fixed)

    def evac(name, src, a, z, out, scale):
        op(name, {"V": lambda: V.tensor_scalar(out, psum(src, a, z), scale, None, MUL),
                  "S": lambda: ACT.activation(out, psum(src, a, z), AF.Copy, scale=scale)}, src, frees=src)

    def gather(name, tile, c0, n, win, a, z, off, reads, planes):
        for h in range(2):
            out, src = tile[:, 4 * c0 + h:4 * (c0 + n):2], T[win + str(h)][:, a:z]
            need = " ".join(p + str(b) for p in planes.split() for b in (h, h + 2))
            op(name + str(h), {"V": lambda out=out, src=src: V.tensor_copy(out, src.indirect(off)),
                               "S": lambda out=out, src=src: ACT.activation(out, src.indirect(off), AF.Copy)},
               reads.replace("#", str(h)) + " " + need)
        return name + "0 " + name + "1"

    def pick(name, dst, a, z, src, w, off, reads):
        q, s = "q", "s"
        op(name + q, {"V": lambda: V.tensor_copy(T[q + dst][:, a:z].bitcast(dt.uint32), T[q + src][:, 0:w].bitcast(dt.uint32).indirect(off))}, reads)
        op(name + s, {"V": lambda: V.tensor_copy(T[s + dst][:, a:z], T[s + src][:, 0:w].indirect(off)),
                      "S": lambda: ACT.activation(T[s + dst][:, a:z], T[s + src][:, 0:w].indirect(off), AF.Copy)}, reads)
        return name + q + " " + name + s

    def dma(name, out, in_, sem, reads):
        op(name, {"Y": lambda: SY.dma_start(out, in_), "S": lambda: ACT.dma_start(out, in_)}, reads, dsem=sem)

    def send(name, t, parts, sem, reads):
        dst = T.cores[(rank + 1 + t) % n_ranks]
        rid, pid, _ = topo.addr(dst)
        width = min(len(topo.engines(core, c)) for c in T.cores if c != core)
        mask = sum(1 << e for e in topo.engines(core, dst)[:width])

        def fn():
            for o, i in parts:
                g.remote_dma(o, i, T.sem[sem], T.sem.sent, pid, rid, mask)
        op(name, {"G": fn}, reads, rsem=sem, inc=len(parts) * width)

    def codes(dst, src):
        return [(T["q" + dst][:].bitcast(dt.uint8), T["q" + src][:, 0:A].bitcast(dt.uint8)), (T["s" + dst][:], T["s" + src][:, 0:A])]

    def product(name, left, nm, c0, n, a, z, win, at, reads):
        for b in range(4):
            mm("m%s%d" % (name, b), [(side(k, 128 * b, 128 * b + 128), side(nm, c0, c0 + n)) for k in left], n,
               "qe%d %s %s" % (b, reads, "lwc lws" if "w" in left else ""))
            evac(name + str(b), "m%s%d" % (name, b), a, z, T[win + str(b % 2)][:, at + b // 2:at + 2 * (z - a):2], 0.015625)

    dma("lu", T.uin[:], T.u[:], "lu", "")
    for i, (a, z) in enumerate(zip(XCUT, XCUT[1:])):
        dma("lx%d" % i, T.xin[:, X0 + 4 * a:X0 + 4 * z], T.x[:, 4 * a:4 * z], "lx%d" % i, "")
    dma("lwc", T.qw[:].bitcast(dt.uint8), T.wc[:], "lwc", "")
    dma("lws", T.sw[:], T.ws[:], "lws", "")
    dma("lv", T.vin[:], T.v[:], "lv", "")

    m, mh2 = T.mf[:, 0:1], T.mf[:, 1:2]
    lane, m16, m16b, lo383, negc, lane_e, lane_o = (T.sc[:, i:i + 1] for i in range(7))
    op("pi", {"G": lambda: g.iota(T.pi[:], [[0, 1]], 0, 1)}, "")
    iota("cr", T.cr[:], [[2, S]], 0)
    iota("room", T.room[:], [[S, 7]], -1, -1)
    iota("cap", T.cap[:], [[-2, S], [ROW, 7]], K + 2 * (S - 1))
    const("zz", T.zz[:], 0)
    for b in range(3):
        const("ez%d" % b, T.eb[:, b:516:4], 0)
    op("eb", {"G": lambda: g.affine_select(T.eb[:, 3:515:4], T.zz[:, 0:128], [[-1, 128]], NE, 64.0, 0, 1)}, "zz")
    for b in range(4):
        quant("qe%d" % b, "e", 128 * b, 128 * b + 128, T.eb[:, 3 - b:515 - b], "eb ez0 ez1 ez2")
    ts("mi0", T.mi[:, 0:1], T.pi[:], 15, None, AND, None, "pi")
    ts("mi1", T.mi[:, 1:2], T.pi[:], 14, None, AND, None, "pi")
    cp("mf", T.mf[:], T.mi[:], "mi0 mi1")
    lin("lane", lane, mh2, -0.5 * ROW, m, "mf")
    lin("lane_e", lane_e, mh2, 0.5 * ROW - 1, m, "mf")
    lin("lane_o", lane_o, mh2, -0.5 * ROW - 1, m, "mf")
    ts("ul", T.ul[:], T.cr[:, 0:8], 8.0, None, MUL, None, "cr")
    lin("m16", m16, m, 16.0, 0.0, "mf")
    lin("m16b", m16b, m, 16.0, 256.0 - (C - 1), "mf")
    ts("lo383", lo383, m, 8.0, C - 1.0, LT, MUL, "mf")
    ts("xl0", T.xl[:, 0:S:3], T.cr[:, 0:8], m16, None, ADD, None, "cr m16")
    ts("xl1", T.xl[:, 1:S:3], T.cr[:, 0:8], m16b, lo383, ADD, ADD, "cr m16b lo383")
    ts("xl2", T.xl[:, 2:S:3], T.cr[:, 0:8], m16, 129.0, ADD, ADD, "cr m16")
    ts("ki", T.ki[:], T.room[:, 1:2], -1.0 / S, 11.5 / S, MUL, ADD, "room")
    ts("negc", negc, T.ki[:], float(S), T.room[:, 1:2], MUL, ADD, "ki room")
    op("far", {"S": lambda: ACT.activation(T.far[:], T.cr[:], AF.Abs, bias=negc, scale=-0.5)}, "cr negc")
    lin("r7", T.r7[:], T.room[:], 1.0 / S, 0.5 / S, "room")
    for b in range(1, 4):
        const("cz%d" % b, T.cm[:, b:4 * NC:4], 0)
    for e in range(7):
        op("cm%d" % e, {"S": lambda e=e: ACT.activation(T.ins[:, e:NC:7], T.far[:], AF.Sign, bias=T.r7[:, e:e + 1], scale=-1.0),
                        "V": lambda e=e: V.tensor_scalar(T.ins[:, e:NC:7], T.far[:], T.r7[:, e:e + 1], None, LT)}, "far r7")
    op("cma", {"S": lambda: ACT.activation(T.cm[:, 0:4 * NC:4], T.ins[:], AF.Relu, scale=BIG)}, " ".join("cm%d" % e for e in range(7)))
    op("cmb", {"G": lambda: g.affine_select(T.cm[:, 25:25 + 28 * 16:28], T.zz[:, 0:16], [[1, 16]], NE, BIG if SBV else BIG / 2, -127, 1)}, "cz1")
    quant("qcone", "cone", 0, NC, T.cm[:], "cz2 cz3 cma cmb")
    if NATIVE:
        iota("f0i", T.f0i[:], [[-16, 40]], 16 * (S - 1), -1)
        op("far0", {"S": lambda: ACT.activation(T.far0[:], T.f0i[:], AF.Abs, bias=m)}, "f0i mf")
        ts("r0", T.r0e[:], T.cr[:, 0:7], 0.5, m, MUL, SUB, "cr mf")
        for e in range(7):
            op("cn%d" % e, {"S": lambda e=e: ACT.activation(T.in0[:, e:280:7], T.far0[:], AF.Sign, bias=T.r0e[:, e:e + 1], scale=-1.0 / 16)}, "far0 r0")
        for b in range(3):
            w, src = BIG if b == 2 else BIG / 2, T.in0[:, 56 * b:56 * b + NC]
            op("cna%d" % b, {"S": lambda b=b, w=w, src=src: ACT.activation(T.cn[:, b:4 * NC:4], src, AF.Relu, scale=w),
                             "V": lambda b=b, w=w, src=src: V.tensor_scalar(T.cn[:, b:4 * NC:4], src, w, 0.0, MUL, MAX)},
               " ".join("cn%d" % e for e in range(7)))
        const("cnz", T.cn[:, 3:4 * NC:4], 0)
        quant("qcn", "cn", 0, NC, T.cn[:], "cna0 cna1 cna2 cnz")
    else:
        const("sz2", T.sg[:, 2:512:4], 0)
    const("sz3", T.sg[:, 3:512:4], 0)
    const("hz", T.h[:, 6:NC + 2 * PAD:7], 0)
    ts("dec0", T.dec0[:], T.cr[:, 0:18], mh2, 25.0, ADD, LT, "cr mf")
    lin("dec", T.dec[:], T.dec0[:], -2.0 * ROW, ROW - 2.0, "dec0")
    const("df0", T.df[:, 0:S], -ROW - 2)
    const("df1", T.df[:, S:2 * S], -ROW + 2)
    lin("cla", T.cl[:, 0:10], T.cr[:, 0:10], 0.5 * ROW, -float(OFF), "cr")
    const("clb", T.cl[:, 10:16], K - OFF)
    lin("clc", T.cl[:, 16:22], T.cr[:, 0:6], -0.5 * ROW, -float(OFF), "cr")
    iota("g3", T.g3[:], [[-ROW, 6], [16, 3]], 5 * ROW)
    lin("own1", T.b1[:, 1:36:2], T.g3[:], 1.0, m, "g3 mf")
    ts("own2", T.f1[:, 1:48:2], T.cr[:], lane_o, 7.0 * ROW, ADD, ADD, "cr lane_o")
    const("bz", T.b0[:, 0:48:2], 0)
    for n in ("r0", "w1" if B1_AT_SENDER else "r1", "w2" if B2_AT_SENDER else "r2"):
        for h in "01":
            const("z" + n + h, T[n + h][:, 0:ROW], 0)
    const("zx1", T.x1[:, 4 * MID:4 * A + 512], 0)
    if XSPLIT:
        const("zx2", T.x2[:, 4 * MID:4 * A + 512], 0)

    def cuts(t, top, reads):
        n = str(t)
        native = NATIVE and t == 0
        parts = ((("a", 256, 2, "qx2", 6), ("b", 128, 1, "qx1", 7), ("d", 0, 0, "qx0", None)) if native else
                 (("a", 0, 0, reads, 6), ("b", 16, 1, reads, 7)))
        for k, c0, b, need, fixed in parts:
            p = "p" + k + n
            mm(p, [(side("x" if native else top, c0, c0 + 128), side("up", 0, 128))], 128, need + " upq ups", fixed=fixed)
            if k == "a" or SBV:
                op("s" + k + n, {"V": lambda p=p, b=b: V.tensor_scalar(T.sg[:, b:512:4], psum(p, 0, 128), 0.0, 0.5, GT, SUB)}, p, "sg%d" % b, frees=p)
            else:
                op("s" + k + n, {"S": lambda p=p, b=b: ACT.activation(T.sg[:, b:512:4], psum(p, 0, 128), AF.Sign, bias=-1e-37)}, p, "sg%d" % b, frees=p)
        op("qs" + n, {"V": lambda: V.quantize_mx(T.qsign[:], T.ssign[:], T.sg[:])}, "sg0 sg1 sz3 " + ("sg2" if NATIVE else "sz2"), "sign")
        cone = "cn" if native else "cone"
        mm("pc" + n, [(side("sign", 0, 128), side(cone, 0, NC))], NC, "sign q" + cone, fixed=6)
        op("h" + n, {"V": lambda: V.tensor_tensor_scan(T.h[:, PAD:PAD + NC], psum("pc" + n, 0, NC), T.cap[:], float(K + ROW), MAX, MIN)},
           "pc%d cap hz" % t, "h", frees="pc" + n)
        lo = 16 if t == R - 1 else 0
        tg = T["tg" + n]
        for j in range(3):
            a = 6 + 7 * 8 * (2 - j)
            scan("tg%d%d" % (t, j), tg[:, 18 * j:18 * j + 18], T.dec[:], T.h[:, a:a + 7 * 17 + 1:7], 0.0, ADD, MAX, "h dec")
            ts("ls%d%d" % (t, j), T["ls" + n][:, 3 * lo + j:66:3], T.cl[:, lo:22], tg[:, 18 * j + 17:18 * j + 18], lane, ADD, ADD,
               "cla clb clc lane tg%d%d" % (t, j))
        return " ".join("ls%d%d" % (t, j) for j in range(3))

    def bottom(t, ls):
        n = str(t)
        ts("e" + n, T.b1[:, 0:36:2], T["ls" + n][:, 0:18], 10.0 * ROW, None, ADD, None, ls, "e")
        op("th" + n, {"V": lambda: V.tensor_copy(T.th[:], T["ml" + n][:, 0:18])}, "sl" + n, "th")
        tt("f" + n, T.b0[:, 1:36:2], T.th[:], T.b1[:, 0:36:2], GT, "th e", "f")
        scan("bo" + n, T.bo[:, 0:36], T.b0[:, 0:36], T.b1[:], 0.0, MUL, MAX, "bz f e own1", "bo")
        cp("lb" + n, T["ls" + n][:, 66:84], T.bo[:, 1:36:2], "bo")

    quant("qu", "u", 0, 128, T.uin[:], "lu")
    pick("up", "up", 0, 128, "u", 128, T.ul[:], "qu ul")
    quant("qv", "v", 0, 128, T.vin[:], "lv")
    for i, (a, z) in enumerate(zip(XCUT, XCUT[1:])):
        quant("qx%d" % i, "x", a, z, T.xin[:, X0 + 4 * a:X0 + 4 * z], "lx%d" % i)
    qx = " ".join("qx%d" % i for i in range(len(XCUT) - 1)) + " xl0 xl1 xl2"
    top0 = pick("ta", "t0", 0, 160, "x", C, T.xl[:, 0:10], qx)
    low0 = pick("tb", "t0", 160, C, "x", C, T.xl[:, 10:S], qx)

    if SPLITSEND:
        send("sc0q", 0, codes("r0", "t0")[:1], "ac0", "taq")
        send("sc0s", 0, codes("r0", "t0")[1:], "ac0", "tas")
    else:
        send("sc0s", 0, codes("r0", "t0"), "ac0", top0)
    if T0CUT < C:
        product("T", "e", "t0", 0, T0CUT, 0, T0CUT, "w0", 0, top0 + " " + low0)
        product("Tl", "e", "t0", C - 128, 128, T0CUT - (C - 128), 128, "w0", 2 * T0CUT, low0)
        t0 = "T Tl"
    else:
        product("T", "e", "t0", 0, C, 0, C, "w0", 0, top0 + " " + low0)
        t0 = "T"
    ls0 = cuts(0, "t0", top0)
    send("sl0", 0, [(T.ml0[:], T.ls0[:, 30:66])], "al0", ls0)
    product("Ra", "e", "r0", 0, A, 0, A, "r0", ROW, "sc0s sc0q" if SPLITSEND else "sc0s")
    x1t = gather("xa", T.x1, 0, A, "w0", 0, 2 * T0CUT, T.ls0[:, 0:18], ls0, "T")
    quant("qt1", "t1", 0, A, T.x1[:, 0:4 * A], x1t)
    ls1 = cuts(1, "t1", "qt1")
    x1m = gather("xb", T.x1, A, MID - A, "w0", 0, 2 * C, T.ls0[:, 18:30], ls0, t0)
    quant("qm1", "t1", A, A + 128, T.x1[:, 4 * A:4 * A + 512], x1m + " zx1")
    product("U", "e", "t1", 0, MID, 0, MID, "w1", ROW, "qt1 qm1")
    bottom(0, ls0)
    be = gather("be", T.xin, A - E2, E2, "r0", 0, ROW + 2 * A, T.ml0[:, 18:24], "sl0 zr0#", "Ra")
    quant("qke", "ke", 0, 128, T.xin[:, 4 * (A - E2):4 * (A - E2) + 512], be + " lx0")
    product("He", "we", "ke", 0, 128, 0, E2, "w0", 2 * C, "qke")
    xc = gather("xc", T.x1, MID, E2, "w0", 0, 2 * (C + E2), T.ls0[:, 66:72], "lb0 qm1", t0 + " He")
    quant("qn1", "n1", 0, 128, T.x1[:, 4 * (MID + E2 - 128):4 * (MID + E2)], xc + " " + x1m)
    product("V", "e", "n1", 0, 128, 128 - E2, 128, "w1", ROW + 2 * MID, "qn1")
    b0 = gather("ba", T.xin, 0, A - E2, "r0", 0, ROW + 2 * A, T.ml0[:, 24:36], "sl0 zr0#", "Ra")
    quant("qk0", "k0", 0, 128, T.xin[:, 0:512], b0 + " " + be)
    product("H", "we", "k0", 0, 128, 0, A - E2, "w0", 2 * (C + E2), "qk0")
    xh = gather("xh", T.x1, MID + E2, A - E2, "w0", 0, 2 * (C + A), T.ls0[:, 72:84], "lb0", t0 + " He H")
    quant("qo1", "o1", 0, 128, T.x1[:, 4 * (C - 128):4 * C], xh + " " + xc)
    product("W", "e", "o1", 0, 128, 128 - (A - E2), 128, "w1", ROW + 2 * (MID + E2), "qo1")

    if B1_AT_SENDER:
        send("sl1", 1, [(T.ml1[:, 0:18], T.ls1[:, 30:48])], "al1", ls1)
        b1 = gather("bb", T.bt1, 0, A, "w1", 0, ROW + 2 * A, T.ls1[:, 48:66], ls1 + " zw1#", "U")
        quant("qk1", "k1", 0, A, T.bt1[:], b1)
        send("sc1s", 1, codes("r1", "k1"), "ac1", "qk1")
        product("I", "we", "r1", 0, A, 0, A, "w1", ROW + 2 * C, "sc1s")
    else:
        send("sc1s", 1, codes("r1", "t1"), "ac1", "qt1")
        send("sl1", 1, [(T.ml1[:], T.ls1[:, 30:66])], "al1", ls1)
        product("Rb", "e", "r1", 0, A, 0, A, "r1", ROW, "sc1s")
        b1 = gather("bb", T.bt1, 0, A, "r1", 0, ROW + 2 * A, T.ml1[:, 18:36], "sl1 zr1#", "Rb")
        quant("qk1", "k1", 0, A, T.bt1[:], b1)
        product("I", "we", "k1", 0, A, 0, A, "w1", ROW + 2 * C, "qk1")
    x2e = gather("xd", T.x2, 0, 4 * S, "w1", ROW, ROW + 2 * MID, T.ls1[:, 0:12], ls1, "U")
    x2l = gather("xe", T.x2, 4 * S, E2, "w1", ROW, ROW + 2 * (MID + E2), T.ls1[:, 12:18], ls1, "U V")
    quant("qt2", "t2", 0, A, T.x2[:, 0:4 * A], x2e + " " + x2l)
    bottom(1, ls1)
    x2m = gather("xf", T.x2, A, MID - A, "w1", ROW, ROW + 2 * C, T.ls1[:, 18:30], ls1, "U V W")
    if XSPLIT:
        quant("qm2", "t2", A, A + 128, T.x2[:, 4 * A:4 * A + 512], x2m + " zx2")
    x2r = gather("xi", T.x2, MID, A, "w1", ROW, ROW + 2 * (C + A), T.ls1[:, 66:84], "lb1 qm2" if XSPLIT else "lb1", "U V W I")
    if XSPLIT:
        quant("qn2", "t2", MID, C, T.x2[:, 4 * MID:4 * C], x2r)
    else:
        quant("qn2", "t2", A, C, T.x2[:, 4 * A:4 * C], x2m + " " + x2r)

    ls2 = cuts(2, "t2", "qt2")
    scan("fw", T.fw[:, ::-1], T.df[:, 0:S], T.h[:, PAD + 6:PAD + NC:7], 0.0, ADD, MAX, "h df0")
    scan("v24", T.v24[:], T.df[:, S:2 * S], T.fw[:], 0.0, ADD, MAX, "fw df1")
    send("sn", 2, [(T.mn[:], T.v24[:])], "an", "v24")
    if B2_AT_SENDER:
        product("Rc", "e", "t2", 0, A, 0, A, "w2", ROW, "qt2")
        product("X", "e", "t2", A, C - A, 0, C - A, "w2", ROW + 2 * A, "qn2")
        b2 = gather("bc", T.bt2, 0, A, "w2", 0, ROW + 2 * A, T.ls2[:, 48:66], ls2 + " zw2#", "Rc")
        quant("qk2", "k2", 0, A, T.bt2[:], b2)
        send("sc2s", 2, codes("r2", "k2"), "ac2", "qk2")
        product("J", "we", "r2", 0, A, 0, A, "w2", ROW + 2 * C, "sc2s")
        t2 = "Rc X J"
    else:
        send("sc2s", 2, codes("r2", "t2"), "ac2", "qt2")
        send("sl2", 2, [(T.ml2[:], T.ls2[:, 48:66])], "al2", ls2)
        if XSPLIT:
            product("X", "e", "t2", 0, MID, 0, MID, "w2", ROW, "qt2 qm2")
            product("Z", "e", "t2", MID, A, 0, A, "w2", ROW + 2 * MID, "qn2")
        else:
            product("X", "e", "t2", 0, C, 0, C, "w2", ROW, "qt2 qn2")
        product("Rc", "e", "r2", 0, A, 0, A, "r2", ROW, "sc2s")
        b2 = gather("bc", T.bt2, 0, A, "r2", 0, ROW + 2 * A, T.ml2[:], "sl2 zr2#", "Rc")
        quant("qk2", "k2", 0, A, T.bt2[:], b2)
        product("J", "we", "k2", 0, A, 0, A, "w2", ROW + 2 * C, "qk2")
        t2 = "X Z J" if XSPLIT else "X J"
    tt("o1", T.o1[:], T.v24[:], T.cap[:, NC - 7::-7], SUB, "v24 cap")
    lin("o2", T.o2[:], T.o1[:], 1.0 / ROW, 0.0, "o1")
    dma("oa", T.oa[:], T.o2[0:128:16, :], "st", "o2")
    ts("le", T.lf[:, 0:48:2], T.v24[:], lane_e, -float(K), ADD, ADD, "v24 lane_e")
    ts("e2", T.f1[:, 0:48:2], T.v24[:], lane_e, 8.0 * ROW - K, ADD, ADD, "v24 lane_e")
    tt("f2", T.b0[:, 1:48:2], T.mn[:], T.f1[:, 0:48:2], GT, "sn e2", "f")
    scan("fo", T.bo[:], T.b0[:], T.f1[:], 0.0, MUL, MAX, "bz f e2 own2", "bo")
    cp("lf", T.lf[:, 1:48:2], T.bo[:, 1:48:2], "bo")
    for p, (a, z) in enumerate(LAST):
        n = str(p)
        xg = gather("xg" + n, T.x3, a, z - a, "w2", ROW, ROW + 2 * (C + A), T.lf[:, a // 8:z // 8], "le lf", t2)
        quant("qf" + n, "fin", a, z, T.x3[:, 4 * a:4 * z], xg)
        mm("my" + n, [(side("v", 0, 128), side("fin", a, z))], z - a, "qv qf" + n)
        evac("ys" + n, "my" + n, 0, z - a, T.ysb[:, a:z], 1.0)
    for ps in OCS:
        a, z = LAST[ps[0]][0], LAST[ps[-1]][1]
        dma("oc%d" % ps[0], T.oc[:, 4 * a:4 * z], T.qfin[:, a:z].bitcast(dt.uint8), "st", " ".join("qf%d" % p for p in ps))
    for ps in YS:
        a, z = LAST[ps[0]][0], LAST[ps[-1]][1]
        dma("y%d" % ps[0], T.y[:, a:z], T.ysb[:, a:z], "st", " ".join("ys%d" % p for p in ps))
    for k in range(4):
        dma("os%d" % k, T.osc[4 * k:4 * k + 4, :], T.sfin[32 * k:32 * k + 4, :], "st", " ".join("qf%d" % p for p in range(len(LAST))))

    writer, readers = {}, {}
    for n, o in ops.items():
        o["deps"] = set(writer[r] for r in o["reads"])
        for w in o["writes"]:
            o["deps"].update(readers.pop(w, []))
            writer[w] = n
        for r in o["reads"]:
            readers.setdefault(r, []).append(n)
    return ops, bank


def rank_program(g, core, T, topo):
    if T.rank_of(core) is None:
        return
    ops, bank = steps(g, core, T, topo)
    order = {e: names.split() for e, names in ORDER.items()}
    reader = {o["frees"]: n for n, o in ops.items() if "frees" in o}
    last, turn = {}, 0
    for n in order["T"]:
        b = ops[n]["fixed"]
        if b is None:
            b, turn = turn % (8 if WIDE and "pc2" in bank else BULK), turn + 1
        if b in last:
            ops[n]["deps"].add(reader[last[b]])
        last[b], bank[n] = n, b
    count, mark = {}, {}
    for e, names in order.items():
        for n in names:
            o = ops[n]
            s, inc = (o["rsem"], o["inc"]) if "rsem" in o else (o["dsem"], 16) if "dsem" in o else ("c" + e, 1)
            count[s] = count.get(s, 0) + inc
            mark[n] = (s, count[s])
            if "rsem" in o:
                count["sent"] = count.get("sent", 0) + inc
    queue = dict(V=g.vector, S=g.scalar, T=g.tensor, G=g, Y=g.sync)
    seen = {}
    for e, names in order.items():
        for n in names:
            o, need = ops[n], {}
            for d in o["deps"]:
                s, v = mark[d]
                need[s] = max(need.get(s, 0), v)
            for s, v in sorted(need.items()):
                if seen.get((e, s), 0) < v:
                    queue[e].wait_ge(T.sem[s], v)
                    seen[(e, s)] = v
            ins = o["alts"][e]()
            if "rsem" not in o:
                ins.then_inc(T.sem[mark[n][0]], 16 if "dsem" in o else 1)
    for s, v in sorted(count.items()):
        if max([w for (e, s2), w in seen.items() if s2 == s] + [0]) < v:
            g.sync.wait_ge(T.sem[s], v)
